import numpy as np, ml_dtypes
CORES = [24,25,26,27,28,29,30,31]
N = 8
import mx_ref
BF = ml_dtypes.bfloat16
def entries(a):
    return np.ascontiguousarray(a.T).reshape(-1)
def table(e):
    return np.ascontiguousarray(np.reshape(e, (-1, 16)).T).astype(np.int32)
def cols(t, e):
    v = np.concatenate([t.reshape(128, -1, 4), np.zeros((128, 1, 4), BF)], axis=1)
    return np.ascontiguousarray(v[:, e]).reshape(128, -1)
def tile(rs):
    return np.stack(rs, axis=2).reshape(128, -1).astype(BF)
def cut(t, i, w=512):
    return t[:, w * i:w * i + w]
def f(rng, *shape):
    return mx_ref.flush((rng.standard_normal(shape, dtype=np.float32) * np.exp2(rng.integers(-2, 3, shape[:-1] + (1,)))).astype(BF))
def wide(rng, *shape, cols=0):
    v = rng.standard_normal(shape, dtype=np.float32) * np.exp2(rng.integers(-12, 13, shape)).astype(np.float32)
    if cols: v *= np.repeat(np.exp2(rng.integers(-cols, cols + 1, shape[:-2] + (1, shape[-1] // 4))) * (rng.random(shape[:-2] + (1, shape[-1] // 4)) > 0.0625), 4, axis=-1).astype(np.float32)
    return mx_ref.flush(v.astype(BF))
S, C1, C2 = 256, 24, 40
def pack(nb):
    return {"nb0": np.stack([table(e) for e in nb[0].reshape(N, S)]), "nb1": np.stack([table(e) for e in nb[1].reshape(N, S)])}
def lists(rng):
    pool = [[(q * S + rng.permutation(S)[:rng.integers(1, 3 * C1 // 4 + 1)]).tolist() for q in range(N)] for r in range(N)]
    skew = []
    for r in range(N):
        p = np.exp2(rng.integers(0, 4, N)).astype(float); p[r] = 0
        skew.append(np.divide(p, p.sum()))
    who = {n: [] for n in range(N * S)}
    near, hand = {}, {}
    for r in range(N):
        for q in range(N):
            if q == r: continue
            for n in pool[r][q]: who[n].append(r)
            near[r, q] = set(pool[r][q]); hand[r, q] = set(pool[r][q])
    def one(r):
        if rng.random() < 0.6: return int(r * S + rng.integers(0, S))
        p = pool[r][int(rng.choice(N, p=skew[r]))]
        return p[rng.integers(0, len(p))]
    def fits(n, w):
        return all((w // S == r or len(near[r, w // S] | {w}) <= C2) and len(hand[r, n // S] | {w}) <= C2 for r in who[n])
    nb = np.zeros((2, N * S), int)
    for n in rng.permutation(N * S).tolist():
        for k in range(2):
            for _ in range(8):
                w = one(n // S)
                if fits(n, w): break
            else: w = n
            nb[k, n] = w
            for r in who[n]:
                if w // S != r: near[r, w // S].add(w)
                hand[r, n // S].add(w)
    for r in range(N):
        free = rng.permutation([n for n in range(r * S, r * S + S) if not who[n]])
        nb[1, free[:S // 20]] = nb[0, free[:S // 20]]
        for k in range(2):
            p = rng.permutation(free)[:2 * (S >> 6)]
            nb[k, p] = p[::-1]
    return pack(nb)
def weights(rng, n):
    return np.stack([f(rng, 128, 512 * n)] * N)
def setup_inputs(rng):
    return {"x": f(rng, N, 128, 4 * S), "a": weights(rng, 8), "v": weights(rng, 2), "u": weights(rng, 2), **lists(rng)}
def setup_inputs_apart(rng):
    d = setup_inputs(rng)
    nb = np.zeros((2, N * S), int)
    e, m = C2 - C1, S - (N - 1) * C1
    h = min(-(-m // (N - 1)), e - 2)
    p = [q * S + rng.permutation(S) for q in range(N)]
    F, H = {}, {}
    for q in range(N):
        for i in range(N - 1):
            r = (q + 1 + i) % N
            F[r, q] = p[q][C1 * i:C1 * i + C1]
            H[r, q] = p[q][(N - 1) * C1 + (h * i + np.arange(h)) % m]
    for r, q in F:
        s = (q + 1) % N
        if s == r: s = (q + 2) % N
        D = np.concatenate([H[r, q], rng.permutation(F[q, s])[:e - h]])
        k = (r + q) % 2
        nb[k, F[r, q]] = rng.permutation(F[q, r])
        nb[1 - k, F[r, q]] = np.concatenate([rng.permutation(D), F[q, r][:C1 - e]])
    for r in range(N):
        rest = p[r][(N - 1) * C1:]
        far = np.concatenate([F[r, q] for q in range(N) if q != r])
        for k in range(2):
            must = [int(n) for q in range(N) if q != r and (r + q) % 2 != k for n in F[r, q][C1 - e:e]]
            nb[k, rest] = rng.permutation(must + rng.choice(np.concatenate([far, p[r]]), m - len(must)).tolist())
    return {**d, **pack(nb)}
def setup_inputs_full(rng):
    d = setup_inputs(rng)
    nb = np.zeros((2, N * S), int)
    p = [q * S + rng.permutation(S) for q in range(N)]
    B = [e[:C1] for e in p]
    for q in range(N):
        some = rng.permutation(np.concatenate(B))[:C1]
        nb[:, B[q]] = rng.permutation(np.concatenate([p[q][C1:C2], some, rng.choice(some, 2 * C1 - C2)])).reshape(2, C1)
        rest = p[q][C1:]
        far = np.concatenate([B[s] for s in range(N) if s != q])
        for k in range(2):
            nb[k, rest] = rng.permutation(np.concatenate([far, rng.choice(np.concatenate([far, p[q]]), len(rest) - len(far))]))
    return {**d, **pack(nb)}
def setup_inputs_hub(rng):
    d = setup_inputs(rng)
    nb = np.zeros((2, N * S), int)
    for r in range(N):
        for k in range(2): nb[k, r * S:r * S + S] = (r + rng.integers(1, N)) % N * S + rng.integers(0, S)
    return {**d, **pack(nb)}
def setup_inputs_spread(rng):
    d = setup_inputs(rng); d["x"] = wide(rng, N, 128, 4 * S); return d
def setup_inputs_most(rng):
    d = setup_inputs(rng)
    nb = np.zeros((2, N * S), int)
    p = [q * S + rng.permutation(S) for q in range(N)]
    B = [e[:C1] for e in p]
    for q in range(N):
        nb[:, B[q]] = rng.permutation(np.concatenate([p[q][:C2], rng.choice(p[q][:C2], 2 * C1 - C2)])).reshape(2, C1)
        far = np.concatenate([B[s] for s in range(N) if s != q])
        must = np.concatenate([far, p[q][C2:]])
        nb[:, p[q][C1:]] = rng.permutation(np.concatenate([must, rng.choice(np.concatenate([far, p[q]]), 2 * (S - C1) - len(must))])).reshape(2, S - C1)
    return {**d, **pack(nb)}
def check_inputs(d):
    b = []
    nb = np.stack([np.concatenate([entries(e) for e in d[n]]) for n in ("nb0", "nb1")])
    for n in ("a", "v", "u"):
        if (d[n] != d[n][:1]).any(): b.append(n + " isn't the same on all ranks")
    if nb.min() < 0 or nb.max() >= N * S: return b + ["nb0, nb1"]
    for r in range(N):
        own = nb[:, r * S:r * S + S]
        first = np.unique(own)
        near = np.unique(np.concatenate([first, nb[0][first], nb[1][first]]))
        for q in range(N):
            if q == r: continue
            if (first // S == q).sum() > C1: b.append("too many neighbours on one other rank")
            if (near // S == q).sum() > C2: b.append("too many nodes of one other rank in two steps")
            behind = np.concatenate([nb[k][own[k][own[k] // S == q]] for k in range(2)])
            if len(np.unique(behind)) > C2: b.append("too many nodes behind neighbours on one other rank")
    return b
def product(w, t, e):
    n, i = np.unique(e, return_inverse=True)
    n = np.concatenate([n, np.full(-len(n) % 16, n[0])])
    return mx_ref.matmul(mx_ref.quantize(np.ascontiguousarray(w)), mx_ref.quantize(cols(t, n)))[:, i.reshape(-1)]
def reference(x, a, v, u, nb0, nb1):
    nb = np.stack([np.concatenate([entries(e) for e in n]) for n in (nb0, nb1)])
    x = np.concatenate(list(x), axis=1)
    named = np.unique(nb)
    R = []
    for b in range(4):
        P = product(cut(a[0], b), x, nb[0][named]) + product(cut(a[0], 4 + b), x, nb[1][named])
        R.append(np.maximum(P, np.float32(0)) * np.float32(0.05))
    h = np.zeros((128, N * S, 4), BF)
    h[:, named] = tile(R).reshape(128, -1, 4)
    h = h.reshape(128, -1)
    y = product(cut(v[0], 0), h, nb[0]) + product(cut(v[0], 1), h, nb[1]) + product(cut(u[0], 0), x, nb[0][nb[0]]) + product(cut(u[0], 1), x, nb[1][nb[1]])
    return {"y": np.stack([y[:, r * S:r * S + S] for r in range(N)])}

@@ -1,0 +1,417 @@
+from concourse.bass import DstId, RemoteDMATransfer
+from concourse.mybir import dt, AluOpType, AxisListType, ActivationFunctionType
+
+N, S, C1 = 8, 256, 24
+NV = 10
+POOL = S + 7 * C1
+UPOOL = 2 * S + 7 * 2 * C1
+
+F32, BF, I32, U16, F16, CODE, PLANE = "float32", "bfloat16", "int32", "uint16", "float16", "float8_e4m3fn_x4", "uint8"
+SCRATCH = {}
+
+
+def _sb(dtype, **bufs):
+    for name in bufs:
+        SCRATCH[name] = ("sbuf", [128, bufs[name]], dtype)
+
+
+_sb(I32, w32=16, w16=32, u1=32, u2=32, u3=32, u4=32, u5=32, u6=32, u7=32)
+_sb(F16, z16=512, zh=512, row=512, cum=256 * NV + 8)
+_sb(BF, rowb=512, eq=512 * NV, sj=512 * (17 - NV), fw=320, fm=32, fs=32, um=48, us=48, tb1=16, tb2=64,
+    z2=2048, zh2=2048, tab=2048, gm=512, gs=512)
+_sb(F32, sa=24, cntd=16, bit=16, nbit=16, pre=16, zz=16, yy=16, tot=32, tott=32, off=1, uf=3, tb0=16,
+    bp=32, eu=32, ef=16, pf=32, pu=32)
+_sb(U16, p16=16, sf=2, su=3, rho=32, po16=32, pu16=32, lf=14, lr=14, lu=21, lru=22)
+_sb(I32, it=16, li=16, pi=1, pai=1, pmi=1, pgi=1, pci=1)
+_sb(F32, bi=16, tr=16, ownc=16, oc0=16, pm=1, pg=1, own=1, nown=1, trow=32, tg=32,
+    m1=32, m2=32, mm=32, one=16, addu=4)
+_sb(BF, loc=16, gcol=1, pa=1, idr=256, jm=512, mk=512, hm=2048, h16=512)
+_sb(BF, xb=1024, ab=4096, vb=1024, ub=1024, ht=1024)
+_sb(F32, yo=S)
+for _n, _w in dict(aq=1024, vq=256, uq=256, xq=S, xg=224, xp=POOL, xk=512, xu=336, up=UPOOL, yu=512, hq=S, hg=224,
+                   hp=POOL, yh=512).items():
+    SCRATCH[_n] = ("sbuf", [128, _w], CODE)
+    SCRATCH[_n + "s"] = ("sbuf", [128, _w], PLANE)
+for _n in ("ps0", "ps1", "ps2", "ps3", "psy"):
+    SCRATCH[_n] = ("psum", [128, 512], F32)
+SEMAPHORES = ["lw", "lw2", "lx", "la", "lv", "vs", "ss", "ts", "gc", "rt", "rf", "ru", "xo", "uc", "st", "ls",
+              "af", "au", "axc", "axs", "auc", "aus", "ahc", "ahs"]
+
+
+def rank_program(g, core, T, topo):
+    rank = T.rank_of(core)
+    if rank is None:
+        return
+    A, Fn = AluOpType, ActivationFunctionType
+    vec, sca, syn, ten, sem = g.vector, g.scalar, g.sync, g.tensor, T.sem
+    queue = {"v": vec, "s": sca, "y": syn, "t": ten, "g": g}
+    cnt = {"vs": 0, "ss": 0, "ts": 0, "gc": 0}
+    seen = {}
+
+    def did(name, ins):
+        ins.then_inc(sem[name], 1)
+        cnt[name] += 1
+        return cnt[name]
+
+    def wait(q, name, val):
+        if seen.get((q, name), 0) < val:
+            seen[(q, name)] = val
+            queue[q].wait_ge(sem[name], val)
+
+    def V(ins):
+        return did("vs", ins)
+
+    def vw(n):
+        wait("v", "vs", n)
+
+    def words(ap):
+        return ap.bitcast(dt.uint32)
+
+    def copy(out, in_):
+        return V(vec.tensor_copy(out, in_))
+
+    def ts(out, in0, s1, op0, s2=None, op1=None):
+        if op1 is None:
+            return V(vec.tensor_scalar(out, in0, s1, None, op0))
+        return V(vec.tensor_scalar(out, in0, s1, s2, op0, op1))
+
+    def tt(out, in0, in1, op):
+        return V(vec.tensor_tensor(out, in0, in1, op))
+
+    def fill(ap, val):
+        return V(vec.memset(ap, val))
+
+    def quant(out, sc, in_):
+        return V(vec.quantize_mx(out, sc, in_))
+
+    def hold(out, keep, data):
+        return V(vec.tensor_tensor_scan(out, keep, data, 0.0, A.mult, A.add))
+
+    def act(out, in_, fn=Fn.Copy, **kw):
+        return did("ss", sca.activation(out, in_, fn, **kw))
+
+    def load(q, out, in_, name):
+        queue[q].dma_start(out, in_).then_inc(sem[name], 16)
+
+    dest = [T.cores[(rank + 1 + i) % N] for i in range(N - 1)]
+    masks = [0] * (N - 1)
+    near, far = 0, 0
+    for i, d in enumerate(dest):
+        e = topo.engines(core, d)
+        if topo.die(d) != topo.die(core):
+            masks[i] = (1 << e[4 * far]) | (1 << e[4 * far + 2])
+            far += 1
+        else:
+            masks[i] = (1 << e[4 * near + 1]) | (1 << e[4 * near + 3])
+            near += 1
+
+    def send(src, dst, name):
+        tr = []
+        for i, d in enumerate(dest):
+            rid, pid, _e = topo.addr(d)
+            tr.append(RemoteDMATransfer(dst_ids=[DstId(rid=rid, pnc=pid)], dma_engine_mask=masks[i],
+                                        remote_sem=sem[name], src=src(i), dst=dst(6 - i)))
+        g.remote_dma_fused(tr, local_sem=sem.ls)
+
+    ARR = 2 * (N - 1)
+
+    for b in range(4):
+        load("y", T.w32[32 * b:32 * b + 16, :], T.nb0[:], "lw")
+        load("s", T.w32[32 * b + 16:32 * b + 32, :], T.nb1[:], "lw")
+    load("y", T.xb[:], T.x[:], "lx")
+    load("y", T.ab[:], T.a[:], "la")
+    for q in range(8):
+        load("y", T.w16[16 * q:16 * q + 16, 0:16], T.nb0[:], "lw2")
+        load("s", T.w16[16 * q:16 * q + 16, 16:32], T.nb1[:], "lw2")
+
+    def iota(out, pattern, mul, small=True):
+        if small:
+            return did("gc", g.iota(out, pattern, 0, mul, allow_small_or_imprecise_dtypes=True))
+        return did("gc", g.iota(out, pattern, 0, mul))
+    iota(T.pi[:], [[1, 1]], 1, False)
+    g_int = iota(T.it[:], [[1, 16]], 16, False)
+    iota(T.trow[:], [[1, 32]], 0)
+    iota(T.tg[:], [[1, 2], [0, 16]], 0)
+    g_48 = iota(T.jm[:, 0:48], [[0, 3], [1, 16]], 0)
+    iota(T.idr[:], [[1, 16], [16, 16]], 0)
+    g_all = iota(T.jm[:, 48:512], [[0, 29], [1, 16]], 0)
+
+    k = fill(T.hm[:, 0:512], 1.0)
+    fill(T.one[:], 1.0)
+    fill(T.fw[:, 0:32], 0.0)
+    vw(k)
+    k_hm = fill(T.hm[:, 0:512:32], 0.0)
+    k = fill(T.h16[:], 1.0)
+    vw(k_hm)
+    ts(T.z16[:], T.hm[:, 0:512], 0.0, A.mult)
+    ts(T.cum[:, 0:8], T.hm[:, 0:8], 0.0, A.mult)
+    vw(k)
+    fill(T.h16[:, 0:512:16], 0.0)
+    wait("v", "gc", g_int)
+    ts(T.pci[:], T.pi[:], 4, A.logical_shift_right)
+    k = ts(T.li[:], T.it[:], 255, A.bitwise_and)
+    ts(T.pai[:], T.pi[:], 15, A.bitwise_and)
+    ts(T.pmi[:], T.pi[:], 31, A.bitwise_and)
+    k2 = ts(T.pgi[:], T.pi[:], 4, A.logical_shift_right, 1, A.bitwise_and)
+    vw(k)
+    ts(T.gcol[:], T.pci[:], -256.0, A.mult)
+    copy(T.loc[:], T.li[:])
+    ts(T.bi[:], T.li[:], -1.0, A.mult, -0.5, A.add)
+    vw(k2)
+    copy(T.pm[:], T.pmi[:])
+    copy(T.pg[:], T.pgi[:])
+    k = copy(T.pa[:], T.pai[:])
+    ts(T.own[:], T.pci[:], float(rank), A.is_equal)
+    ts(T.nown[:], T.pci[:], float(rank), A.not_equal)
+    ts(T.tr[:], T.li[:], 33.0, A.add)
+    wait("v", "gc", g_48)
+    vw(k)
+    ts(T.m1[:], T.trow[:], T.pm[:, 0:1], A.is_gt)
+    k = ts(T.m2[:], T.tg[:], T.pg[:, 0:1], A.is_equal)
+    ts(T.mk[:, 0:48], T.jm[:, 0:48], T.pa[:, 0:1], A.is_equal)
+    vw(k)
+    tt(T.mm[:], T.m1[:], T.m2[:], A.mult)
+
+    wait("v", "lw", 128)
+    k = copy(T.z16[:, 0:512:32], T.w32[:])
+    vw(k)
+    k = hold(T.zh[:], T.hm[:, 0:512], T.z16[:])
+    vw(k)
+    k = V(vec.transpose(T.row[:], T.zh[:]))
+    vw(k)
+    k_row = ts(T.rowb[:], T.row[:], T.gcol[:, 0:1], A.add)
+    wait("s", "vs", k_row)
+    for m in range(17 - NV):
+        c = NV - 1 + m
+        s_sum = act(T.sj[:, 512 * m:512 * m + 512], T.rowb[:], Fn.Sign, bias=T.bi[:, c:c + 1], scale=1.0,
+                    accum_out=T.sa[:, m:m + 1])
+    vw(k_row)
+    for c in range(NV):
+        k = ts(T.eq[:, 512 * c:512 * c + 512], T.rowb[:], T.loc[:, c:c + 1], A.is_equal)
+    vw(k)
+    k = V(vec.tensor_tensor_scan(T.cum[:, 8:8 + 256 * NV], T.eq[:, 0:512 * NV:2], T.eq[:, 1:512 * NV:2], 0.0,
+                                 A.add, A.add))
+    vw(k)
+    tt(T.cntd[:, 0:NV], T.cum[:, 263:8 + 256 * NV:256], T.cum[:, 7:8 + 256 * (NV - 1):256], A.subtract)
+    wait("v", "ss", s_sum)
+    k = tt(T.cntd[:, NV:16], T.sa[:, 0:16 - NV], T.sa[:, 1:17 - NV], A.subtract)
+    vw(k)
+    k = ts(T.bit[:], T.cntd[:], 0.0, A.is_gt, T.nown[:, 0:1], A.mult)
+    vw(k)
+    k_pre = hold(T.pre[:], T.one[:], T.bit[:])
+    k_nb = ts(T.nbit[:], T.bit[:], -1.0, A.mult, 1.0, A.add)
+    vw(k_pre)
+    k_tot = ts(T.tot[:], T.mm[:], T.pre[:, 15:16], A.mult)
+    vw(k_nb)
+    k_zz = tt(T.zz[:], T.nbit[:], T.tr[:], A.mult)
+    vw(k_tot)
+    k_tott = V(vec.transpose(T.tott[:], T.tot[:]))
+    vw(k_zz)
+    tt(T.yy[:], T.pre[:], T.zz[:], A.max)
+    vw(k_tott)
+    k_off = V(vec.tensor_reduce(T.off[:], T.tott[:], AxisListType.X, A.add))
+    vw(k_off)
+    k_p16 = ts(T.p16[:], T.yy[:], T.off[:, 0:1], A.add, -1.0, A.add)
+    wait("v", "gc", g_all)
+    vw(k_p16)
+    k_sc = copy(T.fw[:, 0:320].indirect(T.p16[:, 0:16]), T.idr[:])
+    vw(k_sc)
+    k = tt(T.fm[:], T.fw[:, 0:32], T.mk[:, 0:32], A.mult)
+    vw(k)
+    k = hold(T.fs[:], T.h16[:, 0:32], T.fm[:])
+    vw(k)
+    k_sf = copy(T.sf[:], T.fs[:, 15:32:16])
+
+    wait("g", "vs", k_sf)
+    send(lambda i: T.sf[:], lambda j: T.lf[:, 2 * j:2 * j + 2], "af")
+
+    ts(T.tb0[:], T.pre[:], T.off[:, 0:1], A.add, T.nown[:, 0:1], A.mult)
+    k = ts(T.oc0[:], T.loc[:], -231.0, A.add, T.own[:, 0:1], A.mult)
+    tt(T.um[:, 0:24], T.fw[:, 0:24], T.mk[:, 0:24], A.mult)
+    k2 = tt(T.um[:, 24:48], T.fw[:, 0:24], T.mk[:, 24:48], A.mult)
+    fill(T.addu[:, 0:1], 0.0)
+    fill(T.addu[:, 2:3], 256.0)
+    vw(k)
+    k = ts(T.ownc[:], T.oc0[:], -1.0, A.add)
+    vw(k2)
+    k2 = hold(T.us[:], T.h16[:, 0:48], T.um[:])
+    vw(k)
+    k_tb = tt(T.tb1[:], T.tb0[:], T.ownc[:], A.add)
+    k2 = ts(T.addu[:, 1:2], T.pa[:], 8.0, A.is_ge, 256.0, A.mult)
+    wait("v", "lx", 16)
+    k_xq = quant(T.xq[:], T.xqs[:], T.xb[:])
+    vw(k2)
+    k = tt(T.uf[:], T.us[:, 15:48:16], T.addu[:, 0:3], A.add)
+    wait("v", "lw2", 256)
+    ts(T.u1[:], T.w16[:], 63, A.bitwise_and)
+    ts(T.u2[:], T.w16[:], 6, A.logical_shift_right)
+    vw(k)
+    k_su = copy(T.su[:], T.uf[:])
+    wait("g", "vs", k_su)
+    send(lambda i: T.su[:], lambda j: T.lu[:, 3 * j:3 * j + 3], "au")
+
+    wait("y", "vs", k_tb)
+    for b in range(4):
+        load("y", T.tb2[32 * b:32 * b + 32, :], T.tb1[:], "rt")
+    wait("y", "vs", k_xq)
+    load("y", T.xp[:, 0:S].bitcast(dt.uint8), T.xq[:].bitcast(dt.uint8), "xo")
+    load("y", T.xps[:, 0:S], T.xqs[:], "xo")
+    for m in range(4):
+        act(T.z2[:, 512 * m:512 * m + 512], T.hm[:, 0:512], scale=0.0)
+    for m in range(1, 4):
+        s_hm = act(T.hm[:, 512 * m:512 * m + 512], T.hm[:, 0:512])
+    wait("y", "af", ARR)
+    wait("s", "af", ARR)
+    for q in range(8):
+        load("ys"[q % 2], T.lr[16 * q:16 * q + 16, :], T.lf[16 * rank:16 * rank + 16, :], "rf")
+    load("y", T.vb[:], T.v[:], "lv")
+    load("y", T.ub[:], T.u[:], "lv")
+    wait("y", "au", ARR)
+    for q in range(8):
+        load("y", T.lru[16 * q:16 * q + 16, 0:21], T.lu[16 * rank:16 * rank + 16, :], "ru")
+
+    k = ts(T.u3[:], T.w16[:], 8, A.logical_shift_right)
+    vw(k)
+    k2 = ts(T.u4[:], T.u1[:], 32, A.mult)
+    k = ts(T.u5[:], T.u3[:], 8 - rank, A.add)
+    ts(T.mk[:, 48:512], T.jm[:, 48:512], T.pa[:, 0:1], A.is_equal)
+    vw(k)
+    k2 = tt(T.u6[:], T.u4[:], T.u2[:], A.add)
+    k = ts(T.u7[:], T.u5[:], 7, A.bitwise_and)
+    vw(k)
+    ts(T.bp[:], T.u7[:], 24.0, A.mult, 232.0, A.add)
+    ts(T.ef[:], T.u7[:, 0:16], 0.0, A.is_gt, 232.0, A.mult)
+    ts(T.eu[:, 16:32], T.u7[:, 16:32], 24.0, A.mult, 256.0, A.add)
+    k = ts(T.eu[:, 0:16], T.u7[:, 0:16], 24.0, A.mult)
+    copy(T.rho[:], T.u6[:])
+    vw(k)
+    tt(T.eu[:, 0:16], T.eu[:, 0:16], T.ef[:], A.add)
+    wait("v", "la", 16)
+    quant(T.aq[:, 0:512], T.aqs[:, 0:512], T.ab[:, 0:2048])
+    quant(T.aq[:, 512:1024], T.aqs[:, 512:1024], T.ab[:, 2048:4096])
+    wait("v", "rt", 64)
+    wait("v", "ss", s_hm)
+    k = copy(T.z2[:, 0:2048:32], T.tb2[:])
+    vw(k)
+    k_zh2 = hold(T.zh2[:], T.hm[:], T.z2[:])
+
+    wait("v", "rf", 128)
+    k_xs = copy(words(T.xg[:, 0:224]), words(T.xq[:, 0:S]).indirect(T.lr[:, 0:14]))
+    wait("s", "rf", 128)
+    wait("s", "vs", k_xq)
+    s_xs = act(T.xgs[:, 0:224], T.xqs[:, 0:S].indirect(T.lr[:, 0:14]))
+    wait("g", "vs", k_xs)
+    send(lambda i: T.xg[:, 32 * i:32 * i + C1].bitcast(dt.uint8),
+         lambda j: T.xp[:, S + C1 * j:S + C1 * j + C1].bitcast(dt.uint8), "axc")
+    wait("g", "ss", s_xs)
+    send(lambda i: T.xgs[:, 32 * i:32 * i + C1], lambda j: T.xps[:, S + C1 * j:S + C1 * j + C1], "axs")
+
+    vw(k_zh2)
+    k = V(vec.transpose(T.tab[:], T.zh2[:]))
+    vw(k)
+    k = tt(T.gm[:], T.tab[:].indirect(T.rho[:, 0:32]), T.mk[:], A.mult)
+    vw(k)
+    k = hold(T.gs[:], T.h16[:], T.gm[:])
+    vw(k)
+    k = tt(T.pf[:], T.gs[:, 15:512:16], T.bp[:], A.add)
+    vw(k)
+    k_po = copy(T.po16[:], T.pf[:])
+    k = tt(T.pu[:], T.pf[:], T.eu[:], A.add)
+    vw(k)
+    copy(T.pu16[:], T.pu[:])
+
+    wait("v", "xo", 32)
+    wait("s", "xo", 32)
+    wait("s", "vs", k_po)
+    wait("v", "axc", ARR)
+    wait("s", "axs", ARR)
+    k_xk, s_xk = [], []
+    for kk in range(2):
+        o, w = S * kk, 16 * kk
+        k_xk.append(copy(words(T.xk[:, o:o + S]), words(T.xp[:, 0:POOL]).indirect(T.po16[:, w:w + 16])))
+        s_xk.append(act(T.xks[:, o:o + S], T.xps[:, 0:POOL].indirect(T.po16[:, w:w + 16])))
+    ps = [T.ps0, T.ps1, T.ps2, T.ps3]
+    t_p = [0] * 4
+    for kk in range(2):
+        wait("t", "vs", k_xk[kk])
+        wait("t", "ss", s_xk[kk])
+        o = S * kk
+        for b in range(4):
+            w = 128 * (4 * kk + b)
+            t_p[b] = did("ts", ten.matmul_mx(ps[b][:, 0:S], T.aq[:, w:w + 128], T.aqs[:, w:w + 128],
+                                             T.xk[:, o:o + S], T.xks[:, o:o + S], kk == 0, kk == 1))
+    wait("v", "ru", 128)
+    vw(k_xk[1])
+    k_xu = copy(words(T.xu[:, 0:336]), words(T.xk[:, 0:2 * S]).indirect(T.lru[:, 0:21]))
+    wait("s", "ru", 128)
+    wait("s", "ss", s_xk[1])
+    s_xu = act(T.xus[:, 0:336], T.xks[:, 0:2 * S].indirect(T.lru[:, 0:21]))
+    wait("g", "vs", k_xu)
+    send(lambda i: T.xu[:, 48 * i:48 * i + 48].bitcast(dt.uint8),
+         lambda j: T.up[:, 512 + 48 * j:560 + 48 * j].bitcast(dt.uint8), "auc")
+    wait("g", "ss", s_xu)
+    send(lambda i: T.xus[:, 48 * i:48 * i + 48], lambda j: T.ups[:, 512 + 48 * j:560 + 48 * j], "aus")
+    wait("y", "vs", k_xk[1])
+    wait("y", "ss", s_xk[1])
+    load("y", T.up[:, 0:512].bitcast(dt.uint8), T.xk[:].bitcast(dt.uint8), "uc")
+    load("y", T.ups[:, 0:512], T.xks[:], "uc")
+    for b in range(4):
+        out = T.ht[:, b:4 * S:4]
+        if b % 2 == 0:
+            wait("s", "ts", t_p[b])
+            s_r = act(out, ps[b][:, 0:S], Fn.Relu, scale=0.05)
+        else:
+            wait("v", "ts", t_p[b])
+            k = ts(out, ps[b][:, 0:S], 0.0, A.max, 0.05, A.mult)
+    wait("v", "ss", s_r)
+    vw(k)
+    k_hq = quant(T.hq[:], T.hqs[:], T.ht[:])
+    vw(k_hq)
+    k_hs = copy(words(T.hg[:, 0:224]), words(T.hq[:, 0:S]).indirect(T.lr[:, 0:14]))
+    wait("s", "vs", k_hq)
+    s_hs = act(T.hgs[:, 0:224], T.hqs[:, 0:S].indirect(T.lr[:, 0:14]))
+    wait("g", "vs", k_hs)
+    send(lambda i: T.hg[:, 32 * i:32 * i + C1].bitcast(dt.uint8),
+         lambda j: T.hp[:, S + C1 * j:S + C1 * j + C1].bitcast(dt.uint8), "ahc")
+    wait("g", "ss", s_hs)
+    send(lambda i: T.hgs[:, 32 * i:32 * i + C1], lambda j: T.hps[:, S + C1 * j:S + C1 * j + C1], "ahs")
+    k_hp = quant(T.hp[:, 0:S], T.hps[:, 0:S], T.ht[:])
+    wait("v", "lv", 32)
+    quant(T.vq[:], T.vqs[:], T.vb[:])
+    quant(T.uq[:], T.uqs[:], T.ub[:])
+
+    wait("v", "uc", 32)
+    wait("v", "auc", ARR)
+    k_yu = copy(words(T.yu[:]), words(T.up[:, 0:UPOOL]).indirect(T.pu16[:, 0:32]))
+    wait("s", "vs", k_hp)
+    wait("s", "uc", 32)
+    wait("s", "aus", ARR)
+    s_yu = act(T.yus[:], T.ups[:, 0:UPOOL].indirect(T.pu16[:, 0:32]))
+    wait("t", "vs", k_yu)
+    wait("t", "ss", s_yu)
+    for kk in range(2):
+        o, w = S * kk, 128 * kk
+        did("ts", ten.matmul_mx(T.psy[:, 0:S], T.uq[:, w:w + 128], T.uqs[:, w:w + 128],
+                                T.yu[:, o:o + S], T.yus[:, o:o + S], kk == 0, False))
+    wait("v", "ahc", ARR)
+    wait("s", "ahs", ARR)
+    vw(k_hp)
+    for kk in range(2):
+        o, w = S * kk, 16 * kk
+        k = copy(words(T.yh[:, o:o + S]), words(T.hp[:, 0:POOL]).indirect(T.po16[:, w:w + 16]))
+        s = act(T.yhs[:, o:o + S], T.hps[:, 0:POOL].indirect(T.po16[:, w:w + 16]))
+        wait("t", "vs", k)
+        wait("t", "ss", s)
+        w = 128 * kk
+        t_y = did("ts", ten.matmul_mx(T.psy[:, 0:S], T.vq[:, w:w + 128], T.vqs[:, w:w + 128],
+                                      T.yh[:, o:o + S], T.yhs[:, o:o + S], False, kk == 1))
+    wait("v", "ts", t_y)
+    k = copy(T.yo[:], T.psy[:, 0:S])
+    wait("y", "vs", k)
+    load("y", T.y[:], T.yo[:], "st")
+
+    ends = {"lw": 128, "lw2": 256, "lx": 16, "la": 16, "lv": 32, "rt": 64, "rf": 128, "ru": 128, "xo": 32, "uc": 32,
+            "ls": 8 * ARR, "af": ARR, "au": ARR, "axc": ARR, "axs": ARR, "auc": ARR, "aus": ARR, "ahc": ARR,
+            "ahs": ARR, "st": 16, **cnt}
+    for name in ends:
+        wait("g", name, ends[name])

@@ -1,10 +1,15 @@
 from concourse.bass import DstId, RemoteDMATransfer
-from concourse.mybir import dt, AluOpType, AxisListType, ActivationFunctionType
+from concourse.mybir import dt, AluOpType, ActivationFunctionType
 
 N, S, C1 = 8, 256, 24
-NV = 10
+FAR = 176
 POOL = S + 7 * C1
-UPOOL = 2 * S + 7 * 2 * C1
+KW = 448
+PAD, TOP = 16, 528
+STEP = 513
+MID = 212.0
+NTV = 9
+EARLY = True
 
 F32, BF, I32, U16, F16, CODE, PLANE = "float32", "bfloat16", "int32", "uint16", "float16", "float8_e4m3fn_x4", "uint8"
 SCRATCH = {}
@@ -15,27 +20,24 @@ def _sb(dtype, **bufs):
         SCRATCH[name] = ("sbuf", [128, bufs[name]], dtype)
 
 
-_sb(I32, w32=16, w16=32, u1=32, u2=32, u3=32, u4=32, u5=32, u6=32, u7=32)
-_sb(F16, z16=512, zh=512, row=512, cum=256 * NV + 8)
-_sb(BF, rowb=512, eq=512 * NV, sj=512 * (17 - NV), fw=320, fm=32, fs=32, um=48, us=48, tb1=16, tb2=64,
-    z2=2048, zh2=2048, tab=2048, gm=512, gs=512)
-_sb(F32, sa=24, cntd=16, bit=16, nbit=16, pre=16, zz=16, yy=16, tot=32, tott=32, off=1, uf=3, tb0=16,
-    bp=32, eu=32, ef=16, pf=32, pu=32)
-_sb(U16, p16=16, sf=2, su=3, rho=32, po16=32, pu16=32, lf=14, lr=14, lu=21, lru=22)
-_sb(I32, it=16, li=16, pi=1, pai=1, pmi=1, pgi=1, pci=1)
-_sb(F32, bi=16, tr=16, ownc=16, oc0=16, pm=1, pg=1, own=1, nown=1, trow=32, tg=32,
-    m1=32, m2=32, mm=32, one=16, addu=4)
-_sb(BF, loc=16, gcol=1, pa=1, idr=256, jm=512, mk=512, hm=2048, h16=512)
-_sb(BF, xb=1024, ab=4096, vb=1024, ub=1024, ht=1024)
+_sb(I32, w16=32, go=9)
+_sb(U16, off=32, pl16=32, ms=4, lf=14, lr2=28, cu=22, po16=32, co16=24)
+_sb(F16, rw=2048, lc=512)
+_sb(F32, sr=2048, cv=2560, sm=9, a513=8, b512=8, ge=8, t32=32, cof=24)
+_sb(BF, z=512, zh=512, row=512, cw=512, cb=544, le=1024, gm=512, gt=512, gm2=448, gt2=448, gm3=512, gt3=512, pc=64)
+_sb(I32, dio=32, dm=32, p3=4, p3m=4)
+_sb(F32, eye=32, tw=544, blk=1, bq=6, sg=2, hi8=1, odds=1, pm=5, jio=24, pio=32)
+_sb(BF, one=512, hk=512, ownr=S, c3=3, s1=1)
+_sb(BF, xb=1024, ab=4096, vb=1024, ub=1024, ht=1024, hr=4 * FAR)
 _sb(F32, yo=S)
-for _n, _w in dict(aq=1024, vq=256, uq=256, xq=S, xg=224, xp=POOL, xk=512, xu=336, up=UPOOL, yu=512, hq=S, hg=224,
-                   hp=POOL, yh=512).items():
+for _n, _w in dict(aq=1024, vq=256, uq=256, xq=S, xg=224, xp=POOL, xu=336, ul=336, xk=2 * KW, yu=512,
+                   hp=S + FAR, yh=512).items():
     SCRATCH[_n] = ("sbuf", [128, _w], CODE)
     SCRATCH[_n + "s"] = ("sbuf", [128, _w], PLANE)
-for _n in ("ps0", "ps1", "ps2", "ps3", "psy"):
+for _n in ("ps0", "ps1", "ps2", "ps3", "pr0", "pr1", "pr2", "pr3"):
     SCRATCH[_n] = ("psum", [128, 512], F32)
-SEMAPHORES = ["lw", "lw2", "lx", "la", "lv", "vs", "ss", "ts", "gc", "rt", "rf", "ru", "xo", "uc", "st", "ls",
-              "af", "au", "axc", "axs", "auc", "aus", "ahc", "ahs"]
+SEMAPHORES = ["lw", "lx", "la", "lb", "lu", "lv", "vs", "ss", "ts", "gc", "rp", "rf", "st", "l1", "l2", "l3",
+              "af", "axc", "axs", "auc", "aus"]
 
 
 def rank_program(g, core, T, topo):
@@ -58,42 +60,67 @@ def rank_program(g, core, T, topo):
             seen[(q, name)] = val
             queue[q].wait_ge(sem[name], val)
 
-    def V(ins):
-        return did("vs", ins)
-
     def vw(n):
         wait("v", "vs", n)
+
+    def sw(n):
+        wait("s", "ss", n)
 
     def words(ap):
         return ap.bitcast(dt.uint32)
 
+    def raw(ap):
+        return ap.bitcast(dt.uint8)
+
     def copy(out, in_):
-        return V(vec.tensor_copy(out, in_))
+        return did("vs", vec.tensor_copy(out, in_))
 
     def ts(out, in0, s1, op0, s2=None, op1=None):
         if op1 is None:
-            return V(vec.tensor_scalar(out, in0, s1, None, op0))
-        return V(vec.tensor_scalar(out, in0, s1, s2, op0, op1))
+            return did("vs", vec.tensor_scalar(out, in0, s1, None, op0))
+        return did("vs", vec.tensor_scalar(out, in0, s1, s2, op0, op1))
 
     def tt(out, in0, in1, op):
-        return V(vec.tensor_tensor(out, in0, in1, op))
+        return did("vs", vec.tensor_tensor(out, in0, in1, op))
 
     def fill(ap, val):
-        return V(vec.memset(ap, val))
+        return did("vs", vec.memset(ap, val))
 
     def quant(out, sc, in_):
-        return V(vec.quantize_mx(out, sc, in_))
+        return did("vs", vec.quantize_mx(out, sc, in_))
 
-    def hold(out, keep, data):
-        return V(vec.tensor_tensor_scan(out, keep, data, 0.0, A.mult, A.add))
+    def scan(out, d0, d1, op0, op1):
+        return did("vs", vec.tensor_tensor_scan(out, d0, d1, 0.0, op0, op1))
+
+    def turn(out, in_):
+        return did("vs", vec.transpose(out, in_))
 
     def act(out, in_, fn=Fn.Copy, **kw):
         return did("ss", sca.activation(out, in_, fn, **kw))
 
+    def line(out, in_, scale, bias):
+        return act(out, in_, Fn.Identity, bias=bias, scale=scale)
+
     def load(q, out, in_, name):
         queue[q].dma_start(out, in_).then_inc(sem[name], 16)
 
-    dest = [T.cores[(rank + 1 + i) % N] for i in range(N - 1)]
+    def iota(out, pattern, base, mul, whole=False):
+        if whole:
+            return did("gc", g.iota(out, pattern, base, mul))
+        return did("gc", g.iota(out, pattern, base, mul, allow_small_or_imprecise_dtypes=True))
+
+    def pick_codes(dst, a, n, src, wa, wb, offs):
+        return copy(words(T[dst][:, a:a + n]), words(T[src][:, wa:wb]).indirect(offs))
+
+    def pick_scales(dst, a, n, src, wa, wb, offs):
+        return act(T[dst + "s"][:, a:a + n], T[src + "s"][:, wa:wb].indirect(offs))
+
+    def product(out, w, wa, x, xa, n, start, stop):
+        return did("ts", ten.matmul_mx(out[:, 0:n], T[w][:, wa:wa + 128], T[w + "s"][:, wa:wa + 128],
+                                       T[x][:, xa:xa + n], T[x + "s"][:, xa:xa + n], start, stop))
+
+    other = [(rank + 1 + i) % N for i in range(N - 1)]
+    dest = [T.cores[q] for q in other]
     masks = [0] * (N - 1)
     near, far = 0, 0
     for i, d in enumerate(dest):
@@ -105,313 +132,316 @@ def rank_program(g, core, T, topo):
             masks[i] = (1 << e[4 * near + 1]) | (1 << e[4 * near + 3])
             near += 1
 
-    def send(src, dst, name):
+    def send(src, dst, name, left):
         tr = []
         for i, d in enumerate(dest):
             rid, pid, _e = topo.addr(d)
             tr.append(RemoteDMATransfer(dst_ids=[DstId(rid=rid, pnc=pid)], dma_engine_mask=masks[i],
                                         remote_sem=sem[name], src=src(i), dst=dst(6 - i)))
-        g.remote_dma_fused(tr, local_sem=sem.ls)
+        g.remote_dma_fused(tr, local_sem=sem[left])
 
     ARR = 2 * (N - 1)
+    home = 32 * (rank // 2)
 
-    for b in range(4):
-        load("y", T.w32[32 * b:32 * b + 16, :], T.nb0[:], "lw")
-        load("s", T.w32[32 * b + 16:32 * b + 32, :], T.nb1[:], "lw")
-    load("y", T.xb[:], T.x[:], "lx")
-    load("y", T.ab[:], T.a[:], "la")
     for q in range(8):
-        load("y", T.w16[16 * q:16 * q + 16, 0:16], T.nb0[:], "lw2")
-        load("s", T.w16[16 * q:16 * q + 16, 16:32], T.nb1[:], "lw2")
+        load("y", T.w16[16 * q:16 * q + 16, 0:16], T.nb0[:], "lw")
+        load("s", T.w16[16 * q:16 * q + 16, 16:32], T.nb1[:], "lw")
+    load("y", T.xb[:], T.x[:], "lx")
+    load("y", T.ab[:, 0:2048], T.a[:, 0:2048], "la")
+    load("y", T.ab[:, 2048:4096], T.a[:, 2048:4096], "lb")
 
-    def iota(out, pattern, mul, small=True):
-        if small:
-            return did("gc", g.iota(out, pattern, 0, mul, allow_small_or_imprecise_dtypes=True))
-        return did("gc", g.iota(out, pattern, 0, mul))
-    iota(T.pi[:], [[1, 1]], 1, False)
-    g_int = iota(T.it[:], [[1, 16]], 16, False)
-    iota(T.trow[:], [[1, 32]], 0)
-    iota(T.tg[:], [[1, 2], [0, 16]], 0)
-    g_48 = iota(T.jm[:, 0:48], [[0, 3], [1, 16]], 0)
-    iota(T.idr[:], [[1, 16], [16, 16]], 0)
-    g_all = iota(T.jm[:, 48:512], [[0, 29], [1, 16]], 0)
+    g_dio = iota(T.dio[:], [[1, 32]], 128, -1, True)
+    for c in range(4):
+        g_p3 = iota(T.p3[:, c:c + 1], [[1, 1]], 0, (4, 8, 2, 16)[c], True)
+    k = iota(T.one[:], [[0, 512]], 1, 0)
+    iota(T.z[:], [[0, 512]], 0, 0)
+    wait("g", "gc", k)
+    g_hk = did("gc", g.affine_select(T.hk[:], T.one[:], [[0, 16], [1, 32]], A.not_equal, 0.0, 0, 0))
+    iota(T.cb[:, 0:PAD], [[0, PAD]], 0, 0)
+    iota(T.cb[:, TOP:TOP + 16], [[0, 16]], 0, 0)
+    g_own = iota(T.ownr[:], [[1, S]], -int(MID), 0)
+    iota(T.pio[:], [[64, 16], [0, 2]], 0, 0)
+    iota(T.jio[:, 0:12], [[96, 4], [28, 3]], 0, 0)
+    g_j = iota(T.jio[:, 12:24], [[96, 4], [22, 3]], 32, 0)
 
-    k = fill(T.hm[:, 0:512], 1.0)
-    fill(T.one[:], 1.0)
-    fill(T.fw[:, 0:32], 0.0)
+    fill(T.tw[:, 0:PAD], 0.0)
+    fill(T.tw[:, TOP:TOP + 16], 0.0)
+    fill(T.cv[:, 2303:2560:256], 0.0)
+    wait("v", "gc", g_dio)
+    k = ts(T.dm[:], T.dio[:], 31, A.bitwise_and)
     vw(k)
-    k_hm = fill(T.hm[:, 0:512:32], 0.0)
-    k = fill(T.h16[:], 1.0)
-    vw(k_hm)
-    ts(T.z16[:], T.hm[:, 0:512], 0.0, A.mult)
-    ts(T.cum[:, 0:8], T.hm[:, 0:8], 0.0, A.mult)
+    k_eye = ts(T.eye[:], T.dm[:], 0.0, A.is_equal)
+    wait("s", "vs", k_eye)
+    for c in range(16):
+        level, out = float(STEP * (c // 2) + 1 + 512 * (c % 2)), T.tw[:, PAD + 32 * c:PAD + 32 * c + 32]
+        if c < NTV:
+            ts(out, T.dm[:], 0.0, A.is_equal, level, A.mult)
+        else:
+            s_tw = act(out, T.eye[:], scale=level)
+    wait("v", "gc", g_p3)
+    k = ts(T.p3m[:, 3:4], T.p3[:, 3:4], 3 * 512, A.bitwise_and)
+    k2 = ts(T.p3m[:, 0:3], T.p3[:, 0:3], 63, A.bitwise_and)
     vw(k)
-    fill(T.h16[:, 0:512:16], 0.0)
-    wait("v", "gc", g_int)
-    ts(T.pci[:], T.pi[:], 4, A.logical_shift_right)
-    k = ts(T.li[:], T.it[:], 255, A.bitwise_and)
-    ts(T.pai[:], T.pi[:], 15, A.bitwise_and)
-    ts(T.pmi[:], T.pi[:], 31, A.bitwise_and)
-    k2 = ts(T.pgi[:], T.pi[:], 4, A.logical_shift_right, 1, A.bitwise_and)
-    vw(k)
-    ts(T.gcol[:], T.pci[:], -256.0, A.mult)
-    copy(T.loc[:], T.li[:])
-    ts(T.bi[:], T.li[:], -1.0, A.mult, -0.5, A.add)
+    k_blk = ts(T.blk[:], T.p3m[:, 3:4], -float(PAD), A.add)
     vw(k2)
-    copy(T.pm[:], T.pmi[:])
-    copy(T.pg[:], T.pgi[:])
-    k = copy(T.pa[:], T.pai[:])
-    ts(T.own[:], T.pci[:], float(rank), A.is_equal)
-    ts(T.nown[:], T.pci[:], float(rank), A.not_equal)
-    ts(T.tr[:], T.li[:], 33.0, A.add)
-    wait("v", "gc", g_48)
-    vw(k)
-    ts(T.m1[:], T.trow[:], T.pm[:, 0:1], A.is_gt)
-    k = ts(T.m2[:], T.tg[:], T.pg[:, 0:1], A.is_equal)
-    ts(T.mk[:, 0:48], T.jm[:, 0:48], T.pa[:, 0:1], A.is_equal)
-    vw(k)
-    tt(T.mm[:], T.m1[:], T.m2[:], A.mult)
+    copy(T.c3[:], T.p3m[:, 0:3])
+    ts(T.s1[:], T.p3m[:, 1:2], 0.125, A.mult, 16.0, A.add)
 
-    wait("v", "lw", 128)
-    k = copy(T.z16[:, 0:512:32], T.w32[:])
-    vw(k)
-    k = hold(T.zh[:], T.hm[:, 0:512], T.z16[:])
-    vw(k)
-    k = V(vec.transpose(T.row[:], T.zh[:]))
-    vw(k)
-    k_row = ts(T.rowb[:], T.row[:], T.gcol[:, 0:1], A.add)
-    wait("s", "vs", k_row)
-    for m in range(17 - NV):
-        c = NV - 1 + m
-        s_sum = act(T.sj[:, 512 * m:512 * m + 512], T.rowb[:], Fn.Sign, bias=T.bi[:, c:c + 1], scale=1.0,
-                    accum_out=T.sa[:, m:m + 1])
-    vw(k_row)
-    for c in range(NV):
-        k = ts(T.eq[:, 512 * c:512 * c + 512], T.rowb[:], T.loc[:, c:c + 1], A.is_equal)
-    vw(k)
-    k = V(vec.tensor_tensor_scan(T.cum[:, 8:8 + 256 * NV], T.eq[:, 0:512 * NV:2], T.eq[:, 1:512 * NV:2], 0.0,
-                                 A.add, A.add))
-    vw(k)
-    tt(T.cntd[:, 0:NV], T.cum[:, 263:8 + 256 * NV:256], T.cum[:, 7:8 + 256 * (NV - 1):256], A.subtract)
-    wait("v", "ss", s_sum)
-    k = tt(T.cntd[:, NV:16], T.sa[:, 0:16 - NV], T.sa[:, 1:17 - NV], A.subtract)
-    vw(k)
-    k = ts(T.bit[:], T.cntd[:], 0.0, A.is_gt, T.nown[:, 0:1], A.mult)
-    vw(k)
-    k_pre = hold(T.pre[:], T.one[:], T.bit[:])
-    k_nb = ts(T.nbit[:], T.bit[:], -1.0, A.mult, 1.0, A.add)
-    vw(k_pre)
-    k_tot = ts(T.tot[:], T.mm[:], T.pre[:, 15:16], A.mult)
-    vw(k_nb)
-    k_zz = tt(T.zz[:], T.nbit[:], T.tr[:], A.mult)
-    vw(k_tot)
-    k_tott = V(vec.transpose(T.tott[:], T.tot[:]))
-    vw(k_zz)
-    tt(T.yy[:], T.pre[:], T.zz[:], A.max)
-    vw(k_tott)
-    k_off = V(vec.tensor_reduce(T.off[:], T.tott[:], AxisListType.X, A.add))
+    vw(k_blk)
+    wait("v", "lw", 256)
+    k_off = ts(T.off[:], T.w16[:], T.blk[:, 0:1], A.subtract, float(TOP), A.min)
+    wait("s", "vs", k_off)
+    sw(s_tw)
+    s = act(T.sr[:, 0:512], T.tw[:].indirect(T.off[:]), Fn.Relu, accum_out=T.cv[:, 255:256])
+    sw(s)
+    for m in range(1, 4):
+        s_sum = act(T.sr[:, 512 * m:512 * m + 512], T.sr[:, 0:512], Fn.Relu, bias=-float(STEP * m), scale=1.0,
+                    accum_out=T.cv[:, 256 * m + 255:256 * m + 256])
+    for h in range(2):
+        first = PAD / S + h + N - 1 - rank
+        act(T.bq[:, h:h + 1], T.blk[:], Fn.Sign, bias=first - (N - 0.5), scale=1.0 / S)
+        s = line(T.bq[:, 2 + h:3 + h], T.blk[:], C1 / S, C1 * (first - N / 2) + S - 1 - MID)
+    act(T.sg[:, 0:1], T.c3[:, 0:1], Fn.Sign, bias=-30.0, scale=1.0)
+    act(T.sg[:, 1:2], T.c3[:, 2:3], Fn.Sign, bias=-31.0, scale=1.0)
+    sw(s)
+    for h in range(2):
+        line(T.bq[:, 4 + h:5 + h], T.bq[:, h:h + 1], -C1 * N / 2, T.bq[:, 2 + h:3 + h])
+    a = PAD + S * (rank % 2)
+    wait("s", "gc", g_own)
+    s_bq = act(T.cb[home:home + 32, a:a + S], T.ownr[home:home + 32, :])
+
+    wait("v", "ss", s_tw)
     vw(k_off)
-    k_p16 = ts(T.p16[:], T.yy[:], T.off[:, 0:1], A.add, -1.0, A.add)
-    wait("v", "gc", g_all)
-    vw(k_p16)
-    k_sc = copy(T.fw[:, 0:320].indirect(T.p16[:, 0:16]), T.idr[:])
-    vw(k_sc)
-    k = tt(T.fm[:], T.fw[:, 0:32], T.mk[:, 0:32], A.mult)
+    k_rw = [ts(T.rw[:, 0:512], T.tw[:].indirect(T.off[:]), float(4 * STEP), A.subtract, 0.0, A.max)]
+    vw(k_rw[0])
+    for m in range(4):
+        if m < 3:
+            k_rw.append(ts(T.rw[:, 512 * m + 512:512 * m + 1024], T.rw[:, 0:512], float(STEP * (m + 1)), A.subtract,
+                           0.0, A.max))
+        vw(k_rw[m])
+        k = scan(T.cv[:, 1024 + 256 * m:1280 + 256 * m], T.rw[:, 512 * m:512 * m + 512:2],
+                 T.rw[:, 512 * m + 1:512 * m + 512:2], A.add, A.add)
+    wait("v", "ss", s_sum)
     vw(k)
-    k = hold(T.fs[:], T.h16[:, 0:32], T.fm[:])
+    k = tt(T.sm[:], T.cv[:, 255:2304:256], T.cv[:, 511:2560:256], A.subtract)
     vw(k)
-    k_sf = copy(T.sf[:], T.fs[:, 15:32:16])
-
-    wait("g", "vs", k_sf)
-    send(lambda i: T.sf[:], lambda j: T.lf[:, 2 * j:2 * j + 2], "af")
-
-    ts(T.tb0[:], T.pre[:], T.off[:, 0:1], A.add, T.nown[:, 0:1], A.mult)
-    k = ts(T.oc0[:], T.loc[:], -231.0, A.add, T.own[:, 0:1], A.mult)
-    tt(T.um[:, 0:24], T.fw[:, 0:24], T.mk[:, 0:24], A.mult)
-    k2 = tt(T.um[:, 24:48], T.fw[:, 0:24], T.mk[:, 24:48], A.mult)
-    fill(T.addu[:, 0:1], 0.0)
-    fill(T.addu[:, 2:3], 256.0)
+    k = ts(T.go[:], T.sm[:], 1.0 / STEP, A.mult, -0.499, A.add)
     vw(k)
-    k = ts(T.ownc[:], T.oc0[:], -1.0, A.add)
+    k = ts(T.b512[:], T.go[:, 1:9], 512.0, A.mult)
+    k2 = ts(T.a513[:], T.go[:, 0:8], float(STEP), A.mult)
+    vw(k)
+    k = tt(T.ge[:], T.sm[:, 1:9], T.b512[:], A.subtract)
+    wait("v", "gc", g_hk)
     vw(k2)
-    k2 = hold(T.us[:], T.h16[:, 0:48], T.um[:])
+    tt(T.z[:, 0:512:64], T.sm[:, 0:8], T.a513[:], A.not_equal)
     vw(k)
-    k_tb = tt(T.tb1[:], T.tb0[:], T.ownc[:], A.add)
-    k2 = ts(T.addu[:, 1:2], T.pa[:], 8.0, A.is_ge, 256.0, A.mult)
+    k = tt(T.z[:, 32:512:64], T.go[:, 0:8], T.ge[:], A.not_equal)
+    vw(k)
+    k = scan(T.zh[:], T.hk[:], T.z[:], A.mult, A.add)
+    vw(k)
+    k = turn(T.row[:], T.zh[:])
+    vw(k)
+    for h in range(2):
+        k_cw = scan(T.cw[:, S * h:S * h + S], T.row[:, S * h:S * h + S], T.row[:, S * h:S * h + S], A.add, A.max)
+    vw(k_cw)
+    k_le = [ts(T.le[:, 0:512], T.cw[:], 4.0, A.mult, T.c3[:, 0:1], A.is_le),
+            ts(T.le[:, 512:1024], T.cw[:], T.s1[:, 0:1], A.is_le)]
+    for t in range(2):
+        vw(k_le[t])
+        for h in range(2):
+            a, o = 512 * t + S * h, 128 * (2 * h + t)
+            k = scan(T.lc[:, o:o + 128], T.le[:, a:a + S:2], T.le[:, a + 1:a + S:2], A.add, A.add)
+    vw(k)
+    k_ms = ts(T.ms[:], T.lc[:, 127:512:128], float(S - 1), A.min)
+
+    wait("g", "vs", k_ms)
+    send(lambda i: T.ms[:, 2 * (other[i] % 2):2 * (other[i] % 2) + 2], lambda j: T.lf[:, 2 * j:2 * j + 2], "af", "l1")
+
+    wait("s", "vs", k_cw)
+    sw(s_bq)
+    for h in range(2):
+        parts = [(0, 128)]
+        if h == rank % 2:
+            parts = [(lo, hi) for lo, hi in ((0, home), (home + 32, 64), (max(home + 32, 64), 128)) if lo < hi]
+        for lo, hi in parts:
+            s = line(T.cb[lo:hi, PAD + S * h:PAD + S * h + S], T.cw[lo:hi, S * h:S * h + S], 1.0,
+                     T.bq[lo:hi, 4 + h:5 + h])
+    sw(s)
+    s_gm = act(T.gm[:], T.cb[:].indirect(T.off[:]))
     wait("v", "lx", 16)
     k_xq = quant(T.xq[:], T.xqs[:], T.xb[:])
-    vw(k2)
-    k = tt(T.uf[:], T.us[:, 15:48:16], T.addu[:, 0:3], A.add)
-    wait("v", "lw2", 256)
-    ts(T.u1[:], T.w16[:], 63, A.bitwise_and)
-    ts(T.u2[:], T.w16[:], 6, A.logical_shift_right)
+    wait("v", "gc", g_j)
+    ts(T.pl16[:], T.pio[:], T.c3[:, 2:3], A.add, 0.5, A.mult)
+    quant(T.xp[:, 0:S], T.xps[:, 0:S], T.xb[:])
+    wait("v", "ss", s_gm)
+    k = turn(T.gt[:], T.gm[:])
     vw(k)
-    k_su = copy(T.su[:], T.uf[:])
-    wait("g", "vs", k_su)
-    send(lambda i: T.su[:], lambda j: T.lu[:, 3 * j:3 * j + 3], "au")
-
-    wait("y", "vs", k_tb)
-    for b in range(4):
-        load("y", T.tb2[32 * b:32 * b + 32, :], T.tb1[:], "rt")
-    wait("y", "vs", k_xq)
-    load("y", T.xp[:, 0:S].bitcast(dt.uint8), T.xq[:].bitcast(dt.uint8), "xo")
-    load("y", T.xps[:, 0:S], T.xqs[:], "xo")
-    for m in range(4):
-        act(T.z2[:, 512 * m:512 * m + 512], T.hm[:, 0:512], scale=0.0)
-    for m in range(1, 4):
-        s_hm = act(T.hm[:, 512 * m:512 * m + 512], T.hm[:, 0:512])
+    k_pp = copy(T.pc[:, 48:64], T.gt[:, 0:512:32])
+    wait("y", "vs", k_pp)
+    for t in range(1, 4):
+        load("y", T.pc[0:128 - 32 * t, 16 * t - 16:16 * t], T.pc[32 * t:128, 48:64], "rp")
+        load("y", T.pc[128 - 32 * t:128, 16 * t - 16:16 * t], T.pc[0:32 * t, 48:64], "rp")
     wait("y", "af", ARR)
-    wait("s", "af", ARR)
-    for q in range(8):
-        load("ys"[q % 2], T.lr[16 * q:16 * q + 16, :], T.lf[16 * rank:16 * rank + 16, :], "rf")
-    load("y", T.vb[:], T.v[:], "lv")
-    load("y", T.ub[:], T.u[:], "lv")
-    wait("y", "au", ARR)
-    for q in range(8):
-        load("y", T.lru[16 * q:16 * q + 16, 0:21], T.lu[16 * rank:16 * rank + 16, :], "ru")
-
-    k = ts(T.u3[:], T.w16[:], 8, A.logical_shift_right)
-    vw(k)
-    k2 = ts(T.u4[:], T.u1[:], 32, A.mult)
-    k = ts(T.u5[:], T.u3[:], 8 - rank, A.add)
-    ts(T.mk[:, 48:512], T.jm[:, 48:512], T.pa[:, 0:1], A.is_equal)
-    vw(k)
-    k2 = tt(T.u6[:], T.u4[:], T.u2[:], A.add)
-    k = ts(T.u7[:], T.u5[:], 7, A.bitwise_and)
-    vw(k)
-    ts(T.bp[:], T.u7[:], 24.0, A.mult, 232.0, A.add)
-    ts(T.ef[:], T.u7[:, 0:16], 0.0, A.is_gt, 232.0, A.mult)
-    ts(T.eu[:, 16:32], T.u7[:, 16:32], 24.0, A.mult, 256.0, A.add)
-    k = ts(T.eu[:, 0:16], T.u7[:, 0:16], 24.0, A.mult)
-    copy(T.rho[:], T.u6[:])
-    vw(k)
-    tt(T.eu[:, 0:16], T.eu[:, 0:16], T.ef[:], A.add)
+    for t in range(1, 4):
+        b = (home + 32 * t) % 128
+        load("y", T.lf[b:b + 32, :], T.lf[home:home + 32, :], "rf")
+    wait("s", "gc", g_j)
+    line(T.hi8[:], T.sg[:, 0:1], S / 2, S / 2)
+    s_add = line(T.odds[:], T.sg[:, 1:2], S / 2, S / 2)
+    line(T.pm[:, 0:1], T.c3[:, 0:1], 0.25, 0.0)
+    s = line(T.pm[:, 1:2], T.c3[:, 0:1], 0.25, -6.0)
+    sw(s)
+    for c, (by, b) in enumerate(((12.0, 0), (24.0, 1), (-12.0, 0))):
+        s = line(T.pm[:, 2 + c:3 + c], T.sg[:, 0:1], by, T.pm[:, b:b + 1])
+    sw(s)
+    for c, b in enumerate((0, 2, 0, 0, 3, 4)):
+        a = 12 * (c // 3)
+        line(T.cof[:, a + c % 3:a + 12:3], T.jio[:, a + c % 3:a + 12:3], 1.0, T.pm[:, b:b + 1])
     wait("v", "la", 16)
     quant(T.aq[:, 0:512], T.aqs[:, 0:512], T.ab[:, 0:2048])
-    quant(T.aq[:, 512:1024], T.aqs[:, 512:1024], T.ab[:, 2048:4096])
-    wait("v", "rt", 64)
-    wait("v", "ss", s_hm)
-    k = copy(T.z2[:, 0:2048:32], T.tb2[:])
-    vw(k)
-    k_zh2 = hold(T.zh2[:], T.hm[:], T.z2[:])
 
-    wait("v", "rf", 128)
-    k_xs = copy(words(T.xg[:, 0:224]), words(T.xq[:, 0:S]).indirect(T.lr[:, 0:14]))
-    wait("s", "rf", 128)
+    def places():
+        wait("v", "rp", 96)
+        k = tt(T.t32[:], T.pc[:, 0:32], T.pc[:, 32:64], A.add)
+        vw(k)
+        k = tt(T.z[:, 0:512:32], T.t32[:, 0:16], T.t32[:, 16:32], A.add)
+        vw(k)
+        k = scan(T.zh[:], T.hk[:], T.z[:], A.mult, A.add)
+        vw(k)
+        return turn(T.row[:], T.zh[:])
+    if EARLY:
+        k_row = places()
+
+    wait("v", "rf", 48)
+    wait("s", "rf", 48)
     wait("s", "vs", k_xq)
-    s_xs = act(T.xgs[:, 0:224], T.xqs[:, 0:S].indirect(T.lr[:, 0:14]))
-    wait("g", "vs", k_xs)
-    send(lambda i: T.xg[:, 32 * i:32 * i + C1].bitcast(dt.uint8),
-         lambda j: T.xp[:, S + C1 * j:S + C1 * j + C1].bitcast(dt.uint8), "axc")
-    wait("g", "ss", s_xs)
-    send(lambda i: T.xgs[:, 32 * i:32 * i + C1], lambda j: T.xps[:, S + C1 * j:S + C1 * j + C1], "axs")
+    k = pick_codes("xg", 0, 224, "xq", 0, S, T.lf[:])
+    s = pick_scales("xg", 0, 224, "xq", 0, S, T.lf[:])
+    wait("g", "ss", s)
+    send(lambda i: T.xgs[:, 32 * i:32 * i + C1], lambda j: T.xps[:, S + C1 * j:S + C1 * j + C1], "axs", "l2")
+    wait("g", "vs", k)
+    send(lambda i: raw(T.xg[:, 32 * i:32 * i + C1]), lambda j: raw(T.xp[:, S + C1 * j:S + C1 * j + C1]), "axc", "l2")
 
-    vw(k_zh2)
-    k = V(vec.transpose(T.tab[:], T.zh2[:]))
+    wait("v", "ss", s_add)
+    for e in range(2):
+        ts(T.lr2[:, e:28:4], T.lf[:, 0:14:2], T.odds[:, 0:1], A.add)
+        k_lr = ts(T.lr2[:, 2 + e:28:4], T.lf[:, 1:14:2], T.hi8[:, 0:1], A.add)
+    if not EARLY:
+        k_row = places()
+    wait("s", "vs", max(k_row, k_lr))
+    s_g2 = act(T.gm2[:], T.row[:].indirect(T.lr2[:]))
+    s_g3 = act(T.gm3[:], T.row[:].indirect(T.pl16[:]))
+    wait("v", "lb", 16)
+    quant(T.aq[:, 512:1024], T.aqs[:, 512:1024], T.ab[:, 2048:4096])
+    wait("v", "ss", s_g2)
+    k = turn(T.gt2[:], T.gm2[:])
+    ts(T.co16[:], T.cof[:], 335.0, A.min)
     vw(k)
-    k = tt(T.gm[:], T.tab[:].indirect(T.rho[:, 0:32]), T.mk[:], A.mult)
+    for c, a in enumerate((0, 32, 16)):
+        k_cu = ts(T.cu[:, c:21:3], T.gt2[:, a:448:64], MID, A.add)
+    wait("v", "ss", s_g3)
+    k = turn(T.gt3[:], T.gm3[:])
     vw(k)
-    k = hold(T.gs[:], T.h16[:], T.gm[:])
-    vw(k)
-    k = tt(T.pf[:], T.gs[:, 15:512:16], T.bp[:], A.add)
-    vw(k)
-    k_po = copy(T.po16[:], T.pf[:])
-    k = tt(T.pu[:], T.pf[:], T.eu[:], A.add)
-    vw(k)
-    copy(T.pu16[:], T.pu[:])
+    k_po = ts(T.po16[:], T.gt3[:, 0:512:16], MID, A.add)
 
-    wait("v", "xo", 32)
-    wait("s", "xo", 32)
-    wait("s", "vs", k_po)
+    ps = [T.ps0, T.ps1, T.ps2, T.ps3]
+    pr = [T.pr0, T.pr1, T.pr2, T.pr3]
+
+    def layer(banks, xa, n, k_x, s_x):
+        done = [0] * 4
+        for kk in range(2):
+            wait("t", "vs", k_x[kk])
+            wait("t", "ss", s_x[kk])
+            for b in range(4):
+                done[b] = product(banks[b], "aq", 128 * (4 * kk + b), "xk", xa[kk], n, kk == 0, kk == 1)
+        return done
+
+    def relu_v(tile, n, banks, b, done):
+        wait("v", "ts", done[b])
+        return ts(tile[:, b:4 * n:4], banks[b][:, 0:n], 0.0, A.max, 0.05, A.mult)
+
+    def relu_s(tile, n, banks, b, done):
+        wait("s", "ts", done[b])
+        return act(tile[:, b:4 * n:4], banks[b][:, 0:n], Fn.Relu, scale=0.05)
+
+    po = [T.po16[:, 0:16], T.po16[:, 16:32]]
+    wait("s", "vs", k_cu)
     wait("v", "axc", ARR)
     wait("s", "axs", ARR)
-    k_xk, s_xk = [], []
-    for kk in range(2):
-        o, w = S * kk, 16 * kk
-        k_xk.append(copy(words(T.xk[:, o:o + S]), words(T.xp[:, 0:POOL]).indirect(T.po16[:, w:w + 16])))
-        s_xk.append(act(T.xks[:, o:o + S], T.xps[:, 0:POOL].indirect(T.po16[:, w:w + 16])))
-    ps = [T.ps0, T.ps1, T.ps2, T.ps3]
-    t_p = [0] * 4
-    for kk in range(2):
-        wait("t", "vs", k_xk[kk])
-        wait("t", "ss", s_xk[kk])
-        o = S * kk
-        for b in range(4):
-            w = 128 * (4 * kk + b)
-            t_p[b] = did("ts", ten.matmul_mx(ps[b][:, 0:S], T.aq[:, w:w + 128], T.aqs[:, w:w + 128],
-                                             T.xk[:, o:o + S], T.xks[:, o:o + S], kk == 0, kk == 1))
-    wait("v", "ru", 128)
-    vw(k_xk[1])
-    k_xu = copy(words(T.xu[:, 0:336]), words(T.xk[:, 0:2 * S]).indirect(T.lru[:, 0:21]))
-    wait("s", "ru", 128)
-    wait("s", "ss", s_xk[1])
-    s_xu = act(T.xus[:, 0:336], T.xks[:, 0:2 * S].indirect(T.lru[:, 0:21]))
-    wait("g", "vs", k_xu)
-    send(lambda i: T.xu[:, 48 * i:48 * i + 48].bitcast(dt.uint8),
-         lambda j: T.up[:, 512 + 48 * j:560 + 48 * j].bitcast(dt.uint8), "auc")
-    wait("g", "ss", s_xu)
-    send(lambda i: T.xus[:, 48 * i:48 * i + 48], lambda j: T.ups[:, 512 + 48 * j:560 + 48 * j], "aus")
-    wait("y", "vs", k_xk[1])
-    wait("y", "ss", s_xk[1])
-    load("y", T.up[:, 0:512].bitcast(dt.uint8), T.xk[:].bitcast(dt.uint8), "uc")
-    load("y", T.ups[:, 0:512], T.xks[:], "uc")
-    for b in range(4):
-        out = T.ht[:, b:4 * S:4]
-        if b % 2 == 0:
-            wait("s", "ts", t_p[b])
-            s_r = act(out, ps[b][:, 0:S], Fn.Relu, scale=0.05)
-        else:
-            wait("v", "ts", t_p[b])
-            k = ts(out, ps[b][:, 0:S], 0.0, A.max, 0.05, A.mult)
-    wait("v", "ss", s_r)
-    vw(k)
-    k_hq = quant(T.hq[:], T.hqs[:], T.ht[:])
-    vw(k_hq)
-    k_hs = copy(words(T.hg[:, 0:224]), words(T.hq[:, 0:S]).indirect(T.lr[:, 0:14]))
-    wait("s", "vs", k_hq)
-    s_hs = act(T.hgs[:, 0:224], T.hqs[:, 0:S].indirect(T.lr[:, 0:14]))
-    wait("g", "vs", k_hs)
-    send(lambda i: T.hg[:, 32 * i:32 * i + C1].bitcast(dt.uint8),
-         lambda j: T.hp[:, S + C1 * j:S + C1 * j + C1].bitcast(dt.uint8), "ahc")
-    wait("g", "ss", s_hs)
-    send(lambda i: T.hgs[:, 32 * i:32 * i + C1], lambda j: T.hps[:, S + C1 * j:S + C1 * j + C1], "ahs")
-    k_hp = quant(T.hp[:, 0:S], T.hps[:, 0:S], T.ht[:])
-    wait("v", "lv", 32)
-    quant(T.vq[:], T.vqs[:], T.vb[:])
+    k = pick_codes("xu", 0, 336, "xp", 0, POOL, T.cu[:, 0:21])
+    s = pick_scales("xu", 0, 336, "xp", 0, POOL, T.cu[:, 0:21])
+    wait("g", "ss", s)
+    send(lambda i: T.xus[:, 48 * i:48 * i + 48], lambda j: T.uls[:, 48 * j:48 * j + 48], "aus", "l3")
+    wait("g", "vs", k)
+    send(lambda i: raw(T.xu[:, 48 * i:48 * i + 48]), lambda j: raw(T.ul[:, 48 * j:48 * j + 48]), "auc", "l3")
+    wait("y", "l2", 2 * ARR)
+    load("y", T.ub[:], T.u[:], "lu")
+    wait("y", "l3", 2 * ARR)
+    load("y", T.vb[:], T.v[:], "lv")
+    vw(k_po)
+    wait("s", "vs", k_po)
+    k_xo = [pick_codes("xk", KW * kk, S, "xp", 0, POOL, po[kk]) for kk in range(2)]
+    s_xo = [pick_scales("xk", KW * kk, S, "xp", 0, POOL, po[kk]) for kk in range(2)]
+    t_own = layer(ps, [0, KW], S, k_xo, s_xo)
+    wait("v", "lu", 16)
     quant(T.uq[:], T.uqs[:], T.ub[:])
-
-    wait("v", "uc", 32)
-    wait("v", "auc", ARR)
-    k_yu = copy(words(T.yu[:]), words(T.up[:, 0:UPOOL]).indirect(T.pu16[:, 0:32]))
-    wait("s", "vs", k_hp)
-    wait("s", "uc", 32)
+    co = [T.co16[:, 0:11], T.co16[:, 12:23]]
     wait("s", "aus", ARR)
-    s_yu = act(T.yus[:], T.ups[:, 0:UPOOL].indirect(T.pu16[:, 0:32]))
-    wait("t", "vs", k_yu)
-    wait("t", "ss", s_yu)
+    s_xr = [pick_scales("xk", KW * kk + S, FAR, "ul", 0, 336, co[kk]) for kk in range(2)]
+    relu_s(T.ht, S, ps, 0, t_own)
+    k_r = relu_v(T.ht, S, ps, 1, t_own)
+    relu_s(T.ht, S, ps, 2, t_own)
+    s_r = relu_s(T.ht, S, ps, 3, t_own)
+    wait("v", "auc", ARR)
+    k_xr = [pick_codes("xk", KW * kk + S, FAR, "ul", 0, 336, co[kk]) for kk in range(2)]
+    t_far = layer(pr, [S, KW + S], FAR, k_xr, s_xr)
+    vw(k_xr[1])
+    sw(s_xr[1])
+    k_yu, s_yu = [0, 0], [0, 0]
     for kk in range(2):
-        o, w = S * kk, 128 * kk
-        did("ts", ten.matmul_mx(T.psy[:, 0:S], T.uq[:, w:w + 128], T.uqs[:, w:w + 128],
-                                T.yu[:, o:o + S], T.yus[:, o:o + S], kk == 0, False))
-    wait("v", "ahc", ARR)
-    wait("s", "ahs", ARR)
+        k_yu[kk] = pick_codes("yu", S * kk, S, "xk", KW * kk, KW * kk + S + FAR, po[kk])
+        s_yu[kk] = pick_scales("yu", S * kk, S, "xk", KW * kk, KW * kk + S + FAR, po[kk])
+    wait("v", "ss", s_r)
+    vw(k_r)
+    quant(T.hp[:, 0:S], T.hps[:, 0:S], T.ht[:])
+    relu_s(T.hr, FAR, pr, 0, t_far)
+    relu_v(T.hr, FAR, pr, 1, t_far)
+    s_r = relu_s(T.hr, FAR, pr, 2, t_far)
+    k_r = relu_v(T.hr, FAR, pr, 3, t_far)
+    wait("v", "lv", 16)
+    quant(T.vq[:], T.vqs[:], T.vb[:])
+    wait("v", "ss", s_r)
+    vw(k_r)
+    k_hp = quant(T.hp[:, S:S + FAR], T.hps[:, S:S + FAR], T.hr[:])
+
+    py = ps[0:2]
+    for kk in range(2):
+        wait("t", "vs", k_yu[kk])
+        wait("t", "ss", s_yu[kk])
+        for h in range(2):
+            product(py[h], "uq", 128 * kk, "yu", S * kk + 128 * h, 128, kk == 0, False)
     vw(k_hp)
-    for kk in range(2):
-        o, w = S * kk, 16 * kk
-        k = copy(words(T.yh[:, o:o + S]), words(T.hp[:, 0:POOL]).indirect(T.po16[:, w:w + 16]))
-        s = act(T.yhs[:, o:o + S], T.hps[:, 0:POOL].indirect(T.po16[:, w:w + 16]))
+    wait("s", "vs", k_hp)
+    t_y = [0, 0]
+    for kk, h, n in ((0, 0, S), (1, 0, 128), (1, 1, 128)):
+        o = S * kk + 128 * h
+        offs = T.po16[:, o // 16:(o + n) // 16]
+        k = pick_codes("yh", o, n, "hp", 0, S + FAR, offs)
+        s = pick_scales("yh", o, n, "hp", 0, S + FAR, offs)
         wait("t", "vs", k)
         wait("t", "ss", s)
-        w = 128 * kk
-        t_y = did("ts", ten.matmul_mx(T.psy[:, 0:S], T.vq[:, w:w + 128], T.vqs[:, w:w + 128],
-                                      T.yh[:, o:o + S], T.yhs[:, o:o + S], False, kk == 1))
-    wait("v", "ts", t_y)
-    k = copy(T.yo[:], T.psy[:, 0:S])
+        for hh in range(h, h + n // 128):
+            t_y[hh] = product(py[hh], "vq", 128 * kk, "yh", S * kk + 128 * hh, 128, False, kk == 1)
+    wait("s", "ts", t_y[0])
+    s = act(T.yo[:, 0:128], py[0][:, 0:128])
+    wait("v", "ts", t_y[1])
+    k = copy(T.yo[:, 128:S], py[1][:, 0:128])
+    sw(s)
+    load("s", T.y[:, 0:128], T.yo[:, 0:128], "st")
     wait("y", "vs", k)
-    load("y", T.y[:], T.yo[:], "st")
+    load("y", T.y[:, 128:S], T.yo[:, 128:S], "st")
 
-    ends = {"lw": 128, "lw2": 256, "lx": 16, "la": 16, "lv": 32, "rt": 64, "rf": 128, "ru": 128, "xo": 32, "uc": 32,
-            "ls": 8 * ARR, "af": ARR, "au": ARR, "axc": ARR, "axs": ARR, "auc": ARR, "aus": ARR, "ahc": ARR,
-            "ahs": ARR, "st": 16, **cnt}
+    ends = {"lw": 256, "lx": 16, "la": 16, "lb": 16, "lu": 16, "lv": 16, "rp": 96, "rf": 48, "l1": ARR,
+            "l2": 2 * ARR, "l3": 2 * ARR, "af": ARR, "axc": ARR, "axs": ARR, "auc": ARR, "aus": ARR, "st": 32, **cnt}
     for name in ends:
         wait("g", name, ends[name])

@@ -8,7 +8,8 @@ KW = 448
 PAD, TOP = 16, 528
 STEP = 513
 MID = 212.0
-NTV = 9
+NTV = 5
+ORDER = (0, 1, 0, 1, 0, 1, 0, 0, 1, 0, 1, 1)
 EARLY = True
 
 F32, BF, I32, U16, F16, CODE, PLANE = "float32", "bfloat16", "int32", "uint16", "float16", "float8_e4m3fn_x4", "uint8"
@@ -24,14 +25,14 @@ _sb(I32, w16=32, go=9)
 _sb(U16, off=32, pl16=32, ms=4, lf=14, lr2=28, cu=22, po16=32, co16=24)
 _sb(F16, rw=2048, lc=512)
 _sb(F32, sr=2048, cv=2560, sm=9, a513=8, b512=8, ge=8, t32=32, cof=24)
-_sb(BF, z=512, zh=512, row=512, cw=512, cb=544, le=1024, gm=512, gt=512, gm2=448, gt2=448, gm3=512, gt3=512, pc=64)
-_sb(I32, dio=32, dm=32, p3=4, p3m=4)
-_sb(F32, eye=32, tw=544, blk=1, bq=6, sg=2, hi8=1, odds=1, pm=5, jio=24, pio=32)
-_sb(BF, one=512, hk=512, ownr=S, c3=3, s1=1)
-_sb(BF, xb=1024, ab=4096, vb=1024, ub=1024, ht=1024, hr=4 * FAR)
+_sb(BF, z=512, zh=512, row=512, cb=544, le=1024, gm=512, gt=512, gm2=448, gt2=448, gm3=512, gt3=512, pc=64)
+_sb(I32, dio=32, dm=32, p3=4, p3m=4, bq=4)
+_sb(F32, tw=544, blk=1, hrow=2, sg=2, hi8=1, odds=1, pm=5, jio=24, pio=32)
+_sb(BF, one=S, hm=512, hk=512, ownr=S, c3=3, bh=2, sl=2)
+_sb(BF, xb=1024, ab=4096, vb=1024, ub=1024, ht=1024, hr=4 * (POOL - S))
 _sb(F32, yo=S)
 for _n, _w in dict(aq=1024, vq=256, uq=256, xq=S, xg=224, xp=POOL, xu=336, ul=336, xk=2 * KW, yu=512,
-                   hp=S + FAR, yh=512).items():
+                   hp=POOL, yh=512).items():
     SCRATCH[_n] = ("sbuf", [128, _w], CODE)
     SCRATCH[_n + "s"] = ("sbuf", [128, _w], PLANE)
 for _n in ("ps0", "ps1", "ps2", "ps3", "pr0", "pr1", "pr2", "pr3"):
@@ -89,8 +90,8 @@ def rank_program(g, core, T, topo):
     def quant(out, sc, in_):
         return did("vs", vec.quantize_mx(out, sc, in_))
 
-    def scan(out, d0, d1, op0, op1):
-        return did("vs", vec.tensor_tensor_scan(out, d0, d1, 0.0, op0, op1))
+    def scan(out, d0, d1, op0, op1, first=0.0):
+        return did("vs", vec.tensor_tensor_scan(out, d0, d1, first, op0, op1))
 
     def turn(out, in_):
         return did("vs", vec.transpose(out, in_))
@@ -121,26 +122,23 @@ def rank_program(g, core, T, topo):
 
     other = [(rank + 1 + i) % N for i in range(N - 1)]
     dest = [T.cores[q] for q in other]
-    masks = [0] * (N - 1)
-    near, far = 0, 0
-    for i, d in enumerate(dest):
-        e = topo.engines(core, d)
-        if topo.die(d) != topo.die(core):
-            masks[i] = (1 << e[4 * far]) | (1 << e[4 * far + 2])
-            far += 1
-        else:
-            masks[i] = (1 << e[4 * near + 1]) | (1 << e[4 * near + 3])
-            near += 1
+    every, halves = list(range(N - 1)), [list(range(0, N - 1, 2)), list(range(1, N - 1, 2))]
 
-    def send(src, dst, name, left):
+    masks, used = [], [0, 0]
+    for d in dest:
+        near = int(topo.die(d) == topo.die(core))
+        masks.append(sum(1 << n for n in topo.engines(core, d)[near::2][used[near]:used[near] + 2]))
+        used[near] += 2
+
+    def send(src, dst, name, left, places=every):
         tr = []
-        for i, d in enumerate(dest):
-            rid, pid, _e = topo.addr(d)
+        for i in places:
+            rid, pid, _e = topo.addr(dest[i])
             tr.append(RemoteDMATransfer(dst_ids=[DstId(rid=rid, pnc=pid)], dma_engine_mask=masks[i],
                                         remote_sem=sem[name], src=src(i), dst=dst(6 - i)))
         g.remote_dma_fused(tr, local_sem=sem[left])
 
-    ARR = 2 * (N - 1)
+    ARR = WIDE = 2 * (N - 1)
     home = 32 * (rank // 2)
 
     for q in range(8):
@@ -149,17 +147,18 @@ def rank_program(g, core, T, topo):
     load("y", T.xb[:], T.x[:], "lx")
     load("y", T.ab[:, 0:2048], T.a[:, 0:2048], "la")
     load("y", T.ab[:, 2048:4096], T.a[:, 2048:4096], "lb")
+    load("y", T.vb[:], T.v[:], "lv")
 
     g_dio = iota(T.dio[:], [[1, 32]], 128, -1, True)
     for c in range(4):
         g_p3 = iota(T.p3[:, c:c + 1], [[1, 1]], 0, (4, 8, 2, 16)[c], True)
-    k = iota(T.one[:], [[0, 512]], 1, 0)
+    g_h = iota(T.hrow[:], [[S, 2]], PAD + S * (N - 1 - rank), 0)
     iota(T.z[:], [[0, 512]], 0, 0)
-    wait("g", "gc", k)
-    g_hk = did("gc", g.affine_select(T.hk[:], T.one[:], [[0, 16], [1, 32]], A.not_equal, 0.0, 0, 0))
-    iota(T.cb[:, 0:PAD], [[0, PAD]], 0, 0)
-    iota(T.cb[:, TOP:TOP + 16], [[0, 16]], 0, 0)
+    g_hm = iota(T.hm[:], [[0, 16], [1, 32]], 0, 0)
     g_own = iota(T.ownr[:], [[1, S]], -int(MID), 0)
+    g_one = iota(T.one[:], [[0, S]], 1, 0)
+    iota(T.cb[:, 0:PAD], [[0, PAD]], 0, 0)
+    g_pad = iota(T.cb[:, TOP:TOP + 16], [[0, 16]], 0, 0)
     iota(T.pio[:], [[64, 16], [0, 2]], 0, 0)
     iota(T.jio[:, 0:12], [[96, 4], [28, 3]], 0, 0)
     g_j = iota(T.jio[:, 12:24], [[96, 4], [22, 3]], 32, 0)
@@ -170,14 +169,16 @@ def rank_program(g, core, T, topo):
     wait("v", "gc", g_dio)
     k = ts(T.dm[:], T.dio[:], 31, A.bitwise_and)
     vw(k)
-    k_eye = ts(T.eye[:], T.dm[:], 0.0, A.is_equal)
-    wait("s", "vs", k_eye)
-    for c in range(16):
-        level, out = float(STEP * (c // 2) + 1 + 512 * (c % 2)), T.tw[:, PAD + 32 * c:PAD + 32 * c + 32]
-        if c < NTV:
-            ts(out, T.dm[:], 0.0, A.is_equal, level, A.mult)
+    for c in range(2):
+        k_tw = ts(T.tw[:, PAD + 32 * c:PAD + 32 * c + 32], T.dm[:], -8192.0, A.mult, 1.0 + 512 * c, A.add)
+    wait("s", "vs", k_tw)
+    vw(k_tw)
+    for m in range(1, 8):
+        out = T.tw[:, PAD + 64 * m:PAD + 64 * m + 64]
+        if m < NTV:
+            ts(out, T.tw[:, PAD:PAD + 64], float(STEP * m), A.add)
         else:
-            s_tw = act(out, T.eye[:], scale=level)
+            s_tw = line(out, T.tw[:, PAD:PAD + 64], 1.0, float(STEP * m))
     wait("v", "gc", g_p3)
     k = ts(T.p3m[:, 3:4], T.p3[:, 3:4], 3 * 512, A.bitwise_and)
     k2 = ts(T.p3m[:, 0:3], T.p3[:, 0:3], 63, A.bitwise_and)
@@ -185,7 +186,6 @@ def rank_program(g, core, T, topo):
     k_blk = ts(T.blk[:], T.p3m[:, 3:4], -float(PAD), A.add)
     vw(k2)
     copy(T.c3[:], T.p3m[:, 0:3])
-    ts(T.s1[:], T.p3m[:, 1:2], 0.125, A.mult, 16.0, A.add)
 
     vw(k_blk)
     wait("v", "lw", 256)
@@ -197,18 +197,18 @@ def rank_program(g, core, T, topo):
     for m in range(1, 4):
         s_sum = act(T.sr[:, 512 * m:512 * m + 512], T.sr[:, 0:512], Fn.Relu, bias=-float(STEP * m), scale=1.0,
                     accum_out=T.cv[:, 256 * m + 255:256 * m + 256])
-    for h in range(2):
-        first = PAD / S + h + N - 1 - rank
-        act(T.bq[:, h:h + 1], T.blk[:], Fn.Sign, bias=first - (N - 0.5), scale=1.0 / S)
-        s = line(T.bq[:, 2 + h:3 + h], T.blk[:], C1 / S, C1 * (first - N / 2) + S - 1 - MID)
-    act(T.sg[:, 0:1], T.c3[:, 0:1], Fn.Sign, bias=-30.0, scale=1.0)
-    act(T.sg[:, 1:2], T.c3[:, 2:3], Fn.Sign, bias=-31.0, scale=1.0)
-    sw(s)
-    for h in range(2):
-        line(T.bq[:, 4 + h:5 + h], T.bq[:, h:h + 1], -C1 * N / 2, T.bq[:, 2 + h:3 + h])
+    line(T.sl[:, 0:1], T.c3[:, 0:1], 0.25, 0.0)
+    line(T.sl[:, 1:2], T.c3[:, 1:2], 0.125, 16.0)
     a = PAD + S * (rank % 2)
     wait("s", "gc", g_own)
     s_bq = act(T.cb[home:home + 32, a:a + S], T.ownr[home:home + 32, :])
+    act(T.sg[:, 0:1], T.c3[:, 0:1], Fn.Sign, bias=-30.0, scale=1.0)
+    act(T.sg[:, 1:2], T.c3[:, 2:3], Fn.Sign, bias=-31.0, scale=1.0)
+    line(T.pm[:, 0:1], T.c3[:, 0:1], 0.25, 0.0)
+    s = line(T.pm[:, 1:2], T.c3[:, 0:1], 0.25, -6.0)
+    sw(s)
+    line(T.hi8[:], T.sg[:, 0:1], S / 2, S / 2)
+    s_add = line(T.odds[:], T.sg[:, 1:2], S / 2, S / 2)
 
     wait("v", "ss", s_tw)
     vw(k_off)
@@ -221,90 +221,113 @@ def rank_program(g, core, T, topo):
         vw(k_rw[m])
         k = scan(T.cv[:, 1024 + 256 * m:1280 + 256 * m], T.rw[:, 512 * m:512 * m + 512:2],
                  T.rw[:, 512 * m + 1:512 * m + 512:2], A.add, A.add)
+    wait("v", "gc", g_h)
+    ts(T.bq[:, 0:2], T.hrow[:], T.blk[:, 0:1], A.add, 1.0 / S, A.mult)
     wait("v", "ss", s_sum)
-    vw(k)
+    vw(k + 1)
     k = tt(T.sm[:], T.cv[:, 255:2304:256], T.cv[:, 511:2560:256], A.subtract)
+    ts(T.bq[:, 2:4], T.bq[:, 0:2], N - 1, A.bitwise_and)
     vw(k)
     k = ts(T.go[:], T.sm[:], 1.0 / STEP, A.mult, -0.499, A.add)
+    vw(k - 1)
+    ts(T.bh[:], T.bq[:, 2:4], float(C1), A.mult, S - 1 - MID, A.add)
     vw(k)
     k = ts(T.b512[:], T.go[:, 1:9], 512.0, A.mult)
     k2 = ts(T.a513[:], T.go[:, 0:8], float(STEP), A.mult)
     vw(k)
     k = tt(T.ge[:], T.sm[:, 1:9], T.b512[:], A.subtract)
-    wait("v", "gc", g_hk)
+    wait("v", "gc", g_hm)
     vw(k2)
     tt(T.z[:, 0:512:64], T.sm[:, 0:8], T.a513[:], A.not_equal)
     vw(k)
     k = tt(T.z[:, 32:512:64], T.go[:, 0:8], T.ge[:], A.not_equal)
     vw(k)
-    k = scan(T.zh[:], T.hk[:], T.z[:], A.mult, A.add)
-    vw(k)
-    k = turn(T.row[:], T.zh[:])
-    vw(k)
-    for h in range(2):
-        k_cw = scan(T.cw[:, S * h:S * h + S], T.row[:, S * h:S * h + S], T.row[:, S * h:S * h + S], A.add, A.max)
-    vw(k_cw)
-    k_le = [ts(T.le[:, 0:512], T.cw[:], 4.0, A.mult, T.c3[:, 0:1], A.is_le),
-            ts(T.le[:, 512:1024], T.cw[:], T.s1[:, 0:1], A.is_le)]
-    for t in range(2):
-        vw(k_le[t])
-        for h in range(2):
-            a, o = 512 * t + S * h, 128 * (2 * h + t)
-            k = scan(T.lc[:, o:o + 128], T.le[:, a:a + S:2], T.le[:, a + 1:a + S:2], A.add, A.add)
-    vw(k)
-    k_ms = ts(T.ms[:], T.lc[:, 127:512:128], float(S - 1), A.min)
+    last = [k, k]
 
-    wait("g", "vs", k_ms)
-    send(lambda i: T.ms[:, 2 * (other[i] % 2):2 * (other[i] % 2) + 2], lambda j: T.lf[:, 2 * j:2 * j + 2], "af", "l1")
+    def hold(h):
+        last[h] = scan(T.zh[:, S * h:S * h + S], T.hm[:, S * h:S * h + S], T.z[:, S * h:S * h + S], A.min, A.add)
 
-    wait("s", "vs", k_cw)
-    sw(s_bq)
-    for h in range(2):
+    def across(h):
+        last[h] = turn(T.row[:, S * h:S * h + S], T.zh[:, S * h:S * h + S])
+
+    def number(h):
+        wait("v", "gc", g_one)
+        wait("v", "ss", s_bq)
         parts = [(0, 128)]
         if h == rank % 2:
             parts = [(lo, hi) for lo, hi in ((0, home), (home + 32, 64), (max(home + 32, 64), 128)) if lo < hi]
         for lo, hi in parts:
-            s = line(T.cb[lo:hi, PAD + S * h:PAD + S * h + S], T.cw[lo:hi, S * h:S * h + S], 1.0,
-                     T.bq[lo:hi, 4 + h:5 + h])
-    sw(s)
+            last[h] = scan(T.cb[lo:hi, PAD + S * h:PAD + S * h + S], T.row[lo:hi, S * h:S * h + S], T.one[lo:hi, 0:S],
+                           A.add, A.mult, T.bh[lo:hi, h:h + 1])
+        k_cw.append(last[h])
+
+    def under(h):
+        for c in (2 * h, 2 * h + 1):
+            last[h] = ts(T.le[:, S * c:S * c + S], T.cb[:, PAD + S * h:PAD + S * h + S], T.bh[:, h:h + 1], A.subtract,
+                         T.sl[:, c % 2:c % 2 + 1], A.is_le)
+
+    def count(h):
+        for c in (2 * h, 2 * h + 1):
+            last[h] = scan(T.lc[:, 128 * c:128 * c + 128], T.le[:, S * c:S * c + S:2], T.le[:, S * c + 1:S * c + S:2],
+                           A.add, A.add)
+
+    def request(h):
+        k = ts(T.ms[:, 2 * h:2 * h + 2], T.lc[:, 256 * h + 127:256 * h + 256:128], float(S - 1), A.min)
+        wait("g", "vs", k)
+        send(lambda i: T.ms[:, 2 * h:2 * h + 2], lambda j: T.lf[:, 2 * j:2 * j + 2], "af", "l1",
+             halves[int(h == rank % 2)])
+    k_cw, steps, done = [], [hold, across, number, under, count, request], [0, 0]
+    for part in ORDER:
+        h = (rank + 1 + part) % 2
+        vw(last[h])
+        steps[done[part]](h)
+        done[part] += 1
+
+    wait("s", "gc", g_pad)
+    wait("s", "vs", max(k_cw))
     s_gm = act(T.gm[:], T.cb[:].indirect(T.off[:]))
-    wait("v", "lx", 16)
-    k_xq = quant(T.xq[:], T.xqs[:], T.xb[:])
-    wait("v", "gc", g_j)
-    ts(T.pl16[:], T.pio[:], T.c3[:, 2:3], A.add, 0.5, A.mult)
-    quant(T.xp[:, 0:S], T.xps[:, 0:S], T.xb[:])
+    s_hk = act(T.hk[:], T.hm[:], Fn.Sign)
     wait("v", "ss", s_gm)
     k = turn(T.gt[:], T.gm[:])
+    wait("v", "gc", g_j)
+    ts(T.pl16[:], T.pio[:], T.c3[:, 2:3], A.add, 0.5, A.mult)
     vw(k)
     k_pp = copy(T.pc[:, 48:64], T.gt[:, 0:512:32])
+    wait("v", "lx", 16)
+    k_xq = quant(T.xq[:], T.xqs[:], T.xb[:])
+    quant(T.xp[:, 0:S], T.xps[:, 0:S], T.xb[:])
     wait("y", "vs", k_pp)
     for t in range(1, 4):
         load("y", T.pc[0:128 - 32 * t, 16 * t - 16:16 * t], T.pc[32 * t:128, 48:64], "rp")
         load("y", T.pc[128 - 32 * t:128, 16 * t - 16:16 * t], T.pc[0:32 * t, 48:64], "rp")
-    wait("y", "af", ARR)
-    for t in range(1, 4):
+    def spread(q, t):
         b = (home + 32 * t) % 128
-        load("y", T.lf[b:b + 32, :], T.lf[home:home + 32, :], "rf")
+        wait(q, "af", WIDE)
+        load(q, T.lf[b:b + 32, :], T.lf[home:home + 32, :], "rf")
+    spread("y", 1)
+    spread("y", 2)
+    load("y", T.ub[:], T.u[:], "lu")
     wait("s", "gc", g_j)
-    line(T.hi8[:], T.sg[:, 0:1], S / 2, S / 2)
-    s_add = line(T.odds[:], T.sg[:, 1:2], S / 2, S / 2)
-    line(T.pm[:, 0:1], T.c3[:, 0:1], 0.25, 0.0)
-    s = line(T.pm[:, 1:2], T.c3[:, 0:1], 0.25, -6.0)
-    sw(s)
     for c, (by, b) in enumerate(((12.0, 0), (24.0, 1), (-12.0, 0))):
         s = line(T.pm[:, 2 + c:3 + c], T.sg[:, 0:1], by, T.pm[:, b:b + 1])
     sw(s)
     for c, b in enumerate((0, 2, 0, 0, 3, 4)):
         a = 12 * (c // 3)
         line(T.cof[:, a + c % 3:a + 12:3], T.jio[:, a + c % 3:a + 12:3], 1.0, T.pm[:, b:b + 1])
+    spread("s", 3)
     wait("v", "la", 16)
     quant(T.aq[:, 0:512], T.aqs[:, 0:512], T.ab[:, 0:2048])
+    wait("v", "lb", 16)
+    quant(T.aq[:, 512:1024], T.aqs[:, 512:1024], T.ab[:, 2048:4096])
+    wait("v", "lv", 16)
+    quant(T.vq[:], T.vqs[:], T.vb[:])
 
     def places():
         wait("v", "rp", 96)
         k = tt(T.t32[:], T.pc[:, 0:32], T.pc[:, 32:64], A.add)
         vw(k)
         k = tt(T.z[:, 0:512:32], T.t32[:, 0:16], T.t32[:, 16:32], A.add)
+        wait("v", "ss", s_hk)
         vw(k)
         k = scan(T.zh[:], T.hk[:], T.z[:], A.mult, A.add)
         vw(k)
@@ -329,11 +352,12 @@ def rank_program(g, core, T, topo):
     if not EARLY:
         k_row = places()
     wait("s", "vs", max(k_row, k_lr))
-    s_g2 = act(T.gm2[:], T.row[:].indirect(T.lr2[:]))
+    s_g2 = act(T.gm2[:, 256:448], T.row[:].indirect(T.lr2[:, 16:28]))
     s_g3 = act(T.gm3[:], T.row[:].indirect(T.pl16[:]))
-    wait("v", "lb", 16)
-    quant(T.aq[:, 512:1024], T.aqs[:, 512:1024], T.ab[:, 2048:4096])
+    vw(max(k_row, k_lr))
+    k = copy(T.gm2[:, 0:256], T.row[:].indirect(T.lr2[:, 0:16]))
     wait("v", "ss", s_g2)
+    vw(k)
     k = turn(T.gt2[:], T.gm2[:])
     ts(T.co16[:], T.cof[:], 335.0, A.min)
     vw(k)
@@ -366,55 +390,50 @@ def rank_program(g, core, T, topo):
 
     po = [T.po16[:, 0:16], T.po16[:, 16:32]]
     wait("s", "vs", k_cu)
+    vw(k_cu)
     wait("v", "axc", ARR)
     wait("s", "axs", ARR)
     k = pick_codes("xu", 0, 336, "xp", 0, POOL, T.cu[:, 0:21])
     s = pick_scales("xu", 0, 336, "xp", 0, POOL, T.cu[:, 0:21])
+    wait("s", "vs", k_po)
+    s_xo = [pick_scales("xk", KW * kk, S, "xp", 0, POOL, po[kk]) for kk in range(2)]
     wait("g", "ss", s)
     send(lambda i: T.xus[:, 48 * i:48 * i + 48], lambda j: T.uls[:, 48 * j:48 * j + 48], "aus", "l3")
     wait("g", "vs", k)
     send(lambda i: raw(T.xu[:, 48 * i:48 * i + 48]), lambda j: raw(T.ul[:, 48 * j:48 * j + 48]), "auc", "l3")
-    wait("y", "l2", 2 * ARR)
-    load("y", T.ub[:], T.u[:], "lu")
-    wait("y", "l3", 2 * ARR)
-    load("y", T.vb[:], T.v[:], "lv")
     vw(k_po)
-    wait("s", "vs", k_po)
     k_xo = [pick_codes("xk", KW * kk, S, "xp", 0, POOL, po[kk]) for kk in range(2)]
-    s_xo = [pick_scales("xk", KW * kk, S, "xp", 0, POOL, po[kk]) for kk in range(2)]
     t_own = layer(ps, [0, KW], S, k_xo, s_xo)
     wait("v", "lu", 16)
     quant(T.uq[:], T.uqs[:], T.ub[:])
     co = [T.co16[:, 0:11], T.co16[:, 12:23]]
     wait("s", "aus", ARR)
     s_xr = [pick_scales("xk", KW * kk + S, FAR, "ul", 0, 336, co[kk]) for kk in range(2)]
-    relu_s(T.ht, S, ps, 0, t_own)
-    k_r = relu_v(T.ht, S, ps, 1, t_own)
-    relu_s(T.ht, S, ps, 2, t_own)
-    s_r = relu_s(T.ht, S, ps, 3, t_own)
+    sw(s_xr[0])
+    s_yu = [pick_scales("yu", 0, S, "xk", 0, S + FAR, po[0])]
+    for b in range(2):
+        k_r = relu_v(T.ht, S, ps, b, t_own)
+        s_r = relu_s(T.ht, S, ps, 2 + b, t_own)
+    sw(s_xr[1])
+    s_yu.append(pick_scales("yu", S, S, "xk", KW, KW + S + FAR, po[1]))
     wait("v", "auc", ARR)
     k_xr = [pick_codes("xk", KW * kk + S, FAR, "ul", 0, 336, co[kk]) for kk in range(2)]
-    t_far = layer(pr, [S, KW + S], FAR, k_xr, s_xr)
-    vw(k_xr[1])
-    sw(s_xr[1])
-    k_yu, s_yu = [0, 0], [0, 0]
-    for kk in range(2):
-        k_yu[kk] = pick_codes("yu", S * kk, S, "xk", KW * kk, KW * kk + S + FAR, po[kk])
-        s_yu[kk] = pick_scales("yu", S * kk, S, "xk", KW * kk, KW * kk + S + FAR, po[kk])
+    t_far = layer(pr, [S, KW + S], POOL - S, k_xr, s_xr)
+    vw(k_xr[0])
+    k_yu = [pick_codes("yu", 0, S, "xk", 0, S + FAR, po[0])]
     wait("v", "ss", s_r)
-    vw(k_r)
     quant(T.hp[:, 0:S], T.hps[:, 0:S], T.ht[:])
-    relu_s(T.hr, FAR, pr, 0, t_far)
-    relu_v(T.hr, FAR, pr, 1, t_far)
-    s_r = relu_s(T.hr, FAR, pr, 2, t_far)
-    k_r = relu_v(T.hr, FAR, pr, 3, t_far)
-    wait("v", "lv", 16)
-    quant(T.vq[:], T.vqs[:], T.vb[:])
+    vw(k_xr[1])
+    k_yu.append(pick_codes("yu", S, S, "xk", KW, KW + S + FAR, po[1]))
+    for b in (0, 2):
+        s_r = relu_s(T.hr, POOL - S, pr, b, t_far)
+        k_r = relu_v(T.hr, POOL - S, pr, b + 1, t_far)
     wait("v", "ss", s_r)
     vw(k_r)
-    k_hp = quant(T.hp[:, S:S + FAR], T.hps[:, S:S + FAR], T.hr[:])
+    k_hp = quant(T.hp[:, S:POOL], T.hps[:, S:POOL], T.hr[:])
 
     py = ps[0:2]
+    wait("t", "ss", s_yu[1])
     for kk in range(2):
         wait("t", "vs", k_yu[kk])
         wait("t", "ss", s_yu[kk])
@@ -426,8 +445,8 @@ def rank_program(g, core, T, topo):
     for kk, h, n in ((0, 0, S), (1, 0, 128), (1, 1, 128)):
         o = S * kk + 128 * h
         offs = T.po16[:, o // 16:(o + n) // 16]
-        k = pick_codes("yh", o, n, "hp", 0, S + FAR, offs)
-        s = pick_scales("yh", o, n, "hp", 0, S + FAR, offs)
+        k = pick_codes("yh", o, n, "hp", 0, POOL, offs)
+        s = pick_scales("yh", o, n, "hp", 0, POOL, offs)
         wait("t", "vs", k)
         wait("t", "ss", s)
         for hh in range(h, h + n // 128):
@@ -441,7 +460,7 @@ def rank_program(g, core, T, topo):
     wait("y", "vs", k)
     load("y", T.y[:, 128:S], T.yo[:, 128:S], "st")
 
-    ends = {"lw": 256, "lx": 16, "la": 16, "lb": 16, "lu": 16, "lv": 16, "rp": 96, "rf": 48, "l1": ARR,
-            "l2": 2 * ARR, "l3": 2 * ARR, "af": ARR, "axc": ARR, "axs": ARR, "auc": ARR, "aus": ARR, "st": 32, **cnt}
+    ends = {"lw": 256, "lx": 16, "la": 16, "lb": 16, "lu": 16, "lv": 16, "rp": 96, "rf": 48, "l1": WIDE,
+            "l2": 2 * ARR, "l3": 2 * ARR, "af": WIDE, "axc": ARR, "axs": ARR, "auc": ARR, "aus": ARR, "st": 32, **cnt}
     for name in ends:
         wait("g", name, ends[name])

@@ -7,10 +7,12 @@ POOL = S + 7 * C1
 KW = 448
 PAD, TOP = 16, 528
 STEP = 513
-MID = 212.0
-NTV = 5
-ORDER = (0, 1, 0, 1, 0, 1, 0, 0, 1, 0, 1, 1)
-EARLY = True
+MID = 212
+WHOLE = 3 << 22
+NTV = 6
+NSV = 3
+ORDER = "aaaaapababababbbbbb"
+Q1, Q2, GV, OWNV = 8, 6, 16, (1,)
 
 F32, BF, I32, U16, F16, CODE, PLANE = "float32", "bfloat16", "int32", "uint16", "float16", "float8_e4m3fn_x4", "uint8"
 SCRATCH = {}
@@ -21,14 +23,14 @@ def _sb(dtype, **bufs):
         SCRATCH[name] = ("sbuf", [128, bufs[name]], dtype)
 
 
-_sb(I32, w16=32, go=9)
-_sb(U16, off=32, pl16=32, ms=4, lf=14, lr2=28, cu=22, po16=32, co16=24)
+_sb(I32, w16=32)
+_sb(U16, off=32, pl16=32, ms=4, lf=14, lr2=28, po16=54, co16=24)
 _sb(F16, rw=2048, lc=512)
-_sb(F32, sr=2048, cv=2560, sm=9, a513=8, b512=8, ge=8, t32=32, cof=24)
-_sb(BF, z=512, zh=512, row=512, cb=544, le=1024, gm=512, gt=512, gm2=448, gt2=448, gm3=512, gt3=512, pc=64)
-_sb(I32, dio=32, dm=32, p3=4, p3m=4, bq=4)
-_sb(F32, tw=544, blk=1, hrow=2, sg=2, hi8=1, odds=1, pm=5, jio=24, pio=32)
-_sb(BF, one=S, hm=512, hk=512, ownr=S, c3=3, bh=2, sl=2)
+_sb(F32, sr=2560, cv=2304, dd=64, go=68, cof=24)
+_sb(BF, z=512, zh=512, row=512, cb=544, le=1024, gm=512, gm2=448, gt2=448, gm3=512, gt3=512, pc=53, pd=53)
+_sb(I32, dio=64, dm=64, pm2=2)
+_sb(F32, tw=544, d0=32, sg=2, hi8=1, odds=1, p32=1, pm=4, jio=24, pio=32)
+_sb(BF, one=S, hm=S, bq=8, sl=2)
 _sb(BF, xb=1024, ab=4096, vb=1024, ub=1024, ht=1024, hr=4 * (POOL - S))
 _sb(F32, yo=S)
 for _n, _w in dict(aq=1024, vq=256, uq=256, xq=S, xg=224, xp=POOL, xu=336, ul=336, xk=2 * KW, yu=512,
@@ -37,7 +39,7 @@ for _n, _w in dict(aq=1024, vq=256, uq=256, xq=S, xg=224, xp=POOL, xu=336, ul=33
     SCRATCH[_n + "s"] = ("sbuf", [128, _w], PLANE)
 for _n in ("ps0", "ps1", "ps2", "ps3", "pr0", "pr1", "pr2", "pr3"):
     SCRATCH[_n] = ("psum", [128, 512], F32)
-SEMAPHORES = ["lw", "lx", "la", "lb", "lu", "lv", "vs", "ss", "ts", "gc", "rp", "rf", "st", "l1", "l2", "l3",
+SEMAPHORES = ["lw", "lx", "la", "lb", "lu", "lv", "vs", "ss", "ts", "gc", "st", "l1", "l2", "l3",
               "af", "axc", "axs", "auc", "aus"]
 
 
@@ -129,17 +131,25 @@ def rank_program(g, core, T, topo):
         near = int(topo.die(d) == topo.die(core))
         masks.append(sum(1 << n for n in topo.engines(core, d)[near::2][used[near]:used[near] + 2]))
         used[near] += 2
+    wide = {}
+    for places in halves:
+        a = 0
+        for i in places:
+            n = 8 if len(places) == 3 and i == places[-1] else 4
+            wide[i] = sum(1 << e for e in topo.engines(core, dest[i])[a:a + n])
+            a += n
 
-    def send(src, dst, name, left, places=every):
+    def send(src, dst, name, left, places=every, mask=masks):
         tr = []
         for i in places:
             rid, pid, _e = topo.addr(dest[i])
-            tr.append(RemoteDMATransfer(dst_ids=[DstId(rid=rid, pnc=pid)], dma_engine_mask=masks[i],
+            tr.append(RemoteDMATransfer(dst_ids=[DstId(rid=rid, pnc=pid)], dma_engine_mask=mask[i],
                                         remote_sem=sem[name], src=src(i), dst=dst(6 - i)))
         g.remote_dma_fused(tr, local_sem=sem[left])
 
-    ARR = WIDE = 2 * (N - 1)
+    ARR, WIDE = 2 * (N - 1), 32
     home = 32 * (rank // 2)
+    lead, mine = (rank + 1) % 2, rank % 2
 
     for q in range(8):
         load("y", T.w16[16 * q:16 * q + 16, 0:16], T.nb0[:], "lw")
@@ -147,226 +157,229 @@ def rank_program(g, core, T, topo):
     load("y", T.xb[:], T.x[:], "lx")
     load("y", T.ab[:, 0:2048], T.a[:, 0:2048], "la")
     load("y", T.ab[:, 2048:4096], T.a[:, 2048:4096], "lb")
+    load("y", T.ub[:], T.u[:], "lu")
     load("y", T.vb[:], T.v[:], "lv")
 
-    g_dio = iota(T.dio[:], [[1, 32]], 128, -1, True)
-    for c in range(4):
-        g_p3 = iota(T.p3[:, c:c + 1], [[1, 1]], 0, (4, 8, 2, 16)[c], True)
-    g_h = iota(T.hrow[:], [[S, 2]], PAD + S * (N - 1 - rank), 0)
-    iota(T.z[:], [[0, 512]], 0, 0)
-    g_hm = iota(T.hm[:], [[0, 16], [1, 32]], 0, 0)
-    g_own = iota(T.ownr[:], [[1, S]], -int(MID), 0)
+    g_dio = iota(T.dio[:], [[1, 2], [-16, 32]], 2048, 16, True)
+    for b in range(4):
+        first = [-1 - MID if q == rank else S + C1 * ((q - rank - 1) % N) - 1 - MID for q in (2 * b, 2 * b + 1)]
+        g_bq = iota(T.bq[32 * b:32 * b + 32, :], [[int(32 * b == home) - first[0], 2], [512 * b - PAD - first[0], 2],
+                                                  [first[1] - first[0], 2]], first[0], 0)
+        wait("g", "gc", g_bq if b == 3 else g_dio)
+    bh, blk, here = [T.bq[:, 0:1], T.bq[:, 1:2]], T.bq[:, 2:3], T.bq[:, 4:5]
+    iota(T.d0[:, 1:32:2], [[0, 16]], 1, 0)
+    iota(T.d0[:, 0:32:4], [[0, 4], [1 - STEP, 2]], 0, 0)
+    iota(T.d0[:, 6:32:8], [[0, 4]], 1, 0)
+    iota(T.dd[:, 1:64:4], [[0, 8], [256, 2]], -256, 0)
+    iota(T.dd[:, 2:64:8], [[0, 8]], WHOLE, 0)
+    iota(T.dd[:, 3:64:8], [[0, 8]], -WHOLE, 0)
+    iota(T.dd[:, 6:64:8], [[0, 8]], 0, 0)
+    g_dd = iota(T.dd[:, 7:64:8], [[0, 8]], 0, 0)
+    g_hm = iota(T.hm[:], [[0, 8], [1, 32]], 0, 0)
     g_one = iota(T.one[:], [[0, S]], 1, 0)
     iota(T.cb[:, 0:PAD], [[0, PAD]], 0, 0)
     g_pad = iota(T.cb[:, TOP:TOP + 16], [[0, 16]], 0, 0)
-    iota(T.pio[:], [[64, 16], [0, 2]], 0, 0)
+    g_pio = iota(T.pio[:], [[32, 16], [0, 2]], 0, 0)
     iota(T.jio[:, 0:12], [[96, 4], [28, 3]], 0, 0)
     g_j = iota(T.jio[:, 12:24], [[96, 4], [22, 3]], 32, 0)
 
     fill(T.tw[:, 0:PAD], 0.0)
     fill(T.tw[:, TOP:TOP + 16], 0.0)
-    fill(T.cv[:, 2303:2560:256], 0.0)
+    fill(T.z[:, S * lead:S * lead + S], 0.0)
+    fill(T.cv[:, 255:256], 0.0)
+    fill(T.go[:, 3:4], 0.0)
     wait("v", "gc", g_dio)
-    k = ts(T.dm[:], T.dio[:], 31, A.bitwise_and)
+    k = ts(T.dm[:], T.dio[:], 16 * 31 + 1, A.bitwise_and)
+    fill(T.d0[:, 2:32:8], 1.0 / STEP)
     vw(k)
-    for c in range(2):
-        k_tw = ts(T.tw[:, PAD + 32 * c:PAD + 32 * c + 32], T.dm[:], -8192.0, A.mult, 1.0 + 512 * c, A.add)
-    wait("s", "vs", k_tw)
-    vw(k_tw)
-    for m in range(1, 8):
-        out = T.tw[:, PAD + 64 * m:PAD + 64 * m + 64]
-        if m < NTV:
-            ts(out, T.tw[:, PAD:PAD + 64], float(STEP * m), A.add)
-        else:
-            s_tw = line(out, T.tw[:, PAD:PAD + 64], 1.0, float(STEP * m))
-    wait("v", "gc", g_p3)
-    k = ts(T.p3m[:, 3:4], T.p3[:, 3:4], 3 * 512, A.bitwise_and)
-    k2 = ts(T.p3m[:, 0:3], T.p3[:, 0:3], 63, A.bitwise_and)
-    vw(k)
-    k_blk = ts(T.blk[:], T.p3m[:, 3:4], -float(PAD), A.add)
-    vw(k2)
-    copy(T.c3[:], T.p3m[:, 0:3])
 
-    vw(k_blk)
+    def piece(m):
+        a = PAD + S * (lead if m > 3 else mine) + 64 * (3 - m % 4)
+        return T.tw[:, a:a + 64]
+    for m in range(8):
+        if m < NTV:
+            k = ts(piece(m), T.dm[:], -512.0, A.mult, float(STEP * (m + 1)), A.add)
+            if m == 0:
+                wait("s", "vs", k)
+        else:
+            s_tw = line(piece(m), piece(0), 1.0, float(STEP * m))
+
+    ready = {}
+
+    def pieces(dst, src, name, a, n):
+        for b in range(a, a + n, 128):
+            yield dst, src, name, b
+    todo = [*pieces("xq", "xb", "lx", 0, S), *pieces("xp", "xb", "lx", 0, S), *pieces("aq", "ab", "la", 0, 512),
+            *pieces("aq", "ab", "lb", 512, 512), *pieces("uq", "ub", "lu", 0, S), *pieces("vq", "vb", "lv", 0, S)]
+
+    def meanwhile(n=1):
+        for dst, src, name, b in todo[:n]:
+            wait("v", name, 16)
+            ready[dst] = quant(T[dst][:, b:b + 128], T[dst + "s"][:, b:b + 128], T[src][:, 4 * b:4 * b + 512])
+        del todo[:n]
+
+    def total(m):
+        return T.cv[:, 2303 - 256 * m:2304 - 256 * m]
+    wait("v", "gc", g_bq)
     wait("v", "lw", 256)
-    k_off = ts(T.off[:], T.w16[:], T.blk[:, 0:1], A.subtract, float(TOP), A.min)
+    k_off = ts(T.off[:], T.w16[:], blk, A.subtract, float(TOP), A.min)
     wait("s", "vs", k_off)
     sw(s_tw)
-    s = act(T.sr[:, 0:512], T.tw[:].indirect(T.off[:]), Fn.Relu, accum_out=T.cv[:, 255:256])
+    s = act(T.sr[:, 0:512], T.tw[:].indirect(T.off[:]), Fn.Relu, accum_out=total(0))
     sw(s)
-    for m in range(1, 4):
-        s_sum = act(T.sr[:, 512 * m:512 * m + 512], T.sr[:, 0:512], Fn.Relu, bias=-float(STEP * m), scale=1.0,
-                    accum_out=T.cv[:, 256 * m + 255:256 * m + 256])
-    line(T.sl[:, 0:1], T.c3[:, 0:1], 0.25, 0.0)
-    line(T.sl[:, 1:2], T.c3[:, 1:2], 0.125, 16.0)
-    a = PAD + S * (rank % 2)
-    wait("s", "gc", g_own)
-    s_bq = act(T.cb[home:home + 32, a:a + S], T.ownr[home:home + 32, :])
-    act(T.sg[:, 0:1], T.c3[:, 0:1], Fn.Sign, bias=-30.0, scale=1.0)
-    act(T.sg[:, 1:2], T.c3[:, 2:3], Fn.Sign, bias=-31.0, scale=1.0)
-    line(T.pm[:, 0:1], T.c3[:, 0:1], 0.25, 0.0)
-    s = line(T.pm[:, 1:2], T.c3[:, 0:1], 0.25, -6.0)
-    sw(s)
-    line(T.hi8[:], T.sg[:, 0:1], S / 2, S / 2)
-    s_add = line(T.odds[:], T.sg[:, 1:2], S / 2, S / 2)
+    s_sum = {}
+    for c, m in enumerate((7, 3, 2, 1)[NSV - 3:]):
+        s_sum[m] = act(T.sr[:, 512 * c + 512:512 * c + 1024], T.sr[:, 0:512], Fn.Relu, bias=-float(STEP * m),
+                       scale=1.0, accum_out=total(m))
+    wait("s", "gc", g_hm)
+    s_z = line(T.z[:, S * mine:S * mine + S], T.hm[:], 0.0, here)
 
+    ts(T.pm2[:, 0:1], T.dio[:, 0:1], 16 * 15, A.bitwise_and)
+    ts(T.pm2[:, 1:2], T.dio[:, 0:1], 16 * 7, A.bitwise_and)
     wait("v", "ss", s_tw)
     vw(k_off)
     k_rw = [ts(T.rw[:, 0:512], T.tw[:].indirect(T.off[:]), float(4 * STEP), A.subtract, 0.0, A.max)]
+    vw(k_off + 2)
+    ts(T.sl[:, 0:1], T.pm2[:, 0:1], 1 / 16, A.mult)
+    ts(T.sl[:, 1:2], T.pm2[:, 1:2], 1 / 16, A.mult, 16.0, A.add)
     vw(k_rw[0])
-    for m in range(4):
-        if m < 3:
+    for m in range(NSV):
+        if m < NSV - 1:
             k_rw.append(ts(T.rw[:, 512 * m + 512:512 * m + 1024], T.rw[:, 0:512], float(STEP * (m + 1)), A.subtract,
                            0.0, A.max))
         vw(k_rw[m])
-        k = scan(T.cv[:, 1024 + 256 * m:1280 + 256 * m], T.rw[:, 512 * m:512 * m + 512:2],
+        k = scan(T.cv[:, 1024 - 256 * m:1280 - 256 * m], T.rw[:, 512 * m:512 * m + 512:2],
                  T.rw[:, 512 * m + 1:512 * m + 512:2], A.add, A.add)
-    wait("v", "gc", g_h)
-    ts(T.bq[:, 0:2], T.hrow[:], T.blk[:, 0:1], A.add, 1.0 / S, A.mult)
-    wait("v", "ss", s_sum)
-    vw(k + 1)
-    k = tt(T.sm[:], T.cv[:, 255:2304:256], T.cv[:, 511:2560:256], A.subtract)
-    ts(T.bq[:, 2:4], T.bq[:, 0:2], N - 1, A.bitwise_and)
-    vw(k)
-    k = ts(T.go[:], T.sm[:], 1.0 / STEP, A.mult, -0.499, A.add)
-    vw(k - 1)
-    ts(T.bh[:], T.bq[:, 2:4], float(C1), A.mult, S - 1 - MID, A.add)
-    vw(k)
-    k = ts(T.b512[:], T.go[:, 1:9], 512.0, A.mult)
-    k2 = ts(T.a513[:], T.go[:, 0:8], float(STEP), A.mult)
-    vw(k)
-    k = tt(T.ge[:], T.sm[:, 1:9], T.b512[:], A.subtract)
-    wait("v", "gc", g_hm)
-    vw(k2)
-    tt(T.z[:, 0:512:64], T.sm[:, 0:8], T.a513[:], A.not_equal)
-    vw(k)
-    k = tt(T.z[:, 32:512:64], T.go[:, 0:8], T.ge[:], A.not_equal)
-    vw(k)
-    last = [k, k]
+    last = {lead: k, mine: k}
+    k_p = ts(T.p32[:], T.dm[:, 0:1], 1 / 16, A.mult)
+
+    def differ(h):
+        i = 4 * int(h == mine)
+        wait("v", "ss", s_sum.get(1 if i else 7, 0))
+        wait("v", "gc", g_dd)
+        for e in (0, 4):
+            last[h] = tt(T.dd[:, 8 * i + e:8 * i + 32:8], T.cv[:, 256 * i + 511:256 * i + 1280:256],
+                         T.cv[:, 256 * i + 255:256 * i + 1024:256], A.subtract)
+
+    def apart(h):
+        a = 32 * int(h == mine)
+        last[h] = scan(T.go[:, a + 4:a + 36], T.d0[:], T.dd[:, a:a + 32], A.mult, A.add)
+
+    def named(h):
+        a = 32 * int(h == mine)
+        wait("v", "ss", s_z if a else 0)
+        last[h] = tt(T.z[:, S * h:S * h + S:32], T.go[:, a + 7:a + 36:4], T.go[:, a + 3:a + 32:4], A.not_equal)
 
     def hold(h):
-        last[h] = scan(T.zh[:, S * h:S * h + S], T.hm[:, S * h:S * h + S], T.z[:, S * h:S * h + S], A.min, A.add)
+        wait("v", "gc", g_hm)
+        last[h] = scan(T.zh[:, S * h:S * h + S], T.hm[:], T.z[:, S * h:S * h + S], A.min, A.max)
 
     def across(h):
         last[h] = turn(T.row[:, S * h:S * h + S], T.zh[:, S * h:S * h + S])
 
     def number(h):
         wait("v", "gc", g_one)
-        wait("v", "ss", s_bq)
-        parts = [(0, 128)]
-        if h == rank % 2:
-            parts = [(lo, hi) for lo, hi in ((0, home), (home + 32, 64), (max(home + 32, 64), 128)) if lo < hi]
-        for lo, hi in parts:
-            last[h] = scan(T.cb[lo:hi, PAD + S * h:PAD + S * h + S], T.row[lo:hi, S * h:S * h + S], T.one[lo:hi, 0:S],
-                           A.add, A.mult, T.bh[lo:hi, h:h + 1])
+        last[h] = scan(T.cb[:, PAD + S * h:PAD + S * h + S], T.row[:, S * h:S * h + S], T.one[:], A.add, A.mult, bh[h])
         k_cw.append(last[h])
 
     def under(h):
         for c in (2 * h, 2 * h + 1):
-            last[h] = ts(T.le[:, S * c:S * c + S], T.cb[:, PAD + S * h:PAD + S * h + S], T.bh[:, h:h + 1], A.subtract,
+            last[h] = ts(T.le[:, S * c:S * c + S], T.cb[:, PAD + S * h:PAD + S * h + S], bh[h], A.subtract,
                          T.sl[:, c % 2:c % 2 + 1], A.is_le)
 
     def count(h):
         for c in (2 * h, 2 * h + 1):
-            last[h] = scan(T.lc[:, 128 * c:128 * c + 128], T.le[:, S * c:S * c + S:2], T.le[:, S * c + 1:S * c + S:2],
-                           A.add, A.add)
+            vw(last[h] - 1)
+            k = scan(T.lc[:, 128 * c:128 * c + 128], T.le[:, S * c:S * c + S:2], T.le[:, S * c + 1:S * c + S:2],
+                     A.add, A.add)
+            last[h] += 1
+        last[h] = k
 
     def request(h):
         k = ts(T.ms[:, 2 * h:2 * h + 2], T.lc[:, 256 * h + 127:256 * h + 256:128], float(S - 1), A.min)
         wait("g", "vs", k)
         send(lambda i: T.ms[:, 2 * h:2 * h + 2], lambda j: T.lf[:, 2 * j:2 * j + 2], "af", "l1",
-             halves[int(h == rank % 2)])
-    k_cw, steps, done = [], [hold, across, number, under, count, request], [0, 0]
+             halves[int(h == mine)], wide)
+    k_cw, steps, done = [], [differ, apart, named, hold, across, number, under, count, request], [0, 0]
     for part in ORDER:
-        h = (rank + 1 + part) % 2
-        vw(last[h])
+        if part == "q":
+            meanwhile()
+            continue
+        if part == "p":
+            wait("v", "gc", g_pio)
+            k_pl = ts(T.pl16[:], T.pio[:], T.p32[:], A.add)
+            continue
+        part = int(part == "b")
+        h = mine if part else lead
+        if steps[done[part]] is not count:
+            vw(last[h])
         steps[done[part]](h)
         done[part] += 1
 
-    wait("s", "gc", g_pad)
-    wait("s", "vs", max(k_cw))
-    s_gm = act(T.gm[:], T.cb[:].indirect(T.off[:]))
-    s_hk = act(T.hk[:], T.hm[:], Fn.Sign)
-    wait("v", "ss", s_gm)
-    k = turn(T.gt[:], T.gm[:])
-    wait("v", "gc", g_j)
-    ts(T.pl16[:], T.pio[:], T.c3[:, 2:3], A.add, 0.5, A.mult)
-    vw(k)
-    k_pp = copy(T.pc[:, 48:64], T.gt[:, 0:512:32])
-    wait("v", "lx", 16)
-    k_xq = quant(T.xq[:], T.xqs[:], T.xb[:])
-    quant(T.xp[:, 0:S], T.xps[:, 0:S], T.xb[:])
-    wait("y", "vs", k_pp)
-    for t in range(1, 4):
-        load("y", T.pc[0:128 - 32 * t, 16 * t - 16:16 * t], T.pc[32 * t:128, 48:64], "rp")
-        load("y", T.pc[128 - 32 * t:128, 16 * t - 16:16 * t], T.pc[0:32 * t, 48:64], "rp")
-    def spread(q, t):
-        b = (home + 32 * t) % 128
-        wait(q, "af", WIDE)
-        load(q, T.lf[b:b + 32, :], T.lf[home:home + 32, :], "rf")
-    spread("y", 1)
-    spread("y", 2)
-    load("y", T.ub[:], T.u[:], "lu")
-    wait("s", "gc", g_j)
-    for c, (by, b) in enumerate(((12.0, 0), (24.0, 1), (-12.0, 0))):
-        s = line(T.pm[:, 2 + c:3 + c], T.sg[:, 0:1], by, T.pm[:, b:b + 1])
+    wait("s", "vs", k_p)
+    act(T.sg[:, 0:1], T.sl[:, 0:1], Fn.Sign, bias=-7.5, scale=1.0)
+    s = act(T.sg[:, 1:2], T.p32[:], Fn.Sign, bias=-15.5, scale=1.0)
     sw(s)
-    for c, b in enumerate((0, 2, 0, 0, 3, 4)):
-        a = 12 * (c // 3)
-        line(T.cof[:, a + c % 3:a + 12:3], T.jio[:, a + c % 3:a + 12:3], 1.0, T.pm[:, b:b + 1])
-    spread("s", 3)
-    wait("v", "la", 16)
-    quant(T.aq[:, 0:512], T.aqs[:, 0:512], T.ab[:, 0:2048])
-    wait("v", "lb", 16)
-    quant(T.aq[:, 512:1024], T.aqs[:, 512:1024], T.ab[:, 2048:4096])
-    wait("v", "lv", 16)
-    quant(T.vq[:], T.vqs[:], T.vb[:])
+    line(T.hi8[:], T.sg[:, 0:1], S / 2, S / 2)
+    s_add = line(T.odds[:], T.sg[:, 1:2], S / 2, S / 2)
+    wait("s", "gc", g_pad)
+    wait("s", "vs", max(k_cw + [k_pl]))
+    s_gm = act(T.gm[:], T.cb[:].indirect(T.off[:]))
+    s = line(T.pm[:, 0:1], T.sl[:, 0:1], 1.0, -6.0)
+    sw(s_gm)
+    s_g3 = act(T.gm3[:], T.gm[:].indirect(T.pl16[:]))
+    sw(s)
+    at = [T.sl[:, 0:1], T.pm[:, 0:1]]
+    for c, (by, b) in enumerate(((12.0, 0), (24.0, 1), (-12.0, 0))):
+        s_pm = line(T.pm[:, 1 + c:2 + c], T.sg[:, 0:1], by, at[b])
+        at.append(T.pm[:, 1 + c:2 + c])
+    meanwhile(Q1)
 
-    def places():
-        wait("v", "rp", 96)
-        k = tt(T.t32[:], T.pc[:, 0:32], T.pc[:, 32:64], A.add)
-        vw(k)
-        k = tt(T.z[:, 0:512:32], T.t32[:, 0:16], T.t32[:, 16:32], A.add)
-        wait("v", "ss", s_hk)
-        vw(k)
-        k = scan(T.zh[:], T.hk[:], T.z[:], A.mult, A.add)
-        vw(k)
-        return turn(T.row[:], T.zh[:])
-    if EARLY:
-        k_row = places()
-
-    wait("v", "rf", 48)
-    wait("s", "rf", 48)
-    wait("s", "vs", k_xq)
-    k = pick_codes("xg", 0, 224, "xq", 0, S, T.lf[:])
+    wait("v", "af", WIDE)
+    for t in range(1, 4):
+        b = (home + 32 * t) % 128
+        k = copy(T.lf[b:b + 32, :], T.lf[home:home + 32, :])
+    wait("s", "vs", k)
     s = pick_scales("xg", 0, 224, "xq", 0, S, T.lf[:])
     wait("g", "ss", s)
     send(lambda i: T.xgs[:, 32 * i:32 * i + C1], lambda j: T.xps[:, S + C1 * j:S + C1 * j + C1], "axs", "l2")
-    wait("g", "vs", k)
-    send(lambda i: raw(T.xg[:, 32 * i:32 * i + C1]), lambda j: raw(T.xp[:, S + C1 * j:S + C1 * j + C1]), "axc", "l2")
-
     wait("v", "ss", s_add)
+    vw(k)
     for e in range(2):
         ts(T.lr2[:, e:28:4], T.lf[:, 0:14:2], T.odds[:, 0:1], A.add)
         k_lr = ts(T.lr2[:, 2 + e:28:4], T.lf[:, 1:14:2], T.hi8[:, 0:1], A.add)
-    if not EARLY:
-        k_row = places()
-    wait("s", "vs", max(k_row, k_lr))
-    s_g2 = act(T.gm2[:, 256:448], T.row[:].indirect(T.lr2[:, 16:28]))
-    s_g3 = act(T.gm3[:], T.row[:].indirect(T.pl16[:]))
-    vw(max(k_row, k_lr))
-    k = copy(T.gm2[:, 0:256], T.row[:].indirect(T.lr2[:, 0:16]))
+    k = pick_codes("xg", 0, 224, "xq", 0, S, T.lf[:])
+    wait("g", "vs", k)
+    send(lambda i: raw(T.xg[:, 32 * i:32 * i + C1]), lambda j: raw(T.xp[:, S + C1 * j:S + C1 * j + C1]), "axc", "l2")
+
+    wait("s", "vs", k_lr)
+    s_g2 = act(T.gm2[:, 16 * GV:448], T.gm[:].indirect(T.lr2[:, GV:28]))
+    sw(s_pm)
+    wait("s", "gc", g_j)
+    for c, b in enumerate((0, 2, 0, 0, 3, 4)):
+        a = 12 * (c // 3)
+        s_cof = line(T.cof[:, a + c % 3:a + 12:3], T.jio[:, a + c % 3:a + 12:3], 1.0, at[b])
+    vw(k_lr)
+    wait("v", "ss", s_gm)
+    k = copy(T.gm2[:, 0:16 * GV], T.gm[:].indirect(T.lr2[:, 0:GV]))
+    wait("v", "ss", s_g3)
+    k3 = turn(T.gt3[:], T.gm3[:])
     wait("v", "ss", s_g2)
     vw(k)
     k = turn(T.gt2[:], T.gm2[:])
-    ts(T.co16[:], T.cof[:], 335.0, A.min)
+    vw(k3)
+    tt(T.pc[0:64, 0:32], T.gt3[0:64, 1:512:16], T.gt3[64:128, 1:512:16], A.add)
     vw(k)
-    for c, a in enumerate((0, 32, 16)):
-        k_cu = ts(T.cu[:, c:21:3], T.gt2[:, a:448:64], MID, A.add)
-    wait("v", "ss", s_g3)
-    k = turn(T.gt3[:], T.gm3[:])
+    for c, a in enumerate((1, 33, 17)):
+        k = tt(T.pc[0:64, 32 + c:53:3], T.gt2[0:64, a:448:64], T.gt2[64:128, a:448:64], A.add)
     vw(k)
-    k_po = ts(T.po16[:], T.gt3[:, 0:512:16], MID, A.add)
+    k = tt(T.pd[0:32, :], T.pc[0:32, :], T.pc[32:64, :], A.add)
+    vw(k)
+    for b in range(4):
+        k_po = ts(T.po16[32 * b:32 * b + 32, 0:53], T.pd[0:32, :], float(MID), A.add)
+    wait("v", "ss", s_cof)
+    k_co = ts(T.co16[:], T.cof[:], 335.0, A.min)
+    meanwhile(Q2)
 
     ps = [T.ps0, T.ps1, T.ps2, T.ps3]
     pr = [T.pr0, T.pr1, T.pr2, T.pr3]
@@ -389,51 +402,49 @@ def rank_program(g, core, T, topo):
         return act(tile[:, b:4 * n:4], banks[b][:, 0:n], Fn.Relu, scale=0.05)
 
     po = [T.po16[:, 0:16], T.po16[:, 16:32]]
-    wait("s", "vs", k_cu)
-    vw(k_cu)
+    wait("s", "vs", k_po)
+    vw(k_po)
     wait("v", "axc", ARR)
     wait("s", "axs", ARR)
-    k = pick_codes("xu", 0, 336, "xp", 0, POOL, T.cu[:, 0:21])
-    s = pick_scales("xu", 0, 336, "xp", 0, POOL, T.cu[:, 0:21])
-    wait("s", "vs", k_po)
+    k = pick_codes("xu", 0, 336, "xp", 0, POOL, T.po16[:, 32:53])
+    s = pick_scales("xu", 0, 336, "xp", 0, POOL, T.po16[:, 32:53])
     s_xo = [pick_scales("xk", KW * kk, S, "xp", 0, POOL, po[kk]) for kk in range(2)]
     wait("g", "ss", s)
     send(lambda i: T.xus[:, 48 * i:48 * i + 48], lambda j: T.uls[:, 48 * j:48 * j + 48], "aus", "l3")
     wait("g", "vs", k)
     send(lambda i: raw(T.xu[:, 48 * i:48 * i + 48]), lambda j: raw(T.ul[:, 48 * j:48 * j + 48]), "auc", "l3")
-    vw(k_po)
     k_xo = [pick_codes("xk", KW * kk, S, "xp", 0, POOL, po[kk]) for kk in range(2)]
     t_own = layer(ps, [0, KW], S, k_xo, s_xo)
-    wait("v", "lu", 16)
-    quant(T.uq[:], T.uqs[:], T.ub[:])
+    meanwhile(len(todo))
     co = [T.co16[:, 0:11], T.co16[:, 12:23]]
+    wait("s", "vs", k_co)
     wait("s", "aus", ARR)
     s_xr = [pick_scales("xk", KW * kk + S, FAR, "ul", 0, 336, co[kk]) for kk in range(2)]
-    sw(s_xr[0])
-    s_yu = [pick_scales("yu", 0, S, "xk", 0, S + FAR, po[0])]
-    for b in range(2):
-        k_r = relu_v(T.ht, S, ps, b, t_own)
-        s_r = relu_s(T.ht, S, ps, 2 + b, t_own)
+    for b in range(4):
+        if b in OWNV:
+            k_r = relu_v(T.ht, S, ps, b, t_own)
+        else:
+            s_r = relu_s(T.ht, S, ps, b, t_own)
     sw(s_xr[1])
-    s_yu.append(pick_scales("yu", S, S, "xk", KW, KW + S + FAR, po[1]))
+    s_yu = [pick_scales("yu", S * kk, S, "xk", KW * kk, KW * kk + S + FAR, po[kk]) for kk in range(2)]
     wait("v", "auc", ARR)
     k_xr = [pick_codes("xk", KW * kk + S, FAR, "ul", 0, 336, co[kk]) for kk in range(2)]
     t_far = layer(pr, [S, KW + S], POOL - S, k_xr, s_xr)
+    wait("v", "ss", s_r)
+    vw(k_r)
+    quant(T.hp[:, 0:S], T.hps[:, 0:S], T.ht[:])
     vw(k_xr[0])
     k_yu = [pick_codes("yu", 0, S, "xk", 0, S + FAR, po[0])]
-    wait("v", "ss", s_r)
-    quant(T.hp[:, 0:S], T.hps[:, 0:S], T.ht[:])
+    for b in range(3):
+        s_r = relu_s(T.hr, POOL - S, pr, b, t_far)
     vw(k_xr[1])
     k_yu.append(pick_codes("yu", S, S, "xk", KW, KW + S + FAR, po[1]))
-    for b in (0, 2):
-        s_r = relu_s(T.hr, POOL - S, pr, b, t_far)
-        k_r = relu_v(T.hr, POOL - S, pr, b + 1, t_far)
+    k_r = relu_v(T.hr, POOL - S, pr, 3, t_far)
     wait("v", "ss", s_r)
     vw(k_r)
     k_hp = quant(T.hp[:, S:POOL], T.hps[:, S:POOL], T.hr[:])
 
     py = ps[0:2]
-    wait("t", "ss", s_yu[1])
     for kk in range(2):
         wait("t", "vs", k_yu[kk])
         wait("t", "ss", s_yu[kk])
@@ -451,16 +462,13 @@ def rank_program(g, core, T, topo):
         wait("t", "ss", s)
         for hh in range(h, h + n // 128):
             t_y[hh] = product(py[hh], "vq", 128 * kk, "yh", S * kk + 128 * hh, 128, False, kk == 1)
-    wait("s", "ts", t_y[0])
-    s = act(T.yo[:, 0:128], py[0][:, 0:128])
-    wait("v", "ts", t_y[1])
-    k = copy(T.yo[:, 128:S], py[1][:, 0:128])
-    sw(s)
-    load("s", T.y[:, 0:128], T.yo[:, 0:128], "st")
-    wait("y", "vs", k)
-    load("y", T.y[:, 128:S], T.yo[:, 128:S], "st")
+    for h in range(2):
+        wait("v", "ts", t_y[h])
+        k = copy(T.yo[:, 128 * h:128 * h + 128], py[h][:, 0:128])
+        wait("ys"[h], "vs", k)
+        load("ys"[h], T.y[:, 128 * h:128 * h + 128], T.yo[:, 128 * h:128 * h + 128], "st")
 
-    ends = {"lw": 256, "lx": 16, "la": 16, "lb": 16, "lu": 16, "lv": 16, "rp": 96, "rf": 48, "l1": WIDE,
-            "l2": 2 * ARR, "l3": 2 * ARR, "af": WIDE, "axc": ARR, "axs": ARR, "auc": ARR, "aus": ARR, "st": 32, **cnt}
+    ends = {"lw": 256, "lx": 16, "la": 16, "lb": 16, "lu": 16, "lv": 16, "l1": WIDE,
+            "l2": 2 * ARR, "l3": 2 * ARR, "af": WIDE, "axc": ARR, "axs": ARR, "auc": ARR, "aus": ARR, **cnt, "st": 32}
     for name in ends:
         wait("g", name, ends[name])

@@ -9,10 +9,14 @@ PAD, TOP = 16, 528
 STEP = 513
 MID = 212
 WHOLE = 3 << 22
-NTV = 6
-NSV = 3
-ORDER = "aaaaapababababbbbbb"
-Q1, Q2, GV, OWNV = 8, 6, 16, (1,)
+NTV = 5
+ORDER = "papapapaaabbbpbbbbb"
+AS, XA = 1, 0
+Q1, QA, GV, XB = 5, 0, 10, 0
+QB, XW, CUT = 0, 32, (2, 2)
+H2, H3, FLIP = "sA sB cA cB", "UA UB uA uB", (1, 1)
+V4 = "q q q uA uB k0 k1 qq r1 x0 x1 o y0 y1 f3 h"
+S4 = "UA UB K0 K1 X0 X1 r0 r2 r3 Y0 Y1 f0 f1 f2"
 
 F32, BF, I32, U16, F16, CODE, PLANE = "float32", "bfloat16", "int32", "uint16", "float16", "float8_e4m3fn_x4", "uint8"
 SCRATCH = {}
@@ -24,13 +28,13 @@ def _sb(dtype, **bufs):
 
 
 _sb(I32, w16=32)
-_sb(U16, off=32, pl16=32, ms=4, lf=14, lr2=28, po16=54, co16=24)
-_sb(F16, rw=2048, lc=512)
-_sb(F32, sr=2560, cv=2304, dd=64, go=68, cof=24)
+_sb(U16, off=32, pl16=32, lf=14, lr2=28, po16=54, co16=24)
+_sb(F16, rw=1536, lc=512, lg=14)
+_sb(F32, sr=2560, cv=2304, dd=64, go=68, cof=24, th=2, ld=2, lh=8)
 _sb(BF, z=512, zh=512, row=512, cb=544, le=1024, gm=512, gm2=448, gt2=448, gm3=512, gt3=512, pc=53, pd=53)
 _sb(I32, dio=64, dm=64, pm2=2)
-_sb(F32, tw=544, d0=32, sg=2, hi8=1, odds=1, p32=1, pm=4, jio=24, pio=32)
-_sb(BF, one=S, hm=S, bq=8, sl=2)
+_sb(F32, tw=544, d0=32, sg=2, hi8=2, p32=1, pm=4, jio=24, pio=32)
+_sb(BF, one=S, hm=S, bq=2, sl=2)
 _sb(BF, xb=1024, ab=4096, vb=1024, ub=1024, ht=1024, hr=4 * (POOL - S))
 _sb(F32, yo=S)
 for _n, _w in dict(aq=1024, vq=256, uq=256, xq=S, xg=224, xp=POOL, xu=336, ul=336, xk=2 * KW, yu=512,
@@ -39,8 +43,8 @@ for _n, _w in dict(aq=1024, vq=256, uq=256, xq=S, xg=224, xp=POOL, xu=336, ul=33
     SCRATCH[_n + "s"] = ("sbuf", [128, _w], PLANE)
 for _n in ("ps0", "ps1", "ps2", "ps3", "pr0", "pr1", "pr2", "pr3"):
     SCRATCH[_n] = ("psum", [128, 512], F32)
-SEMAPHORES = ["lw", "lx", "la", "lb", "lu", "lv", "vs", "ss", "ts", "gc", "st", "l1", "l2", "l3",
-              "af", "axc", "axs", "auc", "aus"]
+SEMAPHORES = ["lw", "lx", "la", "lb", "lu", "lv", "vs", "ss", "ts", "gc", "lp", "st", "l1", "l2", "l3",
+              "afa", "afb", "axc", "axs", "auc", "aus"]
 
 
 def rank_program(g, core, T, topo):
@@ -124,34 +128,34 @@ def rank_program(g, core, T, topo):
 
     other = [(rank + 1 + i) % N for i in range(N - 1)]
     dest = [T.cores[q] for q in other]
-    every, halves = list(range(N - 1)), [list(range(0, N - 1, 2)), list(range(1, N - 1, 2))]
+    halves = [list(range(0, N - 1, 2)), list(range(1, N - 1, 2))]
+    pos = {i: n for n, i in enumerate(halves[0] + halves[1])}
 
-    masks, used = [], [0, 0]
-    for d in dest:
-        near = int(topo.die(d) == topo.die(core))
-        masks.append(sum(1 << n for n in topo.engines(core, d)[near::2][used[near]:used[near] + 2]))
-        used[near] += 2
-    wide = {}
-    for places in halves:
-        a = 0
-        for i in places:
-            n = 8 if len(places) == 3 and i == places[-1] else 4
-            wide[i] = sum(1 << e for e in topo.engines(core, dest[i])[a:a + n])
-            a += n
-
-    def send(src, dst, name, left, places=every, mask=masks):
-        tr = []
-        for i in places:
+    def send(src, dst, name, left, part, flip=0):
+        tr, used = [], [0, 0]
+        for i in halves[part] if part < 2 else range(N - 1):
+            near = int(topo.die(dest[i]) == topo.die(core))
+            n = 2 if part == 2 else 8 if near and part else 4
+            mask = sum(1 << e for e in topo.engines(core, dest[i])[near ^ flip::2][used[near]:used[near] + n])
+            used[near] += n
             rid, pid, _e = topo.addr(dest[i])
-            tr.append(RemoteDMATransfer(dst_ids=[DstId(rid=rid, pnc=pid)], dma_engine_mask=mask[i],
+            tr.append(RemoteDMATransfer(dst_ids=[DstId(rid=rid, pnc=pid)], dma_engine_mask=mask,
                                         remote_sem=sem[name], src=src(i), dst=dst(6 - i)))
         g.remote_dma_fused(tr, local_sem=sem[left])
 
-    ARR, WIDE = 2 * (N - 1), 32
+    def hop(src, w, dst, at, n, names, part, kind):
+        view = raw if kind else (lambda ap: ap)
+        end = "" if kind else "s"
+        send(lambda i: view(T[src + end][:, w * pos[i]:w * pos[i] + n]),
+             lambda j: view(T[dst + end][:, at + n * j:at + n * j + n]), names[kind], names[2], part,
+             int(part == 1 and not kind and FLIP[names[2] == "l3"]))
+
+    ARR = 32
+    arr = {n: 14 if c + "C" in H2 + H3 else ARR for n, c in (("axs", "s"), ("axc", "c"), ("aus", "U"), ("auc", "u"))}
     home = 32 * (rank // 2)
     lead, mine = (rank + 1) % 2, rank % 2
 
-    for q in range(8):
+    for q in range(2):
         load("y", T.w16[16 * q:16 * q + 16, 0:16], T.nb0[:], "lw")
         load("s", T.w16[16 * q:16 * q + 16, 16:32], T.nb1[:], "lw")
     load("y", T.xb[:], T.x[:], "lx")
@@ -163,10 +167,9 @@ def rank_program(g, core, T, topo):
     g_dio = iota(T.dio[:], [[1, 2], [-16, 32]], 2048, 16, True)
     for b in range(4):
         first = [-1 - MID if q == rank else S + C1 * ((q - rank - 1) % N) - 1 - MID for q in (2 * b, 2 * b + 1)]
-        g_bq = iota(T.bq[32 * b:32 * b + 32, :], [[int(32 * b == home) - first[0], 2], [512 * b - PAD - first[0], 2],
-                                                  [first[1] - first[0], 2]], first[0], 0)
+        g_bq = iota(T.bq[32 * b:32 * b + 32, :], [[first[1] - first[0], 2]], first[0], 0)
         wait("g", "gc", g_bq if b == 3 else g_dio)
-    bh, blk, here = [T.bq[:, 0:1], T.bq[:, 1:2]], T.bq[:, 2:3], T.bq[:, 4:5]
+    bh = [T.bq[:, 0:1], T.bq[:, 1:2]]
     iota(T.d0[:, 1:32:2], [[0, 16]], 1, 0)
     iota(T.d0[:, 0:32:4], [[0, 4], [1 - STEP, 2]], 0, 0)
     iota(T.d0[:, 6:32:8], [[0, 4]], 1, 0)
@@ -174,8 +177,12 @@ def rank_program(g, core, T, topo):
     iota(T.dd[:, 2:64:8], [[0, 8]], WHOLE, 0)
     iota(T.dd[:, 3:64:8], [[0, 8]], -WHOLE, 0)
     iota(T.dd[:, 6:64:8], [[0, 8]], 0, 0)
-    g_dd = iota(T.dd[:, 7:64:8], [[0, 8]], 0, 0)
-    g_hm = iota(T.hm[:], [[0, 8], [1, 32]], 0, 0)
+    iota(T.cv[:, 255:256], [[0, 1]], 0, 0)
+    iota(T.go[:, 3:4], [[0, 1]], 0, 0)
+    wait("g", "gc", iota(T.dd[:, 7:64:8], [[0, 8]], 0, 0))
+    g_dd = iota(T.dd[home:home + 32, 35:64:8], [[0, 4]], 1000 - WHOLE, 0)
+    wait("g", "gc", g_dd)
+    g_hm = iota(T.hm[:, 0:S // min(CUT)], [[0, 8 // min(CUT)], [1, 32]], 0, 0)
     g_one = iota(T.one[:], [[0, S]], 1, 0)
     iota(T.cb[:, 0:PAD], [[0, PAD]], 0, 0)
     g_pad = iota(T.cb[:, TOP:TOP + 16], [[0, 16]], 0, 0)
@@ -186,8 +193,6 @@ def rank_program(g, core, T, topo):
     fill(T.tw[:, 0:PAD], 0.0)
     fill(T.tw[:, TOP:TOP + 16], 0.0)
     fill(T.z[:, S * lead:S * lead + S], 0.0)
-    fill(T.cv[:, 255:256], 0.0)
-    fill(T.go[:, 3:4], 0.0)
     wait("v", "gc", g_dio)
     k = ts(T.dm[:], T.dio[:], 16 * 31 + 1, A.bitwise_and)
     fill(T.d0[:, 2:32:8], 1.0 / STEP)
@@ -205,57 +210,55 @@ def rank_program(g, core, T, topo):
             s_tw = line(piece(m), piece(0), 1.0, float(STEP * m))
 
     ready = {}
-
-    def pieces(dst, src, name, a, n):
-        for b in range(a, a + n, 128):
-            yield dst, src, name, b
-    todo = [*pieces("xq", "xb", "lx", 0, S), *pieces("xp", "xb", "lx", 0, S), *pieces("aq", "ab", "la", 0, 512),
-            *pieces("aq", "ab", "lb", 512, 512), *pieces("uq", "ub", "lu", 0, S), *pieces("vq", "vb", "lv", 0, S)]
+    todo = [(dst, src, name, b) for dst, src, name, a, n in
+            (("xq", "xb", "lx", 0, S), ("aq", "ab", "la", 0, 512), ("aq", "ab", "lb", 512, 512),
+             ("uq", "ub", "lu", 0, S), ("vq", "vb", "lv", 0, S)) for b in range(a, a + n, 128)]
 
     def meanwhile(n=1):
         for dst, src, name, b in todo[:n]:
             wait("v", name, 16)
-            ready[dst] = quant(T[dst][:, b:b + 128], T[dst + "s"][:, b:b + 128], T[src][:, 4 * b:4 * b + 512])
+            ready[name] = quant(T[dst][:, b:b + 128], T[dst + "s"][:, b:b + 128], T[src][:, 4 * b:4 * b + 512])
         del todo[:n]
 
     def total(m):
         return T.cv[:, 2303 - 256 * m:2304 - 256 * m]
-    wait("v", "gc", g_bq)
-    wait("v", "lw", 256)
-    k_off = ts(T.off[:], T.w16[:], blk, A.subtract, float(TOP), A.min)
+    wait("v", "lw", 64)
+    for b in range(4):
+        k_off = ts(T.off[32 * b:32 * b + 32, :], T.w16[0:32, :], float(512 * b - PAD), A.subtract, float(TOP), A.min)
     wait("s", "vs", k_off)
     sw(s_tw)
     s = act(T.sr[:, 0:512], T.tw[:].indirect(T.off[:]), Fn.Relu, accum_out=total(0))
     sw(s)
     s_sum = {}
-    for c, m in enumerate((7, 3, 2, 1)[NSV - 3:]):
+    for c, m in enumerate((7, 3, 2, 1)):
         s_sum[m] = act(T.sr[:, 512 * c + 512:512 * c + 1024], T.sr[:, 0:512], Fn.Relu, bias=-float(STEP * m),
                        scale=1.0, accum_out=total(m))
-    wait("s", "gc", g_hm)
-    s_z = line(T.z[:, S * mine:S * mine + S], T.hm[:], 0.0, here)
 
-    ts(T.pm2[:, 0:1], T.dio[:, 0:1], 16 * 15, A.bitwise_and)
-    ts(T.pm2[:, 1:2], T.dio[:, 0:1], 16 * 7, A.bitwise_and)
+    small = [lambda: ts(T.pm2[:, 0:1], T.dio[:, 0:1], 16 * 15, A.bitwise_and),
+             lambda: ts(T.pm2[:, 1:2], T.dio[:, 0:1], 16 * 7, A.bitwise_and),
+             lambda: ts(T.sl[:, 0:1], T.pm2[:, 0:1], 1 / 16, A.mult, 0.5, A.add),
+             lambda: ts(T.sl[:, 1:2], T.pm2[:, 1:2], 1 / 16, A.mult, 16.5, A.add),
+             lambda: ts(T.p32[:], T.dm[:, 0:1], 1 / 16, A.mult),
+             lambda: fill(T.z[:, S * mine:S * mine + S], 0.0),
+             lambda: ts(T.pl16[:], T.pio[:], T.p32[:], A.add)]
+    k_small = [small.pop(0)()]
     wait("v", "ss", s_tw)
     vw(k_off)
     k_rw = [ts(T.rw[:, 0:512], T.tw[:].indirect(T.off[:]), float(4 * STEP), A.subtract, 0.0, A.max)]
-    vw(k_off + 2)
-    ts(T.sl[:, 0:1], T.pm2[:, 0:1], 1 / 16, A.mult)
-    ts(T.sl[:, 1:2], T.pm2[:, 1:2], 1 / 16, A.mult, 16.0, A.add)
+    k_small.append(small.pop(0)())
     vw(k_rw[0])
-    for m in range(NSV):
-        if m < NSV - 1:
+    for m in range(3):
+        if m < 2:
             k_rw.append(ts(T.rw[:, 512 * m + 512:512 * m + 1024], T.rw[:, 0:512], float(STEP * (m + 1)), A.subtract,
                            0.0, A.max))
         vw(k_rw[m])
         k = scan(T.cv[:, 1024 - 256 * m:1280 - 256 * m], T.rw[:, 512 * m:512 * m + 512:2],
                  T.rw[:, 512 * m + 1:512 * m + 512:2], A.add, A.add)
     last = {lead: k, mine: k}
-    k_p = ts(T.p32[:], T.dm[:, 0:1], 1 / 16, A.mult)
 
     def differ(h):
         i = 4 * int(h == mine)
-        wait("v", "ss", s_sum.get(1 if i else 7, 0))
+        wait("v", "ss", s_sum[1 if i else 7])
         wait("v", "gc", g_dd)
         for e in (0, 4):
             last[h] = tt(T.dd[:, 8 * i + e:8 * i + 32:8], T.cv[:, 256 * i + 511:256 * i + 1280:256],
@@ -267,20 +270,35 @@ def rank_program(g, core, T, topo):
 
     def named(h):
         a = 32 * int(h == mine)
-        wait("v", "ss", s_z if a else 0)
         last[h] = tt(T.z[:, S * h:S * h + S:32], T.go[:, a + 7:a + 36:4], T.go[:, a + 3:a + 32:4], A.not_equal)
 
     def hold(h):
         wait("v", "gc", g_hm)
-        last[h] = scan(T.zh[:, S * h:S * h + S], T.hm[:], T.z[:, S * h:S * h + S], A.min, A.max)
+        n = S // CUT[h == mine]
+        for a in range(S * h, S * h + S, n):
+            last[h] = scan(T.zh[:, a:a + n], T.hm[:, 0:n], T.z[:, a:a + n], A.min, A.max)
 
     def across(h):
-        last[h] = turn(T.row[:, S * h:S * h + S], T.zh[:, S * h:S * h + S])
+        n, k = S // CUT[h == mine], last[h] - CUT[h == mine]
+        for a in range(S * h, S * h + S, n):
+            k += 1
+            vw(k)
+            last[h] = turn(T.row[:, a:a + n], T.zh[:, a:a + n])
 
     def number(h):
         wait("v", "gc", g_one)
         last[h] = scan(T.cb[:, PAD + S * h:PAD + S * h + S], T.row[:, S * h:S * h + S], T.one[:], A.add, A.mult, bh[h])
         k_cw.append(last[h])
+        if h == lead and AS:
+            wait("s", "gc", g_bq)
+            wait("s", "vs", k_small[4])
+            sw(line(T.th[:], T.sl[:], 1.0, bh[h]))
+            wait("s", "vs", last[h])
+            for c in range(2):
+                s = act(T.le[:, S * c + 512 * h:S * c + 512 * h + S - 1], T.cb[:, PAD + S * h:PAD + S * h + S - 1],
+                        Fn.Sign, bias=T.th[:, c:c + 1], scale=-1.0, accum_out=T.ld[:, c:c + 1])
+            wait("g", "ss", s)
+            send(lambda i: T.ld[:], lambda j: T.lh[:, 2 * pos[j]:2 * pos[j] + 2], "afa", "l1", 0)
 
     def under(h):
         for c in (2 * h, 2 * h + 1):
@@ -290,79 +308,99 @@ def rank_program(g, core, T, topo):
     def count(h):
         for c in (2 * h, 2 * h + 1):
             vw(last[h] - 1)
-            k = scan(T.lc[:, 128 * c:128 * c + 128], T.le[:, S * c:S * c + S:2], T.le[:, S * c + 1:S * c + S:2],
+            k = scan(T.lc[:, S * h + c % 2:S * h + S:2], T.le[:, S * c:S * c + S:2], T.le[:, S * c + 1:S * c + S:2],
                      A.add, A.add)
             last[h] += 1
-        last[h] = k
-
-    def request(h):
-        k = ts(T.ms[:, 2 * h:2 * h + 2], T.lc[:, 256 * h + 127:256 * h + 256:128], float(S - 1), A.min)
         wait("g", "vs", k)
-        send(lambda i: T.ms[:, 2 * h:2 * h + 2], lambda j: T.lf[:, 2 * j:2 * j + 2], "af", "l1",
-             halves[int(h == mine)], wide)
-    k_cw, steps, done = [], [differ, apart, named, hold, across, number, under, count, request], [0, 0]
+        send(lambda i: T.lc[:, S * h + S - 2:S * h + S], lambda j: T.lg[:, 2 * pos[j]:2 * pos[j] + 2],
+             "af" + "ab"[h == mine], "l1", int(h == mine))
+
+    k_cw, steps, done = [], [differ, apart, named, hold, across, number, under, count], [0, 0]
     for part in ORDER:
         if part == "q":
             meanwhile()
-            continue
-        if part == "p":
-            wait("v", "gc", g_pio)
-            k_pl = ts(T.pl16[:], T.pio[:], T.p32[:], A.add)
-            continue
-        part = int(part == "b")
-        h = mine if part else lead
-        if steps[done[part]] is not count:
-            vw(last[h])
-        steps[done[part]](h)
-        done[part] += 1
+        elif part == "p":
+            if len(small) == 1:
+                wait("v", "gc", g_pio)
+                vw(k_small[-1])
+            k_small.append(small.pop(0)())
+        else:
+            part = int(part == "b")
+            h = mine if part else lead
+            if steps[done[part]] not in (across, count):
+                vw(last[h])
+            steps[done[part]](h)
+            done[part] += 1
 
-    wait("s", "vs", k_p)
-    act(T.sg[:, 0:1], T.sl[:, 0:1], Fn.Sign, bias=-7.5, scale=1.0)
+    act(T.sg[:, 0:1], T.sl[:, 0:1], Fn.Sign, bias=-8.0, scale=1.0)
     s = act(T.sg[:, 1:2], T.p32[:], Fn.Sign, bias=-15.5, scale=1.0)
     sw(s)
-    line(T.hi8[:], T.sg[:, 0:1], S / 2, S / 2)
-    s_add = line(T.odds[:], T.sg[:, 1:2], S / 2, S / 2)
+    s_add = line(T.hi8[:], T.sg[:], S / 2, S / 2)
     wait("s", "gc", g_pad)
-    wait("s", "vs", max(k_cw + [k_pl]))
+    wait("s", "vs", max(k_cw + k_small))
     s_gm = act(T.gm[:], T.cb[:].indirect(T.off[:]))
-    s = line(T.pm[:, 0:1], T.sl[:, 0:1], 1.0, -6.0)
+    line(T.pm[:, 0:1], T.sl[:, 0:1], 1.0, -6.0)
     sw(s_gm)
     s_g3 = act(T.gm3[:], T.gm[:].indirect(T.pl16[:]))
-    sw(s)
+    meanwhile(Q1)
+    wait("y", "vs", ready["lx"])
+    wait("y", "l1", XW)
+    load("y", raw(T.xp[:, 0:S]), raw(T.xq[:]), "lp")
+    load("y", T.xps[:, 0:S], T.xqs[:], "lp")
+
+    cols = ((0, 8), (8, 14))
+    picked = {}
+
+    def x_codes(part):
+        a, b = cols[part]
+        picked["c" + "AB"[part]] = pick_codes("xg", 16 * a, 16 * (b - a), "xq", 0, S, T.lf[:, a:b])
+    for part, (a, b) in enumerate(cols):
+        wait("v", "af" + "ab"[part], 16)
+        for t in range(4):
+            if part == 0 and AS:
+                k = ts(T.lf[32 * t:32 * t + 32, a:b], T.lh[home:home + 32, :], 0.5, A.mult, (S - 1) / 2, A.add)
+            else:
+                k = ts(T.lf[32 * t:32 * t + 32, a:b], T.lg[home:home + 32, a:b], float(S - 1), A.min)
+        wait("s", "vs", k)
+        picked["s" + "AB"[part]] = pick_scales("xg", 16 * a, 16 * (b - a), "xq", 0, S, T.lf[:, a:b])
+        if part == 0:
+            meanwhile(QA)
+            if not XA:
+                vw(k)
+                x_codes(0)
+    meanwhile(QB)
+    vw(k)
+    if XB == 2:
+        x_codes(1)
+    wait("v", "ss", s_add)
+    for e in range(2):
+        ts(T.lr2[:, e:28:4], T.lf[:, 0:14:2], T.hi8[:, 1:2], A.add)
+        k_lr = ts(T.lr2[:, 2 + e:28:4], T.lf[:, 1:14:2], T.hi8[:, 0:1], A.add)
+    if XA:
+        x_codes(0)
+    if XB == 0:
+        x_codes(1)
+    wait("s", "vs", k_lr)
+    sw(s_gm)
+    s_g2 = act(T.gm2[:, 16 * GV:448], T.gm[:].indirect(T.lr2[:, GV:28]))
+    sw(s_gm + 1)
     at = [T.sl[:, 0:1], T.pm[:, 0:1]]
     for c, (by, b) in enumerate(((12.0, 0), (24.0, 1), (-12.0, 0))):
         s_pm = line(T.pm[:, 1 + c:2 + c], T.sg[:, 0:1], by, at[b])
         at.append(T.pm[:, 1 + c:2 + c])
-    meanwhile(Q1)
-
-    wait("v", "af", WIDE)
-    for t in range(1, 4):
-        b = (home + 32 * t) % 128
-        k = copy(T.lf[b:b + 32, :], T.lf[home:home + 32, :])
-    wait("s", "vs", k)
-    s = pick_scales("xg", 0, 224, "xq", 0, S, T.lf[:])
-    wait("g", "ss", s)
-    send(lambda i: T.xgs[:, 32 * i:32 * i + C1], lambda j: T.xps[:, S + C1 * j:S + C1 * j + C1], "axs", "l2")
-    wait("v", "ss", s_add)
-    vw(k)
-    for e in range(2):
-        ts(T.lr2[:, e:28:4], T.lf[:, 0:14:2], T.odds[:, 0:1], A.add)
-        k_lr = ts(T.lr2[:, 2 + e:28:4], T.lf[:, 1:14:2], T.hi8[:, 0:1], A.add)
-    k = pick_codes("xg", 0, 224, "xq", 0, S, T.lf[:])
-    wait("g", "vs", k)
-    send(lambda i: raw(T.xg[:, 32 * i:32 * i + C1]), lambda j: raw(T.xp[:, S + C1 * j:S + C1 * j + C1]), "axc", "l2")
-
-    wait("s", "vs", k_lr)
-    s_g2 = act(T.gm2[:, 16 * GV:448], T.gm[:].indirect(T.lr2[:, GV:28]))
     sw(s_pm)
     wait("s", "gc", g_j)
     for c, b in enumerate((0, 2, 0, 0, 3, 4)):
         a = 12 * (c // 3)
         s_cof = line(T.cof[:, a + c % 3:a + 12:3], T.jio[:, a + c % 3:a + 12:3], 1.0, at[b])
     vw(k_lr)
-    wait("v", "ss", s_gm)
-    k = copy(T.gm2[:, 0:16 * GV], T.gm[:].indirect(T.lr2[:, 0:GV]))
     wait("v", "ss", s_g3)
+    k = copy(T.gm2[:, 0:16 * GV], T.gm[:].indirect(T.lr2[:, 0:GV]))
+    if XB == 1:
+        x_codes(1)
+    for step in H2.split():
+        wait("g", "vs" if step[0] == "c" else "ss", picked[step.replace("C", "B")])
+        hop("xg", 32, "xp", S, C1, ("axs", "axc", "l2"), "ABC".index(step[1]), int(step[0] == "c"))
     k3 = turn(T.gt3[:], T.gm3[:])
     wait("v", "ss", s_g2)
     vw(k)
@@ -375,83 +413,90 @@ def rank_program(g, core, T, topo):
     vw(k)
     k = tt(T.pd[0:32, :], T.pc[0:32, :], T.pc[32:64, :], A.add)
     vw(k)
-    for b in range(4):
-        k_po = ts(T.po16[32 * b:32 * b + 32, 0:53], T.pd[0:32, :], float(MID), A.add)
+    for t in range(4):
+        k_po = ts(T.po16[32 * t:32 * t + 32, 0:53], T.pd[0:32, :], float(MID), A.add)
     wait("v", "ss", s_cof)
-    k_co = ts(T.co16[:], T.cof[:], 335.0, A.min)
-    meanwhile(Q2)
+    k_co = ts(T.co16[:], T.cof[:], -0.5, A.add, 335.0, A.min)
 
     ps = [T.ps0, T.ps1, T.ps2, T.ps3]
     pr = [T.pr0, T.pr1, T.pr2, T.pr3]
-
-    def layer(banks, xa, n, k_x, s_x):
-        done = [0] * 4
-        for kk in range(2):
-            wait("t", "vs", k_x[kk])
-            wait("t", "ss", s_x[kk])
-            for b in range(4):
-                done[b] = product(banks[b], "aq", 128 * (4 * kk + b), "xk", xa[kk], n, kk == 0, kk == 1)
-        return done
-
-    def relu_v(tile, n, banks, b, done):
-        wait("v", "ts", done[b])
-        return ts(tile[:, b:4 * n:4], banks[b][:, 0:n], 0.0, A.max, 0.05, A.mult)
-
-    def relu_s(tile, n, banks, b, done):
-        wait("s", "ts", done[b])
-        return act(tile[:, b:4 * n:4], banks[b][:, 0:n], Fn.Relu, scale=0.05)
-
     po = [T.po16[:, 0:16], T.po16[:, 16:32]]
-    wait("s", "vs", k_po)
-    vw(k_po)
-    wait("v", "axc", ARR)
-    wait("s", "axs", ARR)
-    k = pick_codes("xu", 0, 336, "xp", 0, POOL, T.po16[:, 32:53])
-    s = pick_scales("xu", 0, 336, "xp", 0, POOL, T.po16[:, 32:53])
-    s_xo = [pick_scales("xk", KW * kk, S, "xp", 0, POOL, po[kk]) for kk in range(2)]
-    wait("g", "ss", s)
-    send(lambda i: T.xus[:, 48 * i:48 * i + 48], lambda j: T.uls[:, 48 * j:48 * j + 48], "aus", "l3")
-    wait("g", "vs", k)
-    send(lambda i: raw(T.xu[:, 48 * i:48 * i + 48]), lambda j: raw(T.ul[:, 48 * j:48 * j + 48]), "auc", "l3")
-    k_xo = [pick_codes("xk", KW * kk, S, "xp", 0, POOL, po[kk]) for kk in range(2)]
-    t_own = layer(ps, [0, KW], S, k_xo, s_xo)
-    meanwhile(len(todo))
     co = [T.co16[:, 0:11], T.co16[:, 12:23]]
-    wait("s", "vs", k_co)
-    wait("s", "aus", ARR)
-    s_xr = [pick_scales("xk", KW * kk + S, FAR, "ul", 0, 336, co[kk]) for kk in range(2)]
-    for b in range(4):
-        if b in OWNV:
-            k_r = relu_v(T.ht, S, ps, b, t_own)
-        else:
-            s_r = relu_s(T.ht, S, ps, b, t_own)
-    sw(s_xr[1])
-    s_yu = [pick_scales("yu", S * kk, S, "xk", KW * kk, KW * kk + S + FAR, po[kk]) for kk in range(2)]
-    wait("v", "auc", ARR)
-    k_xr = [pick_codes("xk", KW * kk + S, FAR, "ul", 0, 336, co[kk]) for kk in range(2)]
-    t_far = layer(pr, [S, KW + S], POOL - S, k_xr, s_xr)
-    wait("v", "ss", s_r)
-    vw(k_r)
-    quant(T.hp[:, 0:S], T.hps[:, 0:S], T.ht[:])
-    vw(k_xr[0])
-    k_yu = [pick_codes("yu", 0, S, "xk", 0, S + FAR, po[0])]
-    for b in range(3):
-        s_r = relu_s(T.hr, POOL - S, pr, b, t_far)
-    vw(k_xr[1])
-    k_yu.append(pick_codes("yu", S, S, "xk", KW, KW + S + FAR, po[1]))
-    k_r = relu_v(T.hr, POOL - S, pr, 3, t_far)
-    wait("v", "ss", s_r)
-    vw(k_r)
-    k_hp = quant(T.hp[:, S:POOL], T.hps[:, S:POOL], T.hr[:])
+    v_steps, s_steps = V4.split(), S4.split()
+    when = {"v": {}, "s": {}}
+    n = cnt["vs"]
+    for step in v_steps:
+        n += len(todo) - v_steps.count("q") if step == "qq" else 1
+        when["v"][step] = n
+    for n, step in enumerate(s_steps):
+        when["s"][step] = cnt["ss"] + n + 1
+    bank = {"r%d" % b: cnt["ts"] + 5 + b for b in range(4)}
+    bank.update({"f%d" % b: cnt["ts"] + 13 + b for b in range(4)})
+
+    def after(q, names):
+        for p in "vs":
+            wait(q, p + "s", max([when[p].get(x, 0) for x in names]))
+
+    def steps_of(q, names):
+        for step in names:
+            kind, kk, codes = step[0].lower(), int(step[1]) if step[1:].isdigit() else 0, step[0].islower()
+
+            def pick(dst, a, n, src, wa, wb, offs):
+                if codes or q == "s":
+                    return (pick_codes if codes else pick_scales)(dst, a, n, src, wa, wb, offs)
+                return copy(T[dst + "s"][:, a:a + n], T[src + "s"][:, wa:wb].indirect(offs))
+            if kind == "u":
+                wait(q, "axc" if codes else "axs", arr["axc" if codes else "axs"])
+                a, b = (0, 12) if step[1] == "A" else (12, 21)
+                pick("xu", 16 * a, 16 * (b - a), "xp", 0, POOL, T.po16[:, 32 + a:32 + b])
+            elif kind == "k":
+                wait(q, "axc" if codes else "axs", arr["axc" if codes else "axs"])
+                pick("xk", KW * kk, S, "xp", 0, POOL, po[kk])
+            elif kind == "q":
+                meanwhile(len(todo) if step == "qq" else 1)
+            elif kind == "x":
+                wait(q, "vs", k_co)
+                wait(q, "auc" if codes else "aus", arr["auc" if codes else "aus"])
+                pick("xk", KW * kk + S, FAR, "ul", 0, 336, co[kk])
+            elif kind == "y":
+                after(q, [c + str(kk) for c in ("kx" if codes else "KX")])
+                pick("yu", S * kk, S, "xk", KW * kk, KW * kk + S + FAR, po[kk])
+            elif kind in "rf":
+                tile, n, banks = (T.ht, S, ps) if kind == "r" else (T.hr, POOL - S, pr)
+                wait(q, "ts", bank[step])
+                if q == "v":
+                    ts(tile[:, kk:4 * n:4], banks[kk][:, 0:n], 0.0, A.max, 0.05, A.mult)
+                else:
+                    act(tile[:, kk:4 * n:4], banks[kk][:, 0:n], Fn.Relu, scale=0.05)
+            elif kind == "o":
+                after(q, ["r0", "r1", "r2", "r3"])
+                quant(T.hp[:, 0:S], T.hps[:, 0:S], T.ht[:])
+            else:
+                after(q, ["f0", "f1", "f2", "f3"])
+                quant(T.hp[:, S:POOL], T.hps[:, S:POOL], T.hr[:])
+    for q in "vs":
+        wait(q, "vs", k_po)
+        wait(q, "lp", 32)
+    steps_of("v", v_steps)
+    steps_of("s", s_steps)
+    for step in H3.split():
+        after("g", [step.replace("C", "B")])
+        hop("xu", 48, "ul", 0, 48, ("aus", "auc", "l3"), "ABC".index(step[1]), int(step[0] == "u"))
+    for banks, xa, n, step in ((ps, 0, S, "k"), (pr, S, POOL - S, "x")):
+        for kk in range(2):
+            after("t", [step + str(kk), step.upper() + str(kk)])
+            wait("t", "vs", ready["lb" if kk else "la"])
+            for b in range(4):
+                product(banks[b], "aq", 128 * (4 * kk + b), "xk", KW * kk + xa, n, kk == 0, kk == 1)
 
     py = ps[0:2]
+    after("t", ["r0", "r1", "qq"])
     for kk in range(2):
-        wait("t", "vs", k_yu[kk])
-        wait("t", "ss", s_yu[kk])
+        after("t", ["y%d" % kk, "Y%d" % kk])
         for h in range(2):
             product(py[h], "uq", 128 * kk, "yu", S * kk + 128 * h, 128, kk == 0, False)
-    vw(k_hp)
-    wait("s", "vs", k_hp)
+    after("v", ["o", "h"])
+    after("s", ["o", "h"])
     t_y = [0, 0]
     for kk, h, n in ((0, 0, S), (1, 0, 128), (1, 1, 128)):
         o = S * kk + 128 * h
@@ -468,7 +513,7 @@ def rank_program(g, core, T, topo):
         wait("ys"[h], "vs", k)
         load("ys"[h], T.y[:, 128 * h:128 * h + 128], T.yo[:, 128 * h:128 * h + 128], "st")
 
-    ends = {"lw": 256, "lx": 16, "la": 16, "lb": 16, "lu": 16, "lv": 16, "l1": WIDE,
-            "l2": 2 * ARR, "l3": 2 * ARR, "af": WIDE, "axc": ARR, "axs": ARR, "auc": ARR, "aus": ARR, **cnt, "st": 32}
+    ends = {"lw": 64, "lx": 16, "la": 16, "lb": 16, "lu": 16, "lv": 16, "lp": 32, "l1": ARR,
+            "l2": arr["axs"] + arr["axc"], "l3": arr["aus"] + arr["auc"], "afa": 16, "afb": 16, **arr, **cnt, "st": 32}
     for name in ends:
         wait("g", name, ends[name])

from concourse.bass import DstId, RemoteDMATransfer
from concourse.mybir import dt, AluOpType, ActivationFunctionType

N, S, C1 = 8, 256, 24
FAR = 176
POOL = S + 7 * C1
KW = 448
PAD, TOP = 16, 528
STEP = 513
MID = 212
WHOLE = 3 << 22
NTV = 5
ORDER = "papapapaaabbbpbbbbb"
AS, XA = 1, 0
Q1, QA, GV, XB = 5, 0, 10, 0
QB, XW, CUT = 0, 32, (2, 2)
H2, H3, FLIP = "sA sB cA cB", "UA UB uA uB", (1, 1)
V4 = "q q q uA uB k0 k1 qq r1 x0 x1 o y0 y1 f3 h"
S4 = "UA UB K0 K1 X0 X1 r0 r2 r3 Y0 Y1 f0 f1 f2"

F32, BF, I32, U16, F16, CODE, PLANE = "float32", "bfloat16", "int32", "uint16", "float16", "float8_e4m3fn_x4", "uint8"
SCRATCH = {}


def _sb(dtype, **bufs):
    for name in bufs:
        SCRATCH[name] = ("sbuf", [128, bufs[name]], dtype)


_sb(I32, w16=32)
_sb(U16, off=32, pl16=32, lf=14, lr2=28, po16=54, co16=24)
_sb(F16, rw=1536, lc=512, lg=14)
_sb(F32, sr=2560, cv=2304, dd=64, go=68, cof=24, th=2, ld=2, lh=8)
_sb(BF, z=512, zh=512, row=512, cb=544, le=1024, gm=512, gm2=448, gt2=448, gm3=512, gt3=512, pc=53, pd=53)
_sb(I32, dio=64, dm=64, pm2=2)
_sb(F32, tw=544, d0=32, sg=2, hi8=2, p32=1, pm=4, jio=24, pio=32)
_sb(BF, one=S, hm=S, bq=2, sl=2)
_sb(BF, xb=1024, ab=4096, vb=1024, ub=1024, ht=1024, hr=4 * (POOL - S))
_sb(F32, yo=S)
for _n, _w in dict(aq=1024, vq=256, uq=256, xq=S, xg=224, xp=POOL, xu=336, ul=336, xk=2 * KW, yu=512,
                   hp=POOL, yh=512).items():
    SCRATCH[_n] = ("sbuf", [128, _w], CODE)
    SCRATCH[_n + "s"] = ("sbuf", [128, _w], PLANE)
for _n in ("ps0", "ps1", "ps2", "ps3", "pr0", "pr1", "pr2", "pr3"):
    SCRATCH[_n] = ("psum", [128, 512], F32)
SEMAPHORES = ["lw", "lx", "la", "lb", "lu", "lv", "vs", "ss", "ts", "gc", "lp", "st", "l1", "l2", "l3",
              "afa", "afb", "axc", "axs", "auc", "aus"]


def rank_program(g, core, T, topo):
    rank = T.rank_of(core)
    if rank is None:
        return
    A, Fn = AluOpType, ActivationFunctionType
    vec, sca, syn, ten, sem = g.vector, g.scalar, g.sync, g.tensor, T.sem
    queue = {"v": vec, "s": sca, "y": syn, "t": ten, "g": g}
    cnt = {"vs": 0, "ss": 0, "ts": 0, "gc": 0}
    seen = {}

    def did(name, ins):
        ins.then_inc(sem[name], 1)
        cnt[name] += 1
        return cnt[name]

    def wait(q, name, val):
        if seen.get((q, name), 0) < val:
            seen[(q, name)] = val
            queue[q].wait_ge(sem[name], val)

    def vw(n):
        wait("v", "vs", n)

    def sw(n):
        wait("s", "ss", n)

    def words(ap):
        return ap.bitcast(dt.uint32)

    def raw(ap):
        return ap.bitcast(dt.uint8)

    def copy(out, in_):
        return did("vs", vec.tensor_copy(out, in_))

    def ts(out, in0, s1, op0, s2=None, op1=None):
        if op1 is None:
            return did("vs", vec.tensor_scalar(out, in0, s1, None, op0))
        return did("vs", vec.tensor_scalar(out, in0, s1, s2, op0, op1))

    def tt(out, in0, in1, op):
        return did("vs", vec.tensor_tensor(out, in0, in1, op))

    def fill(ap, val):
        return did("vs", vec.memset(ap, val))

    def quant(out, sc, in_):
        return did("vs", vec.quantize_mx(out, sc, in_))

    def scan(out, d0, d1, op0, op1, first=0.0):
        return did("vs", vec.tensor_tensor_scan(out, d0, d1, first, op0, op1))

    def turn(out, in_):
        return did("vs", vec.transpose(out, in_))

    def act(out, in_, fn=Fn.Copy, **kw):
        return did("ss", sca.activation(out, in_, fn, **kw))

    def line(out, in_, scale, bias):
        return act(out, in_, Fn.Identity, bias=bias, scale=scale)

    def load(q, out, in_, name):
        queue[q].dma_start(out, in_).then_inc(sem[name], 16)

    def iota(out, pattern, base, mul, whole=False):
        if whole:
            return did("gc", g.iota(out, pattern, base, mul))
        return did("gc", g.iota(out, pattern, base, mul, allow_small_or_imprecise_dtypes=True))

    def pick_codes(dst, a, n, src, wa, wb, offs):
        return copy(words(T[dst][:, a:a + n]), words(T[src][:, wa:wb]).indirect(offs))

    def pick_scales(dst, a, n, src, wa, wb, offs):
        return act(T[dst + "s"][:, a:a + n], T[src + "s"][:, wa:wb].indirect(offs))

    def product(out, w, wa, x, xa, n, start, stop):
        return did("ts", ten.matmul_mx(out[:, 0:n], T[w][:, wa:wa + 128], T[w + "s"][:, wa:wa + 128],
                                       T[x][:, xa:xa + n], T[x + "s"][:, xa:xa + n], start, stop))

    other = [(rank + 1 + i) % N for i in range(N - 1)]
    dest = [T.cores[q] for q in other]
    halves = [list(range(0, N - 1, 2)), list(range(1, N - 1, 2))]
    pos = {i: n for n, i in enumerate(halves[0] + halves[1])}

    def send(src, dst, name, left, part, flip=0):
        tr, used = [], [0, 0]
        for i in halves[part] if part < 2 else range(N - 1):
            near = int(topo.die(dest[i]) == topo.die(core))
            n = 2 if part == 2 else 8 if near and part else 4
            mask = sum(1 << e for e in topo.engines(core, dest[i])[near ^ flip::2][used[near]:used[near] + n])
            used[near] += n
            rid, pid, _e = topo.addr(dest[i])
            tr.append(RemoteDMATransfer(dst_ids=[DstId(rid=rid, pnc=pid)], dma_engine_mask=mask,
                                        remote_sem=sem[name], src=src(i), dst=dst(6 - i)))
        g.remote_dma_fused(tr, local_sem=sem[left])

    def hop(src, w, dst, at, n, names, part, kind):
        view = raw if kind else (lambda ap: ap)
        end = "" if kind else "s"
        send(lambda i: view(T[src + end][:, w * pos[i]:w * pos[i] + n]),
             lambda j: view(T[dst + end][:, at + n * j:at + n * j + n]), names[kind], names[2], part,
             int(part == 1 and not kind and FLIP[names[2] == "l3"]))

    ARR = 32
    arr = {n: 14 if c + "C" in H2 + H3 else ARR for n, c in (("axs", "s"), ("axc", "c"), ("aus", "U"), ("auc", "u"))}
    home = 32 * (rank // 2)
    lead, mine = (rank + 1) % 2, rank % 2

    for q in range(2):
        load("y", T.w16[16 * q:16 * q + 16, 0:16], T.nb0[:], "lw")
        load("s", T.w16[16 * q:16 * q + 16, 16:32], T.nb1[:], "lw")
    load("y", T.xb[:], T.x[:], "lx")
    load("y", T.ab[:, 0:2048], T.a[:, 0:2048], "la")
    load("y", T.ab[:, 2048:4096], T.a[:, 2048:4096], "lb")
    load("y", T.ub[:], T.u[:], "lu")
    load("y", T.vb[:], T.v[:], "lv")

    g_dio = iota(T.dio[:], [[1, 2], [-16, 32]], 2048, 16, True)
    for b in range(4):
        first = [-1 - MID if q == rank else S + C1 * ((q - rank - 1) % N) - 1 - MID for q in (2 * b, 2 * b + 1)]
        g_bq = iota(T.bq[32 * b:32 * b + 32, :], [[first[1] - first[0], 2]], first[0], 0)
        wait("g", "gc", g_bq if b == 3 else g_dio)
    bh = [T.bq[:, 0:1], T.bq[:, 1:2]]
    iota(T.d0[:, 1:32:2], [[0, 16]], 1, 0)
    iota(T.d0[:, 0:32:4], [[0, 4], [1 - STEP, 2]], 0, 0)
    iota(T.d0[:, 6:32:8], [[0, 4]], 1, 0)
    iota(T.dd[:, 1:64:4], [[0, 8], [256, 2]], -256, 0)
    iota(T.dd[:, 2:64:8], [[0, 8]], WHOLE, 0)
    iota(T.dd[:, 3:64:8], [[0, 8]], -WHOLE, 0)
    iota(T.dd[:, 6:64:8], [[0, 8]], 0, 0)
    iota(T.cv[:, 255:256], [[0, 1]], 0, 0)
    iota(T.go[:, 3:4], [[0, 1]], 0, 0)
    wait("g", "gc", iota(T.dd[:, 7:64:8], [[0, 8]], 0, 0))
    g_dd = iota(T.dd[home:home + 32, 35:64:8], [[0, 4]], 1000 - WHOLE, 0)
    wait("g", "gc", g_dd)
    g_hm = iota(T.hm[:, 0:S // min(CUT)], [[0, 8 // min(CUT)], [1, 32]], 0, 0)
    g_one = iota(T.one[:], [[0, S]], 1, 0)
    iota(T.cb[:, 0:PAD], [[0, PAD]], 0, 0)
    g_pad = iota(T.cb[:, TOP:TOP + 16], [[0, 16]], 0, 0)
    g_pio = iota(T.pio[:], [[32, 16], [0, 2]], 0, 0)
    iota(T.jio[:, 0:12], [[96, 4], [28, 3]], 0, 0)
    g_j = iota(T.jio[:, 12:24], [[96, 4], [22, 3]], 32, 0)

    fill(T.tw[:, 0:PAD], 0.0)
    fill(T.tw[:, TOP:TOP + 16], 0.0)
    fill(T.z[:, S * lead:S * lead + S], 0.0)
    wait("v", "gc", g_dio)
    k = ts(T.dm[:], T.dio[:], 16 * 31 + 1, A.bitwise_and)
    fill(T.d0[:, 2:32:8], 1.0 / STEP)
    vw(k)

    def piece(m):
        a = PAD + S * (lead if m > 3 else mine) + 64 * (3 - m % 4)
        return T.tw[:, a:a + 64]
    for m in range(8):
        if m < NTV:
            k = ts(piece(m), T.dm[:], -512.0, A.mult, float(STEP * (m + 1)), A.add)
            if m == 0:
                wait("s", "vs", k)
        else:
            s_tw = line(piece(m), piece(0), 1.0, float(STEP * m))

    ready = {}
    todo = [(dst, src, name, b) for dst, src, name, a, n in
            (("xq", "xb", "lx", 0, S), ("aq", "ab", "la", 0, 512), ("aq", "ab", "lb", 512, 512),
             ("uq", "ub", "lu", 0, S), ("vq", "vb", "lv", 0, S)) for b in range(a, a + n, 128)]

    def meanwhile(n=1):
        for dst, src, name, b in todo[:n]:
            wait("v", name, 16)
            ready[name] = quant(T[dst][:, b:b + 128], T[dst + "s"][:, b:b + 128], T[src][:, 4 * b:4 * b + 512])
        del todo[:n]

    def total(m):
        return T.cv[:, 2303 - 256 * m:2304 - 256 * m]
    wait("v", "lw", 64)
    for b in range(4):
        k_off = ts(T.off[32 * b:32 * b + 32, :], T.w16[0:32, :], float(512 * b - PAD), A.subtract, float(TOP), A.min)
    wait("s", "vs", k_off)
    sw(s_tw)
    s = act(T.sr[:, 0:512], T.tw[:].indirect(T.off[:]), Fn.Relu, accum_out=total(0))
    sw(s)
    s_sum = {}
    for c, m in enumerate((7, 3, 2, 1)):
        s_sum[m] = act(T.sr[:, 512 * c + 512:512 * c + 1024], T.sr[:, 0:512], Fn.Relu, bias=-float(STEP * m),
                       scale=1.0, accum_out=total(m))

    small = [lambda: ts(T.pm2[:, 0:1], T.dio[:, 0:1], 16 * 15, A.bitwise_and),
             lambda: ts(T.pm2[:, 1:2], T.dio[:, 0:1], 16 * 7, A.bitwise_and),
             lambda: ts(T.sl[:, 0:1], T.pm2[:, 0:1], 1 / 16, A.mult, 0.5, A.add),
             lambda: ts(T.sl[:, 1:2], T.pm2[:, 1:2], 1 / 16, A.mult, 16.5, A.add),
             lambda: ts(T.p32[:], T.dm[:, 0:1], 1 / 16, A.mult),
             lambda: fill(T.z[:, S * mine:S * mine + S], 0.0),
             lambda: ts(T.pl16[:], T.pio[:], T.p32[:], A.add)]
    k_small = [small.pop(0)()]
    wait("v", "ss", s_tw)
    vw(k_off)
    k_rw = [ts(T.rw[:, 0:512], T.tw[:].indirect(T.off[:]), float(4 * STEP), A.subtract, 0.0, A.max)]
    k_small.append(small.pop(0)())
    vw(k_rw[0])
    for m in range(3):
        if m < 2:
            k_rw.append(ts(T.rw[:, 512 * m + 512:512 * m + 1024], T.rw[:, 0:512], float(STEP * (m + 1)), A.subtract,
                           0.0, A.max))
        vw(k_rw[m])
        k = scan(T.cv[:, 1024 - 256 * m:1280 - 256 * m], T.rw[:, 512 * m:512 * m + 512:2],
                 T.rw[:, 512 * m + 1:512 * m + 512:2], A.add, A.add)
    last = {lead: k, mine: k}

    def differ(h):
        i = 4 * int(h == mine)
        wait("v", "ss", s_sum[1 if i else 7])
        wait("v", "gc", g_dd)
        for e in (0, 4):
            last[h] = tt(T.dd[:, 8 * i + e:8 * i + 32:8], T.cv[:, 256 * i + 511:256 * i + 1280:256],
                         T.cv[:, 256 * i + 255:256 * i + 1024:256], A.subtract)

    def apart(h):
        a = 32 * int(h == mine)
        last[h] = scan(T.go[:, a + 4:a + 36], T.d0[:], T.dd[:, a:a + 32], A.mult, A.add)

    def named(h):
        a = 32 * int(h == mine)
        last[h] = tt(T.z[:, S * h:S * h + S:32], T.go[:, a + 7:a + 36:4], T.go[:, a + 3:a + 32:4], A.not_equal)

    def hold(h):
        wait("v", "gc", g_hm)
        n = S // CUT[h == mine]
        for a in range(S * h, S * h + S, n):
            last[h] = scan(T.zh[:, a:a + n], T.hm[:, 0:n], T.z[:, a:a + n], A.min, A.max)

    def across(h):
        n, k = S // CUT[h == mine], last[h] - CUT[h == mine]
        for a in range(S * h, S * h + S, n):
            k += 1
            vw(k)
            last[h] = turn(T.row[:, a:a + n], T.zh[:, a:a + n])

    def number(h):
        wait("v", "gc", g_one)
        last[h] = scan(T.cb[:, PAD + S * h:PAD + S * h + S], T.row[:, S * h:S * h + S], T.one[:], A.add, A.mult, bh[h])
        k_cw.append(last[h])
        if h == lead and AS:
            wait("s", "gc", g_bq)
            wait("s", "vs", k_small[4])
            sw(line(T.th[:], T.sl[:], 1.0, bh[h]))
            wait("s", "vs", last[h])
            for c in range(2):
                s = act(T.le[:, S * c + 512 * h:S * c + 512 * h + S - 1], T.cb[:, PAD + S * h:PAD + S * h + S - 1],
                        Fn.Sign, bias=T.th[:, c:c + 1], scale=-1.0, accum_out=T.ld[:, c:c + 1])
            wait("g", "ss", s)
            send(lambda i: T.ld[:], lambda j: T.lh[:, 2 * pos[j]:2 * pos[j] + 2], "afa", "l1", 0)

    def under(h):
        for c in (2 * h, 2 * h + 1):
            last[h] = ts(T.le[:, S * c:S * c + S], T.cb[:, PAD + S * h:PAD + S * h + S], bh[h], A.subtract,
                         T.sl[:, c % 2:c % 2 + 1], A.is_le)

    def count(h):
        for c in (2 * h, 2 * h + 1):
            vw(last[h] - 1)
            k = scan(T.lc[:, S * h + c % 2:S * h + S:2], T.le[:, S * c:S * c + S:2], T.le[:, S * c + 1:S * c + S:2],
                     A.add, A.add)
            last[h] += 1
        wait("g", "vs", k)
        send(lambda i: T.lc[:, S * h + S - 2:S * h + S], lambda j: T.lg[:, 2 * pos[j]:2 * pos[j] + 2],
             "af" + "ab"[h == mine], "l1", int(h == mine))

    k_cw, steps, done = [], [differ, apart, named, hold, across, number, under, count], [0, 0]
    for part in ORDER:
        if part == "q":
            meanwhile()
        elif part == "p":
            if len(small) == 1:
                wait("v", "gc", g_pio)
                vw(k_small[-1])
            k_small.append(small.pop(0)())
        else:
            part = int(part == "b")
            h = mine if part else lead
            if steps[done[part]] not in (across, count):
                vw(last[h])
            steps[done[part]](h)
            done[part] += 1

    act(T.sg[:, 0:1], T.sl[:, 0:1], Fn.Sign, bias=-8.0, scale=1.0)
    s = act(T.sg[:, 1:2], T.p32[:], Fn.Sign, bias=-15.5, scale=1.0)
    sw(s)
    s_add = line(T.hi8[:], T.sg[:], S / 2, S / 2)
    wait("s", "gc", g_pad)
    wait("s", "vs", max(k_cw + k_small))
    s_gm = act(T.gm[:], T.cb[:].indirect(T.off[:]))
    line(T.pm[:, 0:1], T.sl[:, 0:1], 1.0, -6.0)
    sw(s_gm)
    s_g3 = act(T.gm3[:], T.gm[:].indirect(T.pl16[:]))
    meanwhile(Q1)
    wait("y", "vs", ready["lx"])
    wait("y", "l1", XW)
    load("y", raw(T.xp[:, 0:S]), raw(T.xq[:]), "lp")
    load("y", T.xps[:, 0:S], T.xqs[:], "lp")

    cols = ((0, 8), (8, 14))
    picked = {}

    def x_codes(part):
        a, b = cols[part]
        picked["c" + "AB"[part]] = pick_codes("xg", 16 * a, 16 * (b - a), "xq", 0, S, T.lf[:, a:b])
    for part, (a, b) in enumerate(cols):
        wait("v", "af" + "ab"[part], 16)
        for t in range(4):
            if part == 0 and AS:
                k = ts(T.lf[32 * t:32 * t + 32, a:b], T.lh[home:home + 32, :], 0.5, A.mult, (S - 1) / 2, A.add)
            else:
                k = ts(T.lf[32 * t:32 * t + 32, a:b], T.lg[home:home + 32, a:b], float(S - 1), A.min)
        wait("s", "vs", k)
        picked["s" + "AB"[part]] = pick_scales("xg", 16 * a, 16 * (b - a), "xq", 0, S, T.lf[:, a:b])
        if part == 0:
            meanwhile(QA)
            if not XA:
                vw(k)
                x_codes(0)
    meanwhile(QB)
    vw(k)
    if XB == 2:
        x_codes(1)
    wait("v", "ss", s_add)
    for e in range(2):
        ts(T.lr2[:, e:28:4], T.lf[:, 0:14:2], T.hi8[:, 1:2], A.add)
        k_lr = ts(T.lr2[:, 2 + e:28:4], T.lf[:, 1:14:2], T.hi8[:, 0:1], A.add)
    if XA:
        x_codes(0)
    if XB == 0:
        x_codes(1)
    wait("s", "vs", k_lr)
    sw(s_gm)
    s_g2 = act(T.gm2[:, 16 * GV:448], T.gm[:].indirect(T.lr2[:, GV:28]))
    sw(s_gm + 1)
    at = [T.sl[:, 0:1], T.pm[:, 0:1]]
    for c, (by, b) in enumerate(((12.0, 0), (24.0, 1), (-12.0, 0))):
        s_pm = line(T.pm[:, 1 + c:2 + c], T.sg[:, 0:1], by, at[b])
        at.append(T.pm[:, 1 + c:2 + c])
    sw(s_pm)
    wait("s", "gc", g_j)
    for c, b in enumerate((0, 2, 0, 0, 3, 4)):
        a = 12 * (c // 3)
        s_cof = line(T.cof[:, a + c % 3:a + 12:3], T.jio[:, a + c % 3:a + 12:3], 1.0, at[b])
    vw(k_lr)
    wait("v", "ss", s_g3)
    k = copy(T.gm2[:, 0:16 * GV], T.gm[:].indirect(T.lr2[:, 0:GV]))
    if XB == 1:
        x_codes(1)
    for step in H2.split():
        wait("g", "vs" if step[0] == "c" else "ss", picked[step.replace("C", "B")])
        hop("xg", 32, "xp", S, C1, ("axs", "axc", "l2"), "ABC".index(step[1]), int(step[0] == "c"))
    k3 = turn(T.gt3[:], T.gm3[:])
    wait("v", "ss", s_g2)
    vw(k)
    k = turn(T.gt2[:], T.gm2[:])
    vw(k3)
    tt(T.pc[0:64, 0:32], T.gt3[0:64, 1:512:16], T.gt3[64:128, 1:512:16], A.add)
    vw(k)
    for c, a in enumerate((1, 33, 17)):
        k = tt(T.pc[0:64, 32 + c:53:3], T.gt2[0:64, a:448:64], T.gt2[64:128, a:448:64], A.add)
    vw(k)
    k = tt(T.pd[0:32, :], T.pc[0:32, :], T.pc[32:64, :], A.add)
    vw(k)
    for t in range(4):
        k_po = ts(T.po16[32 * t:32 * t + 32, 0:53], T.pd[0:32, :], float(MID), A.add)
    wait("v", "ss", s_cof)
    k_co = ts(T.co16[:], T.cof[:], -0.5, A.add, 335.0, A.min)

    ps = [T.ps0, T.ps1, T.ps2, T.ps3]
    pr = [T.pr0, T.pr1, T.pr2, T.pr3]
    po = [T.po16[:, 0:16], T.po16[:, 16:32]]
    co = [T.co16[:, 0:11], T.co16[:, 12:23]]
    v_steps, s_steps = V4.split(), S4.split()
    when = {"v": {}, "s": {}}
    n = cnt["vs"]
    for step in v_steps:
        n += len(todo) - v_steps.count("q") if step == "qq" else 1
        when["v"][step] = n
    for n, step in enumerate(s_steps):
        when["s"][step] = cnt["ss"] + n + 1
    bank = {"r%d" % b: cnt["ts"] + 5 + b for b in range(4)}
    bank.update({"f%d" % b: cnt["ts"] + 13 + b for b in range(4)})

    def after(q, names):
        for p in "vs":
            wait(q, p + "s", max([when[p].get(x, 0) for x in names]))

    def steps_of(q, names):
        for step in names:
            kind, kk, codes = step[0].lower(), int(step[1]) if step[1:].isdigit() else 0, step[0].islower()

            def pick(dst, a, n, src, wa, wb, offs):
                if codes or q == "s":
                    return (pick_codes if codes else pick_scales)(dst, a, n, src, wa, wb, offs)
                return copy(T[dst + "s"][:, a:a + n], T[src + "s"][:, wa:wb].indirect(offs))
            if kind == "u":
                wait(q, "axc" if codes else "axs", arr["axc" if codes else "axs"])
                a, b = (0, 12) if step[1] == "A" else (12, 21)
                pick("xu", 16 * a, 16 * (b - a), "xp", 0, POOL, T.po16[:, 32 + a:32 + b])
            elif kind == "k":
                wait(q, "axc" if codes else "axs", arr["axc" if codes else "axs"])
                pick("xk", KW * kk, S, "xp", 0, POOL, po[kk])
            elif kind == "q":
                meanwhile(len(todo) if step == "qq" else 1)
            elif kind == "x":
                wait(q, "vs", k_co)
                wait(q, "auc" if codes else "aus", arr["auc" if codes else "aus"])
                pick("xk", KW * kk + S, FAR, "ul", 0, 336, co[kk])
            elif kind == "y":
                after(q, [c + str(kk) for c in ("kx" if codes else "KX")])
                pick("yu", S * kk, S, "xk", KW * kk, KW * kk + S + FAR, po[kk])
            elif kind in "rf":
                tile, n, banks = (T.ht, S, ps) if kind == "r" else (T.hr, POOL - S, pr)
                wait(q, "ts", bank[step])
                if q == "v":
                    ts(tile[:, kk:4 * n:4], banks[kk][:, 0:n], 0.0, A.max, 0.05, A.mult)
                else:
                    act(tile[:, kk:4 * n:4], banks[kk][:, 0:n], Fn.Relu, scale=0.05)
            elif kind == "o":
                after(q, ["r0", "r1", "r2", "r3"])
                quant(T.hp[:, 0:S], T.hps[:, 0:S], T.ht[:])
            else:
                after(q, ["f0", "f1", "f2", "f3"])
                quant(T.hp[:, S:POOL], T.hps[:, S:POOL], T.hr[:])
    for q in "vs":
        wait(q, "vs", k_po)
        wait(q, "lp", 32)
    steps_of("v", v_steps)
    steps_of("s", s_steps)
    for step in H3.split():
        after("g", [step.replace("C", "B")])
        hop("xu", 48, "ul", 0, 48, ("aus", "auc", "l3"), "ABC".index(step[1]), int(step[0] == "u"))
    for banks, xa, n, step in ((ps, 0, S, "k"), (pr, S, POOL - S, "x")):
        for kk in range(2):
            after("t", [step + str(kk), step.upper() + str(kk)])
            wait("t", "vs", ready["lb" if kk else "la"])
            for b in range(4):
                product(banks[b], "aq", 128 * (4 * kk + b), "xk", KW * kk + xa, n, kk == 0, kk == 1)

    py = ps[0:2]
    after("t", ["r0", "r1", "qq"])
    for kk in range(2):
        after("t", ["y%d" % kk, "Y%d" % kk])
        for h in range(2):
            product(py[h], "uq", 128 * kk, "yu", S * kk + 128 * h, 128, kk == 0, False)
    after("v", ["o", "h"])
    after("s", ["o", "h"])
    t_y = [0, 0]
    for kk, h, n in ((0, 0, S), (1, 0, 128), (1, 1, 128)):
        o = S * kk + 128 * h
        offs = T.po16[:, o // 16:(o + n) // 16]
        k = pick_codes("yh", o, n, "hp", 0, POOL, offs)
        s = pick_scales("yh", o, n, "hp", 0, POOL, offs)
        wait("t", "vs", k)
        wait("t", "ss", s)
        for hh in range(h, h + n // 128):
            t_y[hh] = product(py[hh], "vq", 128 * kk, "yh", S * kk + 128 * hh, 128, False, kk == 1)
    for h in range(2):
        wait("v", "ts", t_y[h])
        k = copy(T.yo[:, 128 * h:128 * h + 128], py[h][:, 0:128])
        wait("ys"[h], "vs", k)
        load("ys"[h], T.y[:, 128 * h:128 * h + 128], T.yo[:, 128 * h:128 * h + 128], "st")

    ends = {"lw": 64, "lx": 16, "la": 16, "lb": 16, "lu": 16, "lv": 16, "lp": 32, "l1": ARR,
            "l2": arr["axs"] + arr["axc"], "l3": arr["aus"] + arr["auc"], "afa": 16, "afb": 16, **arr, **cnt, "st": 32}
    for name in ends:
        wait("g", name, ends[name])
